import numpy as np
import ml_dtypes


def mxq(x, axis, fmt="e4m3"):
    dtype, down = {"e4m3": (ml_dtypes.float8_e4m3fn, 7), "e5m2": (ml_dtypes.float8_e5m2, 14)}[fmt]
    v = np.moveaxis(np.asarray(x, np.float32).astype(ml_dtypes.bfloat16).astype(np.float64), axis, -1)
    blocks = v.reshape(v.shape[:-1] + (-1, 32))
    amax = np.abs(blocks).max(-1, keepdims=True)
    byte = np.maximum(np.where(amax > 0, np.frexp(amax)[1] - 1 + 127, 0) - down, 1)
    scale = np.exp2(byte - 127.0)
    codes = (blocks / scale).astype(np.float32).astype(dtype).astype(np.float64)
    return np.moveaxis((codes * scale).reshape(v.shape), -1, axis)


WIDE = False


def mx_kscale(k):
    if not WIDE:
        return np.ones(k)
    levels = np.array([10, -10, 5, -5, 0])
    if k % 512:
        return np.exp2(np.random.permutation(np.resize(levels, k // 32))).repeat(32)
    a = np.empty((k // 512, 16))
    for p in range(k // 512):
        a[p, :8] = np.random.permutation(np.resize(levels, 8))
        for g in range(8):
            far = levels[np.abs(levels - a[p, g]) >= 10]
            a[p, g + 8] = far[np.random.randint(len(far))]
    return np.exp2(a.ravel()).repeat(32)


def f64(x):
    return np.asarray(x).astype(np.float64)


def striped(idx):
    return np.tile(np.asarray(idx).reshape(-1, 16).T, (8, 1)).astype(np.uint16)


def unstriped(offs):
    return offs[:16].T.reshape(-1).astype(np.int64)


E, T, J, G, F = 512, 1024, 512, 128, 512


def setup_inputs():
    n = np.random.standard_normal
    idx = np.random.permutation(T)[:J]
    idx2 = np.random.permutation(T)[:J]
    idx3 = np.random.permutation(T)[:J]
    idx4 = np.random.permutation(T)[:J]
    fe = mx_kscale(E)
    return {
        "vals": (n((E, T)) / fe[:, None]).astype(np.float32),
        "ca": (np.random.uniform(0.1, 0.4, (1, J))).astype(np.float32),
        "cb": (np.random.uniform(0.1, 0.4, (1, J))).astype(np.float32),
        "cc": (np.random.uniform(0.1, 0.4, (1, J))).astype(np.float32),
        "cd": (np.random.uniform(0.1, 0.4, (1, J))).astype(np.float32),
        "aw": (np.random.uniform(0.1, 0.9, (1, J))).astype(np.float32),
        "wo": (n((E, F)) * 2 / np.sqrt(E) * fe[:, None]).astype(np.float32),
        "offs": striped(idx),
        "offs2": striped(idx2),
        "offs3": striped(idx3),
        "offs4": striped(idx4),
    }


def reference(vals, ca, cb, cc, cd, aw, wo, offs, offs2, offs3, offs4):
    idx = unstriped(offs)
    idx2 = unstriped(offs2)
    idx3 = unstriped(offs3)
    idx4 = unstriped(offs4)
    v = f64(vals)[:, idx] * f64(ca) + f64(vals)[:, idx2] * f64(cb) + f64(vals)[:, idx3] * f64(cc) + f64(vals)[:, idx4] * f64(cd)
    b = (v * f64(aw)).reshape(E, G, J // G).sum(axis=2)
    woq = mxq(f64(wo), 0, "e4m3")
    bq = mxq(b, 0, "e4m3")
    y = woq.T @ bq
    return y

@@ -1,0 +1,139 @@
+from contextlib import ExitStack
+
+import concourse.mybir as mybir
+from concourse.masks import make_identity
+
+E, T, J, G, F = 512, 1024, 512, 128, 512
+FLOPS = 2 * E * F * G
+
+F32 = mybir.dt.float32
+BF16 = mybir.dt.bfloat16
+U32 = mybir.dt.uint32
+U16 = mybir.dt.uint16
+U8 = mybir.dt.uint8
+FP8X4 = mybir.dt.float8_e4m3fn_x4
+MULT = mybir.AluOpType.mult
+ADD = mybir.AluOpType.add
+
+P = 128
+PACK = 4
+POINTS = J // G
+CORNERS = 4
+
+
+def tile_attend_deformable_kernel(tc, vals, ca, cb, cc, cd, aw, wo, offs, offs2, offs3, offs4, out):
+    nc = tc.nc
+    with ExitStack() as ctx:
+        keep = ctx.enter_context(tc.tile_pool(name="keep", bufs=1))
+        psum = ctx.enter_context(tc.psum_pool(name="psum", bufs=1))
+
+        lists = [keep.tile([P, J // 16], U16, name=f"list{c}") for c in range(CORNERS)]
+        planes = [keep.tile([P, T], F32, name=f"plane{t}") for t in range(PACK)]
+        corner = [keep.tile([P, POINTS], F32, name=f"corner{c}") for c in range(CORNERS)]
+        att = keep.tile([P, POINTS], F32)
+        wo_raw = keep.tile([P, PACK, F], F32)
+
+        vals_planes = vals.rearrange("(p t) n -> t p n", t=PACK)
+        list_src = (offs, offs2, offs3, offs4)
+        corner_src = (ca, cb, cc, cd)
+
+        nc.sync.dma_start(lists[0][:], list_src[0])
+        nc.sync.dma_start(planes[0][:], vals_planes[0])
+        nc.scalar.dma_start(corner[0][:], corner_src[0].rearrange("o (g i) -> (o g) i", i=POINTS))
+        nc.scalar.dma_start(att[:], aw.rearrange("o (g i) -> (o g) i", i=POINTS))
+        for c in range(1, CORNERS):
+            nc.scalar.dma_start(corner[c][:], corner_src[c].rearrange("o (g i) -> (o g) i", i=POINTS))
+            nc.sync.dma_start(lists[c][:], list_src[c])
+        for t in range(1, PACK):
+            nc.sync.dma_start(planes[t][:], vals_planes[t])
+        nc.sync.dma_start(wo_raw[:], wo.rearrange("(p t) f -> p t f", t=PACK))
+
+        ident = keep.tile([P, P], F32)
+        make_identity(nc, ident[:])
+
+        spread = []
+        for c in range(CORNERS):
+            w_col = keep.tile([P, POINTS], F32, name=f"w_col{c}")
+            nc.vector.tensor_tensor(w_col[:], corner[c][:], att[:], MULT)
+            w_bank = psum.tile([P, POINTS, G], F32, name=f"w_bank{c}", tag=f"w_bank{c % 2}")
+            for i in range(POINTS):
+                nc.tensor.transpose(w_bank[:, i, :], w_col[:, i : i + 1].to_broadcast([P, P]), ident[:])
+            w_row = keep.tile([P, G, POINTS], F32, name=f"w_row{c}")
+            if c == 0:
+                nc.vector.tensor_copy(w_row[:], w_bank[:].rearrange("p i g -> p g i"))
+            else:
+                nc.scalar.copy(w_row[:], w_bank[:].rearrange("p i g -> p g i"))
+            spread.append(w_row)
+
+        wo_bf = keep.tile([P, PACK, P, PACK], BF16, align_bytes=64)
+        nc.scalar.copy(wo_bf[:], wo_raw[:].rearrange("p t (m r) -> p r m t", r=PACK))
+
+        b_planes = keep.tile([P, PACK, G], BF16)
+        for t in range(PACK):
+            last_plane = t == PACK - 1
+            acc = psum.tile([G, P], F32, name=f"acc{t}", tag=f"acc{t % 2}")
+            on_pe = CORNERS - 1 if last_plane else CORNERS
+            for c in range(CORNERS):
+                prod = keep.tile([P, J], F32, name=f"prod{t}_{c}")
+                nc.vector.tensor_tensor(
+                    prod[:], planes[t][:].indirect(lists[c][:]), spread[c][:].rearrange("p g i -> p (g i)"), MULT
+                )
+                if c < on_pe:
+                    for i in range(POINTS):
+                        nc.tensor.matmul(
+                            acc[:],
+                            lhsT=prod[:, i::POINTS],
+                            rhs=ident[:],
+                            is_transpose=True,
+                            start=(c == 0 and i == 0),
+                            stop=(c == on_pe - 1 and i == POINTS - 1),
+                        )
+            turned = keep.tile([G, P], F32, name=f"turned{t}")
+            nc.scalar.copy(turned[:], acc[:])
+            back = psum.tile([P, G], F32, name=f"back{t}", tag=f"back{t % 2}")
+            nc.tensor.transpose(back[:], turned[:], ident[:])
+            if last_plane:
+                rest = keep.tile([P, G], F32)
+                nc.vector.tensor_reduce(
+                    rest[:], prod[:].rearrange("p (g i) -> p g i", i=POINTS), mybir.AxisListType.X, ADD
+                )
+                wo_codes = keep.tile([P, F], U32, align_bytes=64)
+                wo_scales = keep.tile([P, F], U8, align_bytes=64)
+                nc.vector.quantize_mx(
+                    out=wo_codes[:].bitcast(FP8X4),
+                    scales=wo_scales[:],
+                    in_=wo_bf[:].rearrange("p r m t -> p (r m t)"),
+                )
+                nc.vector.tensor_tensor(b_planes[:, t, :], back[:], rest[:], ADD)
+            else:
+                nc.scalar.copy(b_planes[:, t, :], back[:])
+
+        b_bf = keep.tile([P, G, PACK], BF16, align_bytes=64)
+        nc.vector.tensor_copy(b_bf[:], b_planes[:].rearrange("p t g -> p g t"))
+        b_codes = keep.tile([P, G], U32, align_bytes=64)
+        b_scales = keep.tile([P, G], U8, align_bytes=64)
+        nc.vector.quantize_mx(
+            out=b_codes[:].bitcast(FP8X4), scales=b_scales[:], in_=b_bf[:].rearrange("p g t -> p (g t)")
+        )
+
+        out_rows = out.rearrange("(m r) g -> m r g", r=PACK)
+        for h in range(2):
+            y = psum.tile([P, 2, G], F32, name=f"y{h}", tag=f"w_bank{h}")
+            for r in range(2):
+                cols = slice((2 * h + r) * P, (2 * h + r + 1) * P)
+                nc.tensor.matmul_mx(
+                    out=y[:, r, :],
+                    lhsT=wo_codes[:, cols].bitcast(FP8X4),
+                    lhsT_scale=wo_scales[:, cols],
+                    rhs=b_codes[:].bitcast(FP8X4),
+                    rhs_scale=b_scales[:],
+                    start=True,
+                    stop=True,
+                )
+            y_sb = keep.tile([P, 2, G], F32, name=f"y_sb{h}")
+            if h == 0:
+                nc.scalar.copy(y_sb[:], y[:])
+                nc.scalar.dma_start(out_rows[:, 2 * h : 2 * h + 2, :], y_sb[:])
+            else:
+                nc.vector.tensor_copy(y_sb[:], y[:])
+                nc.sync.dma_start(out_rows[:, 2 * h : 2 * h + 2, :], y_sb[:])

@@ -14,6 +14,7 @@ U8 = mybir.dt.uint8
 FP8X4 = mybir.dt.float8_e4m3fn_x4
 MULT = mybir.AluOpType.mult
 ADD = mybir.AluOpType.add
+COPY = mybir.ActivationFunctionType.Copy
 
 P = 128
 PACK = 4
@@ -28,7 +29,7 @@ def tile_attend_deformable_kernel(tc, vals, ca, cb, cc, cd, aw, wo, offs, offs2,
         psum = ctx.enter_context(tc.psum_pool(name="psum", bufs=1))
 
         lists = [keep.tile([P, J // 16], U16, name=f"list{c}") for c in range(CORNERS)]
-        planes = [keep.tile([P, T], F32, name=f"plane{t}") for t in range(PACK)]
+        planes = [keep.tile([P, T], F32, name=f"plane{t}", align_bytes=64) for t in range(PACK)]
         corner = [keep.tile([P, POINTS], F32, name=f"corner{c}") for c in range(CORNERS)]
         att = keep.tile([P, POINTS], F32)
         wo_raw = keep.tile([P, PACK, F], F32)
@@ -36,14 +37,21 @@ def tile_attend_deformable_kernel(tc, vals, ca, cb, cc, cd, aw, wo, offs, offs2,
         vals_planes = vals.rearrange("(p t) n -> t p n", t=PACK)
         list_src = (offs, offs2, offs3, offs4)
         corner_src = (ca, cb, cc, cd)
+        spread_order = (1, 2, 3, 0)
 
+        def load_weights(tile, src):
+            nc.sync.dma_start(tile[:], src.rearrange("o (g i) -> (o g) i", i=POINTS))
+
+        load_weights(att, aw)
+        load_weights(corner[1], corner_src[1])
         nc.sync.dma_start(lists[0][:], list_src[0])
         nc.sync.dma_start(planes[0][:], vals_planes[0])
-        nc.scalar.dma_start(corner[0][:], corner_src[0].rearrange("o (g i) -> (o g) i", i=POINTS))
-        nc.scalar.dma_start(att[:], aw.rearrange("o (g i) -> (o g) i", i=POINTS))
-        for c in range(1, CORNERS):
-            nc.scalar.dma_start(corner[c][:], corner_src[c].rearrange("o (g i) -> (o g) i", i=POINTS))
-            nc.sync.dma_start(lists[c][:], list_src[c])
+        nc.sync.dma_start(lists[1][:], list_src[1])
+        load_weights(corner[2], corner_src[2])
+        load_weights(corner[3], corner_src[3])
+        nc.sync.dma_start(lists[2][:], list_src[2])
+        nc.sync.dma_start(lists[3][:], list_src[3])
+        load_weights(corner[0], corner_src[0])
         for t in range(1, PACK):
             nc.sync.dma_start(planes[t][:], vals_planes[t])
         nc.sync.dma_start(wo_raw[:], wo.rearrange("(p t) f -> p t f", t=PACK))
@@ -51,65 +59,89 @@ def tile_attend_deformable_kernel(tc, vals, ca, cb, cc, cd, aw, wo, offs, offs2,
         ident = keep.tile([P, P], F32)
         make_identity(nc, ident[:])
 
-        spread = []
-        for c in range(CORNERS):
+        w_cols = {}
+        spread = {}
+        for c in spread_order:
             w_col = keep.tile([P, POINTS], F32, name=f"w_col{c}")
             nc.vector.tensor_tensor(w_col[:], corner[c][:], att[:], MULT)
             w_bank = psum.tile([P, POINTS, G], F32, name=f"w_bank{c}", tag=f"w_bank{c % 2}")
             for i in range(POINTS):
                 nc.tensor.transpose(w_bank[:, i, :], w_col[:, i : i + 1].to_broadcast([P, P]), ident[:])
-            w_row = keep.tile([P, G, POINTS], F32, name=f"w_row{c}")
-            if c == 0:
-                nc.vector.tensor_copy(w_row[:], w_bank[:].rearrange("p i g -> p g i"))
-            else:
-                nc.scalar.copy(w_row[:], w_bank[:].rearrange("p i g -> p g i"))
-            spread.append(w_row)
+            w_row = keep.tile([P, G, POINTS], F32, name=f"w_row{c}", align_bytes=64)
+            nc.scalar.copy(w_row[:], w_bank[:].rearrange("p i g -> p g i"))
+            w_cols[c] = w_col
+            spread[c] = w_row
 
-        wo_bf = keep.tile([P, PACK, P, PACK], BF16, align_bytes=64)
-        nc.scalar.copy(wo_bf[:], wo_raw[:].rearrange("p t (m r) -> p r m t", r=PACK))
+        wo_bf = [keep.tile([P, P, PACK], BF16, align_bytes=64, name=f"wo_bf{r}") for r in range(PACK)]
+        for r in range(PACK):
+            nc.scalar.copy(wo_bf[r][:], wo_raw[:, :, r::PACK].rearrange("p t m -> p m t"))
+        wo_scales = [keep.tile([P, P], U8, align_bytes=64, name=f"wo_scales{r}") for r in range(PACK)]
+        wo_codes = []
 
-        b_planes = keep.tile([P, PACK, G], BF16)
+        def quantise_wo(tag):
+            r = len(wo_codes)
+            codes = keep.tile([P, P], U32, align_bytes=64, name=f"wo_codes{r}", tag=tag)
+            nc.vector.quantize_mx(
+                out=codes[:].bitcast(FP8X4), scales=wo_scales[r][:], in_=wo_bf[r][:].rearrange("p m t -> p (m t)")
+            )
+            wo_codes.append(codes)
+
+        b_planes = keep.tile([P, PACK, G], BF16, align_bytes=64)
         for t in range(PACK):
             last_plane = t == PACK - 1
             acc = psum.tile([G, P], F32, name=f"acc{t}", tag=f"acc{t % 2}")
-            on_pe = CORNERS - 1 if last_plane else CORNERS
-            for c in range(CORNERS):
-                prod = keep.tile([P, J], F32, name=f"prod{t}_{c}")
+            order = range(CORNERS) if t == 0 else spread_order
+            first_on_pe = 1 if t == 0 else 0
+            last_on_pe = CORNERS - 2 if last_plane else CORNERS - 1
+            addends = []
+            for step, c in enumerate(order):
+                prod = keep.tile([P, J], F32, name=f"prod{t}_{c}", align_bytes=64)
+                if step < first_on_pe:
+                    nc.vector.tensor_copy(prod[:], planes[t][:].indirect(lists[c][:]))
+                    bare = psum.tile([G, POINTS, P], F32)
+                    weighted = keep.tile([G, POINTS, P], F32)
+                    for i in range(POINTS):
+                        nc.tensor.transpose(bare[:, i, :], prod[:, i::POINTS], ident[:])
+                    for i in range(POINTS):
+                        nc.scalar.activation(weighted[:, i, :], bare[:, i, :], COPY, scale=w_cols[c][:, i : i + 1])
+                        addends.append(weighted[:, i, :])
+                    continue
                 nc.vector.tensor_tensor(
                     prod[:], planes[t][:].indirect(lists[c][:]), spread[c][:].rearrange("p g i -> p (g i)"), MULT
                 )
-                if c < on_pe:
+                if step <= last_on_pe:
                     for i in range(POINTS):
                         nc.tensor.matmul(
                             acc[:],
                             lhsT=prod[:, i::POINTS],
                             rhs=ident[:],
                             is_transpose=True,
-                            start=(c == 0 and i == 0),
-                            stop=(c == on_pe - 1 and i == POINTS - 1),
+                            start=(step == first_on_pe and i == 0),
+                            stop=(step == last_on_pe and i == POINTS - 1),
                         )
             turned = keep.tile([G, P], F32, name=f"turned{t}")
             nc.scalar.copy(turned[:], acc[:])
+            addends.append(turned[:])
             back = psum.tile([P, G], F32, name=f"back{t}", tag=f"back{t % 2}")
-            nc.tensor.transpose(back[:], turned[:], ident[:])
+            for n, addend in enumerate(addends):
+                nc.tensor.matmul(
+                    back[:], lhsT=addend, rhs=ident[:], is_transpose=True, start=(n == 0), stop=(n == len(addends) - 1)
+                )
             if last_plane:
-                rest = keep.tile([P, G], F32)
+                rest = keep.tile([P, G], F32, align_bytes=64)
                 nc.vector.tensor_reduce(
                     rest[:], prod[:].rearrange("p (g i) -> p g i", i=POINTS), mybir.AxisListType.X, ADD
                 )
-                wo_codes = keep.tile([P, F], U32, align_bytes=64)
-                wo_scales = keep.tile([P, F], U8, align_bytes=64)
-                nc.vector.quantize_mx(
-                    out=wo_codes[:].bitcast(FP8X4),
-                    scales=wo_scales[:],
-                    in_=wo_bf[:].rearrange("p r m t -> p (r m t)"),
-                )
+                quantise_wo(f"w_row{c}")
+                quantise_wo(f"plane{t}")
                 nc.vector.tensor_tensor(b_planes[:, t, :], back[:], rest[:], ADD)
+                quantise_wo(f"prod{t}_{c}")
             else:
                 nc.scalar.copy(b_planes[:, t, :], back[:])
 
         b_bf = keep.tile([P, G, PACK], BF16, align_bytes=64)
         nc.vector.tensor_copy(b_bf[:], b_planes[:].rearrange("p t g -> p g t"))
+        quantise_wo("rest")
         b_codes = keep.tile([P, G], U32, align_bytes=64)
         b_scales = keep.tile([P, G], U8, align_bytes=64)
         nc.vector.quantize_mx(
@@ -120,11 +152,10 @@ def tile_attend_deformable_kernel(tc, vals, ca, cb, cc, cd, aw, wo, offs, offs2,
         for h in range(2):
             y = psum.tile([P, 2, G], F32, name=f"y{h}", tag=f"w_bank{h}")
             for r in range(2):
-                cols = slice((2 * h + r) * P, (2 * h + r + 1) * P)
                 nc.tensor.matmul_mx(
                     out=y[:, r, :],
-                    lhsT=wo_codes[:, cols].bitcast(FP8X4),
-                    lhsT_scale=wo_scales[:, cols],
+                    lhsT=wo_codes[2 * h + r][:].bitcast(FP8X4),
+                    lhsT_scale=wo_scales[2 * h + r][:],
                     rhs=b_codes[:].bitcast(FP8X4),
                     rhs_scale=b_scales[:],
                     start=True,

@@ -38,6 +38,7 @@ def tile_attend_deformable_kernel(tc, vals, ca, cb, cc, cd, aw, wo, offs, offs2,
         list_src = (offs, offs2, offs3, offs4)
         corner_src = (ca, cb, cc, cd)
         spread_order = (1, 2, 3, 0)
+        plane_order = (2, 0, 1, 3)
 
         def load_weights(tile, src):
             nc.sync.dma_start(tile[:], src.rearrange("o (g i) -> (o g) i", i=POINTS))
@@ -45,14 +46,14 @@ def tile_attend_deformable_kernel(tc, vals, ca, cb, cc, cd, aw, wo, offs, offs2,
         load_weights(att, aw)
         load_weights(corner[1], corner_src[1])
         nc.sync.dma_start(lists[0][:], list_src[0])
-        nc.sync.dma_start(planes[0][:], vals_planes[0])
+        nc.sync.dma_start(planes[plane_order[0]][:], vals_planes[plane_order[0]])
         nc.sync.dma_start(lists[1][:], list_src[1])
         load_weights(corner[2], corner_src[2])
         load_weights(corner[3], corner_src[3])
         nc.sync.dma_start(lists[2][:], list_src[2])
         nc.sync.dma_start(lists[3][:], list_src[3])
         load_weights(corner[0], corner_src[0])
-        for t in range(1, PACK):
+        for t in plane_order[1:]:
             nc.sync.dma_start(planes[t][:], vals_planes[t])
         nc.sync.dma_start(wo_raw[:], wo.rearrange("(p t) f -> p t f", t=PACK))
 
@@ -72,9 +73,12 @@ def tile_attend_deformable_kernel(tc, vals, ca, cb, cc, cd, aw, wo, offs, offs2,
             w_cols[c] = w_col
             spread[c] = w_row
 
-        wo_bf = [keep.tile([P, P, PACK], BF16, align_bytes=64, name=f"wo_bf{r}") for r in range(PACK)]
-        for r in range(PACK):
-            nc.scalar.copy(wo_bf[r][:], wo_raw[:, :, r::PACK].rearrange("p t m -> p m t"))
+        wo_bf = keep.tile([P, PACK, P, PACK], BF16, align_bytes=64)
+        wo_dst = wo_bf[:].rearrange("p r m t -> p m t r")
+        wo_src = wo_raw[:].rearrange("p t (m r) -> p m t r", r=PACK)
+        for q in range(PACK):
+            ms = slice(q * P // PACK, (q + 1) * P // PACK)
+            nc.scalar.copy(wo_dst[:, ms], wo_src[:, ms])
         wo_scales = [keep.tile([P, P], U8, align_bytes=64, name=f"wo_scales{r}") for r in range(PACK)]
         wo_codes = []
 
@@ -82,16 +86,16 @@ def tile_attend_deformable_kernel(tc, vals, ca, cb, cc, cd, aw, wo, offs, offs2,
             r = len(wo_codes)
             codes = keep.tile([P, P], U32, align_bytes=64, name=f"wo_codes{r}", tag=tag)
             nc.vector.quantize_mx(
-                out=codes[:].bitcast(FP8X4), scales=wo_scales[r][:], in_=wo_bf[r][:].rearrange("p m t -> p (m t)")
+                out=codes[:].bitcast(FP8X4), scales=wo_scales[r][:], in_=wo_bf[:, r].rearrange("p m t -> p (m t)")
             )
             wo_codes.append(codes)
 
-        b_planes = keep.tile([P, PACK, G], BF16, align_bytes=64)
-        for t in range(PACK):
-            last_plane = t == PACK - 1
-            acc = psum.tile([G, P], F32, name=f"acc{t}", tag=f"acc{t % 2}")
-            order = range(CORNERS) if t == 0 else spread_order
-            first_on_pe = 1 if t == 0 else 0
+        b_bf = keep.tile([P, G, PACK], BF16, align_bytes=64)
+        for turn, t in enumerate(plane_order):
+            last_plane = turn == PACK - 1
+            acc = psum.tile([G, P], F32, name=f"acc{t}", tag=f"acc{turn % 2}")
+            order = range(CORNERS) if turn == 0 else spread_order
+            first_on_pe = 1 if turn == 0 else 0
             last_on_pe = CORNERS - 2 if last_plane else CORNERS - 1
             addends = []
             for step, c in enumerate(order):
@@ -122,31 +126,29 @@ def tile_attend_deformable_kernel(tc, vals, ca, cb, cc, cd, aw, wo, offs, offs2,
             turned = keep.tile([G, P], F32, name=f"turned{t}")
             nc.scalar.copy(turned[:], acc[:])
             addends.append(turned[:])
-            back = psum.tile([P, G], F32, name=f"back{t}", tag=f"back{t % 2}")
+            back = psum.tile([P, G], F32, name=f"back{t}", tag=f"back{turn % 2}")
             for n, addend in enumerate(addends):
                 nc.tensor.matmul(
                     back[:], lhsT=addend, rhs=ident[:], is_transpose=True, start=(n == 0), stop=(n == len(addends) - 1)
                 )
             if last_plane:
+                quantise_wo(f"w_row{order[-2]}")
                 rest = keep.tile([P, G], F32, align_bytes=64)
                 nc.vector.tensor_reduce(
                     rest[:], prod[:].rearrange("p (g i) -> p g i", i=POINTS), mybir.AxisListType.X, ADD
                 )
                 quantise_wo(f"w_row{c}")
-                quantise_wo(f"plane{t}")
-                nc.vector.tensor_tensor(b_planes[:, t, :], back[:], rest[:], ADD)
+                nc.vector.tensor_tensor(b_bf[:, :, t], back[:], rest[:], ADD)
                 quantise_wo(f"prod{t}_{c}")
             else:
-                nc.scalar.copy(b_planes[:, t, :], back[:])
+                nc.scalar.copy(b_bf[:, :, t], back[:])
 
-        b_bf = keep.tile([P, G, PACK], BF16, align_bytes=64)
-        nc.vector.tensor_copy(b_bf[:], b_planes[:].rearrange("p t g -> p g t"))
-        quantise_wo("rest")
         b_codes = keep.tile([P, G], U32, align_bytes=64)
         b_scales = keep.tile([P, G], U8, align_bytes=64)
         nc.vector.quantize_mx(
             out=b_codes[:].bitcast(FP8X4), scales=b_scales[:], in_=b_bf[:].rearrange("p g t -> p (g t)")
         )
+        quantise_wo("rest")
 
         out_rows = out.rearrange("(m r) g -> m r g", r=PACK)
         for h in range(2):

@@ -20,6 +20,7 @@ P = 128
 PACK = 4
 POINTS = J // G
 CORNERS = 4
+FIRST_DEALT, LAST_DEALT = 8, 12
 
 
 def tile_attend_deformable_kernel(tc, vals, ca, cb, cc, cd, aw, wo, offs, offs2, offs3, offs4, out):
@@ -114,10 +115,17 @@ def tile_attend_deformable_kernel(tc, vals, ca, cb, cc, cd, aw, wo, offs, offs2,
                     prod[:], planes[t][:].indirect(lists[c][:]), spread[c][:].rearrange("p g i -> p (g i)"), MULT
                 )
                 if step <= last_on_pe:
+                    by_point = [prod[:, i::POINTS] for i in range(POINTS)]
+                    if FIRST_DEALT <= turn * CORNERS + step <= LAST_DEALT:
+                        dealt = keep.tile([P, POINTS, G], F32, name=f"dealt{t}_{c}", align_bytes=64)
+                        nc.scalar.copy(
+                            dealt[:].rearrange("p i g -> p g i"), prod[:].rearrange("p (g i) -> p g i", i=POINTS)
+                        )
+                        by_point = [dealt[:, i, :] for i in range(POINTS)]
                     for i in range(POINTS):
                         nc.tensor.matmul(
                             acc[:],
-                            lhsT=prod[:, i::POINTS],
+                            lhsT=by_point[i],
                             rhs=ident[:],
                             is_transpose=True,
                             start=(step == first_on_pe and i == 0),

@@ -20,6 +20,7 @@ P = 128
 PACK = 4
 POINTS = J // G
 CORNERS = 4
+PLAIN = 2
 FIRST_DEALT, LAST_DEALT = 8, 12
 
 
@@ -31,29 +32,29 @@ def tile_attend_deformable_kernel(tc, vals, ca, cb, cc, cd, aw, wo, offs, offs2,
 
         lists = [keep.tile([P, J // 16], U16, name=f"list{c}") for c in range(CORNERS)]
         planes = [keep.tile([P, T], F32, name=f"plane{t}", align_bytes=64) for t in range(PACK)]
-        corner = [keep.tile([P, POINTS], F32, name=f"corner{c}") for c in range(CORNERS)]
+        early = keep.tile([P, POINTS], F32)
+        late = keep.tile([P, CORNERS - 1, 2 * POINTS], F32)
         att = keep.tile([P, POINTS], F32)
         wo_raw = keep.tile([P, PACK, F], F32)
 
         vals_planes = vals.rearrange("(p t) n -> t p n", t=PACK)
         list_src = (offs, offs2, offs3, offs4)
         corner_src = (ca, cb, cc, cd)
-        spread_order = (1, 2, 3, 0)
+        spread_order = (2, 3, 0, 1)
         plane_order = (2, 0, 1, 3)
 
-        def load_weights(tile, src):
-            nc.sync.dma_start(tile[:], src.rearrange("o (g i) -> (o g) i", i=POINTS))
+        def load_weights(dst, src):
+            nc.sync.dma_start(dst, src.rearrange("o (g i) -> (o g) i", i=POINTS))
 
-        load_weights(att, aw)
-        load_weights(corner[1], corner_src[1])
-        nc.sync.dma_start(lists[0][:], list_src[0])
+        load_weights(att[:], aw)
+        load_weights(early[:], corner_src[spread_order[0]])
         nc.sync.dma_start(planes[plane_order[0]][:], vals_planes[plane_order[0]])
+        nc.sync.dma_start(lists[0][:], list_src[0])
         nc.sync.dma_start(lists[1][:], list_src[1])
-        load_weights(corner[2], corner_src[2])
-        load_weights(corner[3], corner_src[3])
+        for n, c in enumerate(spread_order[1:]):
+            load_weights(late[:, n, 0:POINTS], corner_src[c])
         nc.sync.dma_start(lists[2][:], list_src[2])
         nc.sync.dma_start(lists[3][:], list_src[3])
-        load_weights(corner[0], corner_src[0])
         for t in plane_order[1:]:
             nc.sync.dma_start(planes[t][:], vals_planes[t])
         nc.sync.dma_start(wo_raw[:], wo.rearrange("(p t) f -> p t f", t=PACK))
@@ -61,17 +62,24 @@ def tile_attend_deformable_kernel(tc, vals, ca, cb, cc, cd, aw, wo, offs, offs2,
         ident = keep.tile([P, P], F32)
         make_identity(nc, ident[:])
 
-        w_cols = {}
+        w_early = keep.tile([P, POINTS], F32)
+        nc.vector.tensor_tensor(w_early[:], early[:], att[:], MULT)
+        w_late = keep.tile([P, CORNERS - 1, POINTS], F32)
+        w_cols = {spread_order[0]: w_early[:]}
         spread = {}
-        for c in spread_order:
-            w_col = keep.tile([P, POINTS], F32, name=f"w_col{c}")
-            nc.vector.tensor_tensor(w_col[:], corner[c][:], att[:], MULT)
+        for n, c in enumerate(spread_order):
+            if n == 1:
+                nc.vector.tensor_tensor(
+                    w_late[:], late[:, :, 0:POINTS], att[:].unsqueeze(1).to_broadcast([P, CORNERS - 1, POINTS]), MULT
+                )
+            if n > 0:
+                w_cols[c] = w_late[:, n - 1, :]
+            w_col = w_cols[c]
             w_bank = psum.tile([P, POINTS, G], F32, name=f"w_bank{c}", tag=f"w_bank{c % 2}")
             for i in range(POINTS):
                 nc.tensor.transpose(w_bank[:, i, :], w_col[:, i : i + 1].to_broadcast([P, P]), ident[:])
             w_row = keep.tile([P, G, POINTS], F32, name=f"w_row{c}", align_bytes=64)
             nc.scalar.copy(w_row[:], w_bank[:].rearrange("p i g -> p g i"))
-            w_cols[c] = w_col
             spread[c] = w_row
 
         wo_bf = keep.tile([P, PACK, P, PACK], BF16, align_bytes=64)
@@ -96,15 +104,15 @@ def tile_attend_deformable_kernel(tc, vals, ca, cb, cc, cd, aw, wo, offs, offs2,
             last_plane = turn == PACK - 1
             acc = psum.tile([G, P], F32, name=f"acc{t}", tag=f"acc{turn % 2}")
             order = range(CORNERS) if turn == 0 else spread_order
-            first_on_pe = 1 if turn == 0 else 0
+            first_on_pe = PLAIN if turn == 0 else 0
             last_on_pe = CORNERS - 2 if last_plane else CORNERS - 1
             addends = []
             for step, c in enumerate(order):
                 prod = keep.tile([P, J], F32, name=f"prod{t}_{c}", align_bytes=64)
                 if step < first_on_pe:
                     nc.vector.tensor_copy(prod[:], planes[t][:].indirect(lists[c][:]))
-                    bare = psum.tile([G, POINTS, P], F32)
-                    weighted = keep.tile([G, POINTS, P], F32)
+                    bare = psum.tile([G, POINTS, P], F32, name=f"bare{c}", tag=f"bare{c}")
+                    weighted = keep.tile([G, POINTS, P], F32, name=f"weighted{c}")
                     for i in range(POINTS):
                         nc.tensor.transpose(bare[:, i, :], prod[:, i::POINTS], ident[:])
                     for i in range(POINTS):

@@ -20,7 +20,7 @@ P = 128
 PACK = 4
 POINTS = J // G
 CORNERS = 4
-PLAIN = 2
+PLAIN = 3
 FIRST_DEALT, LAST_DEALT = 8, 12
 
 
@@ -32,27 +32,25 @@ def tile_attend_deformable_kernel(tc, vals, ca, cb, cc, cd, aw, wo, offs, offs2,
 
         lists = [keep.tile([P, J // 16], U16, name=f"list{c}") for c in range(CORNERS)]
         planes = [keep.tile([P, T], F32, name=f"plane{t}", align_bytes=64) for t in range(PACK)]
-        early = keep.tile([P, POINTS], F32)
-        late = keep.tile([P, CORNERS - 1, 2 * POINTS], F32)
+        corner = keep.tile([P, CORNERS, 2 * POINTS], F32)
         att = keep.tile([P, POINTS], F32)
         wo_raw = keep.tile([P, PACK, F], F32)
 
         vals_planes = vals.rearrange("(p t) n -> t p n", t=PACK)
         list_src = (offs, offs2, offs3, offs4)
         corner_src = (ca, cb, cc, cd)
-        spread_order = (2, 3, 0, 1)
+        spread_order = (3, 0, 1, 2)
         plane_order = (2, 0, 1, 3)
 
         def load_weights(dst, src):
             nc.sync.dma_start(dst, src.rearrange("o (g i) -> (o g) i", i=POINTS))
 
-        load_weights(att[:], aw)
-        load_weights(early[:], corner_src[spread_order[0]])
         nc.sync.dma_start(planes[plane_order[0]][:], vals_planes[plane_order[0]])
         nc.sync.dma_start(lists[0][:], list_src[0])
+        load_weights(att[:], aw)
+        for c in spread_order:
+            load_weights(corner[:, c, 0:POINTS], corner_src[c])
         nc.sync.dma_start(lists[1][:], list_src[1])
-        for n, c in enumerate(spread_order[1:]):
-            load_weights(late[:, n, 0:POINTS], corner_src[c])
         nc.sync.dma_start(lists[2][:], list_src[2])
         nc.sync.dma_start(lists[3][:], list_src[3])
         for t in plane_order[1:]:
@@ -62,22 +60,15 @@ def tile_attend_deformable_kernel(tc, vals, ca, cb, cc, cd, aw, wo, offs, offs2,
         ident = keep.tile([P, P], F32)
         make_identity(nc, ident[:])
 
-        w_early = keep.tile([P, POINTS], F32)
-        nc.vector.tensor_tensor(w_early[:], early[:], att[:], MULT)
-        w_late = keep.tile([P, CORNERS - 1, POINTS], F32)
-        w_cols = {spread_order[0]: w_early[:]}
+        w_cols = keep.tile([P, CORNERS, POINTS], F32)
+        nc.vector.tensor_tensor(
+            w_cols[:], corner[:, :, 0:POINTS], att[:].unsqueeze(1).to_broadcast([P, CORNERS, POINTS]), MULT
+        )
         spread = {}
-        for n, c in enumerate(spread_order):
-            if n == 1:
-                nc.vector.tensor_tensor(
-                    w_late[:], late[:, :, 0:POINTS], att[:].unsqueeze(1).to_broadcast([P, CORNERS - 1, POINTS]), MULT
-                )
-            if n > 0:
-                w_cols[c] = w_late[:, n - 1, :]
-            w_col = w_cols[c]
+        for c in spread_order:
             w_bank = psum.tile([P, POINTS, G], F32, name=f"w_bank{c}", tag=f"w_bank{c % 2}")
             for i in range(POINTS):
-                nc.tensor.transpose(w_bank[:, i, :], w_col[:, i : i + 1].to_broadcast([P, P]), ident[:])
+                nc.tensor.transpose(w_bank[:, i, :], w_cols[:, c, i : i + 1].to_broadcast([P, P]), ident[:])
             w_row = keep.tile([P, G, POINTS], F32, name=f"w_row{c}", align_bytes=64)
             nc.scalar.copy(w_row[:], w_bank[:].rearrange("p i g -> p g i"))
             spread[c] = w_row
@@ -111,12 +102,12 @@ def tile_attend_deformable_kernel(tc, vals, ca, cb, cc, cd, aw, wo, offs, offs2,
                 prod = keep.tile([P, J], F32, name=f"prod{t}_{c}", align_bytes=64)
                 if step < first_on_pe:
                     nc.vector.tensor_copy(prod[:], planes[t][:].indirect(lists[c][:]))
-                    bare = psum.tile([G, POINTS, P], F32, name=f"bare{c}", tag=f"bare{c}")
+                    bare = psum.tile([G, POINTS, P], F32, name=f"bare{c}", tag=f"bare{c % 2}")
                     weighted = keep.tile([G, POINTS, P], F32, name=f"weighted{c}")
                     for i in range(POINTS):
                         nc.tensor.transpose(bare[:, i, :], prod[:, i::POINTS], ident[:])
                     for i in range(POINTS):
-                        nc.scalar.activation(weighted[:, i, :], bare[:, i, :], COPY, scale=w_cols[c][:, i : i + 1])
+                        nc.scalar.activation(weighted[:, i, :], bare[:, i, :], COPY, scale=w_cols[:, c, i : i + 1])
                         addends.append(weighted[:, i, :])
                     continue
                 nc.vector.tensor_tensor(

@@ -20,8 +20,9 @@ P = 128
 PACK = 4
 POINTS = J // G
 CORNERS = 4
-PLAIN = 3
-FIRST_DEALT, LAST_DEALT = 8, 12
+STRIPE = 16
+PLAIN = 2
+FIRST_DEALT, LAST_DEALT = 5, 7
 
 
 def tile_attend_deformable_kernel(tc, vals, ca, cb, cc, cd, aw, wo, offs, offs2, offs3, offs4, out):
@@ -30,48 +31,59 @@ def tile_attend_deformable_kernel(tc, vals, ca, cb, cc, cd, aw, wo, offs, offs2,
         keep = ctx.enter_context(tc.tile_pool(name="keep", bufs=1))
         psum = ctx.enter_context(tc.psum_pool(name="psum", bufs=1))
 
-        lists = [keep.tile([P, J // 16], U16, name=f"list{c}") for c in range(CORNERS)]
+        lists = [keep.tile([P, J // STRIPE], U16, name=f"list{c}") for c in range(CORNERS)]
         planes = [keep.tile([P, T], F32, name=f"plane{t}", align_bytes=64) for t in range(PACK)]
-        corner = keep.tile([P, CORNERS, 2 * POINTS], F32)
+        corner = [keep.tile([P, POINTS], F32, name=f"corner{c}") for c in range(CORNERS)]
         att = keep.tile([P, POINTS], F32)
         wo_raw = keep.tile([P, PACK, F], F32)
 
         vals_planes = vals.rearrange("(p t) n -> t p n", t=PACK)
         list_src = (offs, offs2, offs3, offs4)
         corner_src = (ca, cb, cc, cd)
-        spread_order = (3, 0, 1, 2)
+        spread_order = [(PLAIN + n) % CORNERS for n in range(CORNERS)]
         plane_order = (2, 0, 1, 3)
 
-        def load_weights(dst, src):
-            nc.sync.dma_start(dst, src.rearrange("o (g i) -> (o g) i", i=POINTS))
+        def load_weights(queue, tile, src):
+            queue.dma_start(tile[:], src.rearrange("o (g i) -> (o g) i", i=POINTS))
 
-        nc.sync.dma_start(planes[plane_order[0]][:], vals_planes[plane_order[0]])
-        nc.sync.dma_start(lists[0][:], list_src[0])
-        load_weights(att[:], aw)
-        for c in spread_order:
-            load_weights(corner[:, c, 0:POINTS], corner_src[c])
-        nc.sync.dma_start(lists[1][:], list_src[1])
-        nc.sync.dma_start(lists[2][:], list_src[2])
-        nc.sync.dma_start(lists[3][:], list_src[3])
-        for t in plane_order[1:]:
-            nc.sync.dma_start(planes[t][:], vals_planes[t])
+        def load_corner(queue, n):
+            load_weights(queue, corner[spread_order[n]], corner_src[spread_order[n]])
+
+        def load_list(c):
+            nc.sync.dma_start(lists[c][:], list_src[c])
+
+        def load_plane(turn):
+            nc.sync.dma_start(planes[plane_order[turn]][:], vals_planes[plane_order[turn]])
+
+        load_plane(0)
+        load_weights(nc.scalar, att, aw)
+        load_corner(nc.scalar, 0)
+        load_corner(nc.scalar, 1)
+        load_list(0)
+        load_list(1)
+        load_corner(nc.sync, 2)
+        load_corner(nc.sync, 3)
+        load_list(2)
+        load_list(3)
+        for turn in range(1, PACK):
+            load_plane(turn)
         nc.sync.dma_start(wo_raw[:], wo.rearrange("(p t) f -> p t f", t=PACK))
 
         ident = keep.tile([P, P], F32)
         make_identity(nc, ident[:])
 
-        w_cols = keep.tile([P, CORNERS, POINTS], F32)
-        nc.vector.tensor_tensor(
-            w_cols[:], corner[:, :, 0:POINTS], att[:].unsqueeze(1).to_broadcast([P, CORNERS, POINTS]), MULT
-        )
+        w_cols = {}
         spread = {}
-        for c in spread_order:
-            w_bank = psum.tile([P, POINTS, G], F32, name=f"w_bank{c}", tag=f"w_bank{c % 2}")
+        for n, c in enumerate(spread_order):
+            w_col = keep.tile([P, POINTS], F32, name=f"w_col{c}")
+            nc.gpsimd.tensor_tensor(w_col[:], corner[c][:], att[:], MULT)
+            w_bank = psum.tile([P, POINTS, G], F32, name=f"w_bank{c}", tag=f"wide{n}")
             for i in range(POINTS):
-                nc.tensor.transpose(w_bank[:, i, :], w_cols[:, c, i : i + 1].to_broadcast([P, P]), ident[:])
+                nc.tensor.transpose(w_bank[:, i, :], w_col[:, i : i + 1].to_broadcast([P, P]), ident[:])
             w_row = keep.tile([P, G, POINTS], F32, name=f"w_row{c}", align_bytes=64)
             nc.scalar.copy(w_row[:], w_bank[:].rearrange("p i g -> p g i"))
-            spread[c] = w_row
+            w_cols[c] = w_col
+            spread[c] = w_row[:].rearrange("p g i -> p (g i)")
 
         wo_bf = keep.tile([P, PACK, P, PACK], BF16, align_bytes=64)
         wo_dst = wo_bf[:].rearrange("p r m t -> p m t r")
@@ -102,17 +114,15 @@ def tile_attend_deformable_kernel(tc, vals, ca, cb, cc, cd, aw, wo, offs, offs2,
                 prod = keep.tile([P, J], F32, name=f"prod{t}_{c}", align_bytes=64)
                 if step < first_on_pe:
                     nc.vector.tensor_copy(prod[:], planes[t][:].indirect(lists[c][:]))
-                    bare = psum.tile([G, POINTS, P], F32, name=f"bare{c}", tag=f"bare{c % 2}")
+                    bare = psum.tile([G, POINTS, P], F32, name=f"bare{c}", tag=f"wide{c}")
                     weighted = keep.tile([G, POINTS, P], F32, name=f"weighted{c}")
                     for i in range(POINTS):
                         nc.tensor.transpose(bare[:, i, :], prod[:, i::POINTS], ident[:])
                     for i in range(POINTS):
-                        nc.scalar.activation(weighted[:, i, :], bare[:, i, :], COPY, scale=w_cols[:, c, i : i + 1])
+                        nc.scalar.activation(weighted[:, i, :], bare[:, i, :], COPY, scale=w_cols[c][:, i : i + 1])
                         addends.append(weighted[:, i, :])
                     continue
-                nc.vector.tensor_tensor(
-                    prod[:], planes[t][:].indirect(lists[c][:]), spread[c][:].rearrange("p g i -> p (g i)"), MULT
-                )
+                nc.vector.tensor_tensor(prod[:], planes[t][:].indirect(lists[c][:]), spread[c], MULT)
                 if step <= last_on_pe:
                     by_point = [prod[:, i::POINTS] for i in range(POINTS)]
                     if FIRST_DEALT <= turn * CORNERS + step <= LAST_DEALT:
@@ -159,7 +169,7 @@ def tile_attend_deformable_kernel(tc, vals, ca, cb, cc, cd, aw, wo, offs, offs2,
 
         out_rows = out.rearrange("(m r) g -> m r g", r=PACK)
         for h in range(2):
-            y = psum.tile([P, 2, G], F32, name=f"y{h}", tag=f"w_bank{h}")
+            y = psum.tile([P, 2, G], F32, name=f"y{h}", tag=f"wide{h}")
             for r in range(2):
                 nc.tensor.matmul_mx(
                     out=y[:, r, :],

@@ -55,11 +55,11 @@ def tile_attend_deformable_kernel(tc, vals, ca, cb, cc, cd, aw, wo, offs, offs2,
         def load_plane(turn):
             nc.sync.dma_start(planes[plane_order[turn]][:], vals_planes[plane_order[turn]])
 
-        load_plane(0)
-        load_weights(nc.scalar, att, aw)
-        load_corner(nc.scalar, 0)
-        load_corner(nc.scalar, 1)
+        nc.scalar.dma_start(planes[plane_order[0]][:], vals_planes[plane_order[0]])
         load_list(0)
+        load_weights(nc.sync, att, aw)
+        load_corner(nc.sync, 0)
+        load_corner(nc.sync, 1)
         load_list(1)
         load_corner(nc.sync, 2)
         load_corner(nc.sync, 3)
@@ -91,16 +91,18 @@ def tile_attend_deformable_kernel(tc, vals, ca, cb, cc, cd, aw, wo, offs, offs2,
         for q in range(PACK):
             ms = slice(q * P // PACK, (q + 1) * P // PACK)
             nc.scalar.copy(wo_dst[:, ms], wo_src[:, ms])
-        wo_scales = [keep.tile([P, P], U8, align_bytes=64, name=f"wo_scales{r}") for r in range(PACK)]
+        wo_scales = keep.tile([P, F], U8, align_bytes=64)
         wo_codes = []
 
-        def quantise_wo(tag):
+        def quantise_wo(tag, blocks=1):
             r = len(wo_codes)
-            codes = keep.tile([P, P], U32, align_bytes=64, name=f"wo_codes{r}", tag=tag)
+            codes = keep.tile([P, blocks * P], U32, align_bytes=64, name=f"wo_codes{r}", tag=tag)
             nc.vector.quantize_mx(
-                out=codes[:].bitcast(FP8X4), scales=wo_scales[r][:], in_=wo_bf[:, r].rearrange("p m t -> p (m t)")
+                out=codes[:].bitcast(FP8X4),
+                scales=wo_scales[:, r * P : (r + blocks) * P],
+                in_=wo_bf[:, r : r + blocks].rearrange("p r m t -> p (r m t)"),
             )
-            wo_codes.append(codes)
+            wo_codes.extend(codes[:, n * P : (n + 1) * P] for n in range(blocks))
 
         b_bf = keep.tile([P, G, PACK], BF16, align_bytes=64)
         for turn, t in enumerate(plane_order):
@@ -122,7 +124,11 @@ def tile_attend_deformable_kernel(tc, vals, ca, cb, cc, cd, aw, wo, offs, offs2,
                         nc.scalar.activation(weighted[:, i, :], bare[:, i, :], COPY, scale=w_cols[c][:, i : i + 1])
                         addends.append(weighted[:, i, :])
                     continue
-                nc.vector.tensor_tensor(prod[:], planes[t][:].indirect(lists[c][:]), spread[c], MULT)
+                pieces = 2 if step > last_on_pe else 1
+                for h in range(pieces):
+                    js = slice(h * J // pieces, (h + 1) * J // pieces)
+                    offsets = lists[c][:, js.start // STRIPE : js.stop // STRIPE]
+                    nc.vector.tensor_tensor(prod[:, js], planes[t][:].indirect(offsets), spread[c][:, js], MULT)
                 if step <= last_on_pe:
                     by_point = [prod[:, i::POINTS] for i in range(POINTS)]
                     if FIRST_DEALT <= turn * CORNERS + step <= LAST_DEALT:
@@ -140,7 +146,7 @@ def tile_attend_deformable_kernel(tc, vals, ca, cb, cc, cd, aw, wo, offs, offs2,
                             start=(step == first_on_pe and i == 0),
                             stop=(step == last_on_pe and i == POINTS - 1),
                         )
-            turned = keep.tile([G, P], F32, name=f"turned{t}")
+            turned = keep.tile([G, P], F32, name=f"turned{t}", align_bytes=64)
             nc.scalar.copy(turned[:], acc[:])
             addends.append(turned[:])
             back = psum.tile([P, G], F32, name=f"back{t}", tag=f"back{turn % 2}")
@@ -149,14 +155,14 @@ def tile_attend_deformable_kernel(tc, vals, ca, cb, cc, cd, aw, wo, offs, offs2,
                     back[:], lhsT=addend, rhs=ident[:], is_transpose=True, start=(n == 0), stop=(n == len(addends) - 1)
                 )
             if last_plane:
-                quantise_wo(f"w_row{order[-2]}")
                 rest = keep.tile([P, G], F32, align_bytes=64)
-                nc.vector.tensor_reduce(
-                    rest[:], prod[:].rearrange("p (g i) -> p g i", i=POINTS), mybir.AxisListType.X, ADD
-                )
+                by_query = prod[:].rearrange("p (g i) -> p g i", i=POINTS)
+                for h in range(pieces):
+                    gs = slice(h * G // pieces, (h + 1) * G // pieces)
+                    nc.vector.tensor_reduce(rest[:, gs], by_query[:, gs], mybir.AxisListType.X, ADD)
                 quantise_wo(f"w_row{c}")
                 nc.vector.tensor_tensor(b_bf[:, :, t], back[:], rest[:], ADD)
-                quantise_wo(f"prod{t}_{c}")
+                quantise_wo(f"turned{t}")
             else:
                 nc.scalar.copy(b_bf[:, :, t], back[:])
 
@@ -165,25 +171,23 @@ def tile_attend_deformable_kernel(tc, vals, ca, cb, cc, cd, aw, wo, offs, offs2,
         nc.vector.quantize_mx(
             out=b_codes[:].bitcast(FP8X4), scales=b_scales[:], in_=b_bf[:].rearrange("p g t -> p (g t)")
         )
-        quantise_wo("rest")
+        quantise_wo("rest", blocks=2)
 
         out_rows = out.rearrange("(m r) g -> m r g", r=PACK)
-        for h in range(2):
-            y = psum.tile([P, 2, G], F32, name=f"y{h}", tag=f"wide{h}")
-            for r in range(2):
-                nc.tensor.matmul_mx(
-                    out=y[:, r, :],
-                    lhsT=wo_codes[2 * h + r][:].bitcast(FP8X4),
-                    lhsT_scale=wo_scales[2 * h + r][:],
-                    rhs=b_codes[:].bitcast(FP8X4),
-                    rhs_scale=b_scales[:],
-                    start=True,
-                    stop=True,
-                )
-            y_sb = keep.tile([P, 2, G], F32, name=f"y_sb{h}")
-            if h == 0:
-                nc.scalar.copy(y_sb[:], y[:])
-                nc.scalar.dma_start(out_rows[:, 2 * h : 2 * h + 2, :], y_sb[:])
-            else:
+        for r in range(PACK):
+            y = psum.tile([P, G], F32, name=f"y{r}", tag=f"wide{r}")
+            nc.tensor.matmul_mx(
+                out=y[:],
+                lhsT=wo_codes[r].bitcast(FP8X4),
+                lhsT_scale=wo_scales[:, r * P : (r + 1) * P],
+                rhs=b_codes[:].bitcast(FP8X4),
+                rhs_scale=b_scales[:],
+                start=True,
+                stop=True,
+            )
+            y_sb = keep.tile([P, G], F32, name=f"y_sb{r}")
+            if r % 2 == 0:
                 nc.vector.tensor_copy(y_sb[:], y[:])
-                nc.sync.dma_start(out_rows[:, 2 * h : 2 * h + 2, :], y_sb[:])
+            else:
+                nc.scalar.copy(y_sb[:], y[:])
+            (nc.scalar if r == PACK - 1 else nc.sync).dma_start(out_rows[:, r, :], y_sb[:])

@@ -185,9 +185,10 @@ def tile_attend_deformable_kernel(tc, vals, ca, cb, cc, cd, aw, wo, offs, offs2,
                 start=True,
                 stop=True,
             )
-            y_sb = keep.tile([P, G], F32, name=f"y_sb{r}")
             if r % 2 == 0:
-                nc.vector.tensor_copy(y_sb[:], y[:])
+                y_sb = keep.tile([P, 2, G], F32, name=f"y_sb{r}")
+                nc.vector.tensor_copy(y_sb[:, 0, :], y[:])
             else:
-                nc.scalar.copy(y_sb[:], y[:])
-            (nc.scalar if r == PACK - 1 else nc.sync).dma_start(out_rows[:, r, :], y_sb[:])
+                nc.scalar.copy(y_sb[:, 1, :], y[:])
+                queue = nc.scalar if r == PACK - 1 else nc.sync
+                queue.dma_start(out_rows[:, r - 1 : r + 1, :], y_sb[:])

@@ -23,6 +23,7 @@ CORNERS = 4
 STRIPE = 16
 PLAIN = 2
 FIRST_DEALT, LAST_DEALT = 5, 7
+CUT = 384
 
 
 def tile_attend_deformable_kernel(tc, vals, ca, cb, cc, cd, aw, wo, offs, offs2, offs3, offs4, out):
@@ -104,6 +105,11 @@ def tile_attend_deformable_kernel(tc, vals, ca, cb, cc, cd, aw, wo, offs, offs2,
             )
             wo_codes.extend(codes[:, n * P : (n + 1) * P] for n in range(blocks))
 
+        def gather(dst, t, c, j0, j1):
+            offsets = lists[c][:, j0 // STRIPE : j1 // STRIPE]
+            nc.vector.tensor_tensor(dst, planes[t][:].indirect(offsets), spread[c][:, j0:j1], MULT)
+
+        on_vector = keep.tile([P, 2 * J - CUT], F32, align_bytes=64)
         b_bf = keep.tile([P, G, PACK], BF16, align_bytes=64)
         for turn, t in enumerate(plane_order):
             last_plane = turn == PACK - 1
@@ -113,7 +119,10 @@ def tile_attend_deformable_kernel(tc, vals, ca, cb, cc, cd, aw, wo, offs, offs2,
             last_on_pe = CORNERS - 2 if last_plane else CORNERS - 1
             addends = []
             for step, c in enumerate(order):
-                prod = keep.tile([P, J], F32, name=f"prod{t}_{c}", align_bytes=64)
+                if last_plane and step > last_on_pe:
+                    prod = on_vector[:, :J]
+                else:
+                    prod = keep.tile([P, J], F32, name=f"prod{t}_{c}", align_bytes=64)
                 if step < first_on_pe:
                     nc.vector.tensor_copy(prod[:], planes[t][:].indirect(lists[c][:]))
                     bare = psum.tile([G, POINTS, P], F32, name=f"bare{c}", tag=f"wide{c}")
@@ -124,11 +133,15 @@ def tile_attend_deformable_kernel(tc, vals, ca, cb, cc, cd, aw, wo, offs, offs2,
                         nc.scalar.activation(weighted[:, i, :], bare[:, i, :], COPY, scale=w_cols[c][:, i : i + 1])
                         addends.append(weighted[:, i, :])
                     continue
-                pieces = 2 if step > last_on_pe else 1
-                for h in range(pieces):
-                    js = slice(h * J // pieces, (h + 1) * J // pieces)
-                    offsets = lists[c][:, js.start // STRIPE : js.stop // STRIPE]
-                    nc.vector.tensor_tensor(prod[:, js], planes[t][:].indirect(offsets), spread[c][:, js], MULT)
+                if last_plane and step == last_on_pe:
+                    nc.vector.memset(prod[:, CUT:], 0.0)
+                    gather(prod[:, :CUT], t, c, 0, CUT)
+                elif last_plane and step > last_on_pe:
+                    gather(prod[:, :CUT], t, c, 0, CUT)
+                    gather(on_vector[:, J:], t, order[last_on_pe], CUT, J)
+                    gather(prod[:, CUT:], t, c, CUT, J)
+                else:
+                    gather(prod[:], t, c, 0, J)
                 if step <= last_on_pe:
                     by_point = [prod[:, i::POINTS] for i in range(POINTS)]
                     if FIRST_DEALT <= turn * CORNERS + step <= LAST_DEALT:
@@ -156,13 +169,13 @@ def tile_attend_deformable_kernel(tc, vals, ca, cb, cc, cd, aw, wo, offs, offs2,
                 )
             if last_plane:
                 rest = keep.tile([P, G], F32, align_bytes=64)
-                by_query = prod[:].rearrange("p (g i) -> p g i", i=POINTS)
-                for h in range(pieces):
-                    gs = slice(h * G // pieces, (h + 1) * G // pieces)
-                    nc.vector.tensor_reduce(rest[:, gs], by_query[:, gs], mybir.AxisListType.X, ADD)
-                quantise_wo(f"w_row{c}")
-                nc.vector.tensor_tensor(b_bf[:, :, t], back[:], rest[:], ADD)
-                quantise_wo(f"turned{t}")
+                one = on_vector[:, :CUT].rearrange("p (g i) -> p g i", i=POINTS)
+                two = on_vector[:, CUT:].rearrange("p (c g i) -> p g c i", c=2, i=POINTS)
+                nc.vector.tensor_reduce(rest[:, : CUT // POINTS], one, mybir.AxisListType.X, ADD)
+                nc.vector.tensor_reduce(rest[:, CUT // POINTS :], two, mybir.AxisListType.XY, ADD)
+                for gs in (slice(0, CUT // POINTS), slice(CUT // POINTS, G)):
+                    nc.vector.tensor_tensor(b_bf[:, gs, t], back[:, gs], rest[:, gs], ADD)
+                quantise_wo(f"turned{t}", blocks=2)
             else:
                 nc.scalar.copy(b_bf[:, :, t], back[:])
 

@@ -133,12 +133,12 @@ def tile_attend_deformable_kernel(tc, vals, ca, cb, cc, cd, aw, wo, offs, offs2,
                         nc.scalar.activation(weighted[:, i, :], bare[:, i, :], COPY, scale=w_cols[c][:, i : i + 1])
                         addends.append(weighted[:, i, :])
                     continue
-                if last_plane and step == last_on_pe:
+                if last_plane and step == 0:
                     nc.vector.memset(prod[:, CUT:], 0.0)
                     gather(prod[:, :CUT], t, c, 0, CUT)
                 elif last_plane and step > last_on_pe:
                     gather(prod[:, :CUT], t, c, 0, CUT)
-                    gather(on_vector[:, J:], t, order[last_on_pe], CUT, J)
+                    gather(on_vector[:, J:], t, order[0], CUT, J)
                     gather(prod[:, CUT:], t, c, CUT, J)
                 else:
                     gather(prod[:], t, c, 0, J)

@@ -137,9 +137,8 @@ def tile_attend_deformable_kernel(tc, vals, ca, cb, cc, cd, aw, wo, offs, offs2,
                     nc.vector.memset(prod[:, CUT:], 0.0)
                     gather(prod[:, :CUT], t, c, 0, CUT)
                 elif last_plane and step > last_on_pe:
-                    gather(prod[:, :CUT], t, c, 0, CUT)
+                    gather(prod, t, c, 0, J)
                     gather(on_vector[:, J:], t, order[0], CUT, J)
-                    gather(prod[:, CUT:], t, c, CUT, J)
                 else:
                     gather(prod[:], t, c, 0, J)
                 if step <= last_on_pe:

@@ -86,12 +86,6 @@ def tile_attend_deformable_kernel(tc, vals, ca, cb, cc, cd, aw, wo, offs, offs2,
             w_cols[c] = w_col
             spread[c] = w_row[:].rearrange("p g i -> p (g i)")
 
-        wo_bf = keep.tile([P, PACK, P, PACK], BF16, align_bytes=64)
-        wo_dst = wo_bf[:].rearrange("p r m t -> p m t r")
-        wo_src = wo_raw[:].rearrange("p t (m r) -> p m t r", r=PACK)
-        for q in range(PACK):
-            ms = slice(q * P // PACK, (q + 1) * P // PACK)
-            nc.scalar.copy(wo_dst[:, ms], wo_src[:, ms])
         wo_scales = keep.tile([P, F], U8, align_bytes=64)
         wo_codes = []
 
@@ -177,6 +171,13 @@ def tile_attend_deformable_kernel(tc, vals, ca, cb, cc, cd, aw, wo, offs, offs2,
                 quantise_wo(f"turned{t}", blocks=2)
             else:
                 nc.scalar.copy(b_bf[:, :, t], back[:])
+            if turn == 1:
+                wo_bf = keep.tile([P, PACK, P, PACK], BF16, tag=f"dealt{t}_{spread_order[-1]}", align_bytes=64)
+                wo_dst = wo_bf[:].rearrange("p r m t -> p m t r")
+                wo_src = wo_raw[:].rearrange("p t (m r) -> p m t r", r=PACK)
+                for q in range(PACK):
+                    ms = slice(q * P // PACK, (q + 1) * P // PACK)
+                    nc.scalar.copy(wo_dst[:, ms], wo_src[:, ms])
 
         b_codes = keep.tile([P, G], U32, align_bytes=64)
         b_scales = keep.tile([P, G], U8, align_bytes=64)

@@ -22,7 +22,6 @@ POINTS = J // G
 CORNERS = 4
 STRIPE = 16
 PLAIN = 2
-FIRST_DEALT, LAST_DEALT = 5, 7
 CUT = 384
 
 
@@ -137,12 +136,6 @@ def tile_attend_deformable_kernel(tc, vals, ca, cb, cc, cd, aw, wo, offs, offs2,
                     gather(prod[:], t, c, 0, J)
                 if step <= last_on_pe:
                     by_point = [prod[:, i::POINTS] for i in range(POINTS)]
-                    if FIRST_DEALT <= turn * CORNERS + step <= LAST_DEALT:
-                        dealt = keep.tile([P, POINTS, G], F32, name=f"dealt{t}_{c}", align_bytes=64)
-                        nc.scalar.copy(
-                            dealt[:].rearrange("p i g -> p g i"), prod[:].rearrange("p (g i) -> p g i", i=POINTS)
-                        )
-                        by_point = [dealt[:, i, :] for i in range(POINTS)]
                     for i in range(POINTS):
                         nc.tensor.matmul(
                             acc[:],
@@ -172,7 +165,7 @@ def tile_attend_deformable_kernel(tc, vals, ca, cb, cc, cd, aw, wo, offs, offs2,
             else:
                 nc.scalar.copy(b_bf[:, :, t], back[:])
             if turn == 1:
-                wo_bf = keep.tile([P, PACK, P, PACK], BF16, tag=f"dealt{t}_{spread_order[-1]}", align_bytes=64)
+                wo_bf = keep.tile([P, PACK, P, PACK], BF16, tag=f"prod{t}_{spread_order[-1]}", align_bytes=64)
                 wo_dst = wo_bf[:].rearrange("p r m t -> p m t r")
                 wo_src = wo_raw[:].rearrange("p t (m r) -> p m t r", r=PACK)
                 for q in range(PACK):

@@ -21,7 +21,6 @@ PACK = 4
 POINTS = J // G
 CORNERS = 4
 STRIPE = 16
-PLAIN = 2
 CUT = 384
 
 
@@ -40,55 +39,81 @@ def tile_attend_deformable_kernel(tc, vals, ca, cb, cc, cd, aw, wo, offs, offs2,
         vals_planes = vals.rearrange("(p t) n -> t p n", t=PACK)
         list_src = (offs, offs2, offs3, offs4)
         corner_src = (ca, cb, cc, cd)
-        spread_order = [(PLAIN + n) % CORNERS for n in range(CORNERS)]
-        plane_order = (2, 0, 1, 3)
 
-        def load_weights(queue, tile, src):
-            queue.dma_start(tile[:], src.rearrange("o (g i) -> (o g) i", i=POINTS))
+        def load_weights(tile, src):
+            nc.sync.dma_start(tile[:], src.rearrange("o (g i) -> (o g) i", i=POINTS))
 
-        def load_corner(queue, n):
-            load_weights(queue, corner[spread_order[n]], corner_src[spread_order[n]])
+        def load_corner(c):
+            load_weights(corner[c], corner_src[c])
 
         def load_list(c):
             nc.sync.dma_start(lists[c][:], list_src[c])
 
-        def load_plane(turn):
-            nc.sync.dma_start(planes[plane_order[turn]][:], vals_planes[plane_order[turn]])
+        def load_plane(t):
+            nc.sync.dma_start(planes[t][:], vals_planes[t])
 
-        nc.scalar.dma_start(planes[plane_order[0]][:], vals_planes[plane_order[0]])
+        nc.scalar.dma_start(planes[0][:], vals_planes[0])
         load_list(0)
-        load_weights(nc.sync, att, aw)
-        load_corner(nc.sync, 0)
-        load_corner(nc.sync, 1)
         load_list(1)
-        load_corner(nc.sync, 2)
-        load_corner(nc.sync, 3)
+        load_weights(att, aw)
+        load_corner(1)
+        load_corner(2)
         load_list(2)
+        load_corner(3)
+        load_plane(1)
         load_list(3)
-        for turn in range(1, PACK):
-            load_plane(turn)
+        load_corner(0)
+        load_plane(2)
+        load_plane(3)
         nc.sync.dma_start(wo_raw[:], wo.rearrange("(p t) f -> p t f", t=PACK))
 
         ident = keep.tile([P, P], F32)
         make_identity(nc, ident[:])
 
-        w_cols = {}
-        spread = {}
-        for n, c in enumerate(spread_order):
+        w_banks = {}
+        w_rows = {}
+        for c in (1, 2, 3, 0):
             w_col = keep.tile([P, POINTS], F32, name=f"w_col{c}")
             nc.gpsimd.tensor_tensor(w_col[:], corner[c][:], att[:], MULT)
-            w_bank = psum.tile([P, POINTS, G], F32, name=f"w_bank{c}", tag=f"wide{n}")
+            w_bank = psum.tile([P, POINTS, G], F32, name=f"w_bank{c}", tag=f"wide{c}")
             for i in range(POINTS):
                 nc.tensor.transpose(w_bank[:, i, :], w_col[:, i : i + 1].to_broadcast([P, P]), ident[:])
+            w_banks[c] = w_bank[:].rearrange("p i g -> p g i")
+
+        def offsets(c, j0, j1):
+            return lists[c][:, j0 // STRIPE : j1 // STRIPE]
+
+        def gather_weighted(dst, t, c, j0, j1):
+            nc.vector.tensor_tensor(dst, planes[t][:].indirect(offsets(c, j0, j1)), w_rows[c][:, j0:j1], MULT)
+
+        bare = {}
+
+        def gather_bare(dst, t, c):
+            bare[t, c] = dst
+            window = planes[t][:].indirect(lists[c][:])
+            if (t, c) == (0, 1):
+                nc.vector.tensor_copy(dst, window)
+            else:
+                nc.scalar.activation(dst, window, COPY)
+
+        def gather_pair(t):
+            pair = keep.tile([P, 2, J], F32, name=f"pair{t}", tag=f"pair{t % 2}", align_bytes=64)
+            gather_bare(pair[:, 0, :], t, 0)
+            gather_bare(pair[:, 1, :], t, 1)
+
+        first_scalar = keep.tile([P, J], F32, align_bytes=64, tag="pair0")
+        first_vector = keep.tile([P, J], F32, align_bytes=64, tag="pair1")
+        gather_bare(first_scalar[:], 0, 0)
+        gather_bare(first_vector[:], 0, 1)
+        for c in (2, 3):
             w_row = keep.tile([P, G, POINTS], F32, name=f"w_row{c}", align_bytes=64)
-            nc.scalar.copy(w_row[:], w_bank[:].rearrange("p i g -> p g i"))
-            w_cols[c] = w_col
-            spread[c] = w_row[:].rearrange("p g i -> p (g i)")
+            nc.scalar.copy(w_row[:], w_banks[c])
+            w_rows[c] = w_row[:].rearrange("p g i -> p (g i)")
 
         wo_scales = keep.tile([P, F], U8, align_bytes=64)
         wo_codes = []
 
-        def quantise_wo(tag, blocks=1):
+        def quantise_wo(tag, blocks):
             r = len(wo_codes)
             codes = keep.tile([P, blocks * P], U32, align_bytes=64, name=f"wo_codes{r}", tag=tag)
             nc.vector.quantize_mx(
@@ -98,61 +123,53 @@ def tile_attend_deformable_kernel(tc, vals, ca, cb, cc, cd, aw, wo, offs, offs2,
             )
             wo_codes.extend(codes[:, n * P : (n + 1) * P] for n in range(blocks))
 
-        def gather(dst, t, c, j0, j1):
-            offsets = lists[c][:, j0 // STRIPE : j1 // STRIPE]
-            nc.vector.tensor_tensor(dst, planes[t][:].indirect(offsets), spread[c][:, j0:j1], MULT)
-
         on_vector = keep.tile([P, 2 * J - CUT], F32, align_bytes=64)
         b_bf = keep.tile([P, G, PACK], BF16, align_bytes=64)
-        for turn, t in enumerate(plane_order):
-            last_plane = turn == PACK - 1
-            acc = psum.tile([G, P], F32, name=f"acc{t}", tag=f"acc{turn % 2}")
-            order = range(CORNERS) if turn == 0 else spread_order
-            first_on_pe = PLAIN if turn == 0 else 0
-            last_on_pe = CORNERS - 2 if last_plane else CORNERS - 1
-            addends = []
+        for t in range(PACK):
+            last_plane = t == PACK - 1
+            acc = psum.tile([G, P], F32, name=f"acc{t}", tag=f"acc{t % 2}")
+            order = (1, 2, 3, 0) if t == 0 else (0, 1, 2) if last_plane else (2, 3, 0, 1)
             for step, c in enumerate(order):
-                if last_plane and step > last_on_pe:
-                    prod = on_vector[:, :J]
+                prod = keep.tile([P, J], F32, name=f"prod{t}_{c}", align_bytes=64)
+                if (t, c) in bare:
+                    nc.vector.tensor_tensor(
+                        prod[:].rearrange("p (g i) -> p g i", i=POINTS),
+                        bare[t, c].rearrange("p (g i) -> p g i", i=POINTS),
+                        w_banks[c],
+                        MULT,
+                    )
+                elif last_plane:
+                    nc.gpsimd.memset(prod[:, CUT:], 0.0)
+                    gather_weighted(prod[:, :CUT], t, c, 0, CUT)
                 else:
-                    prod = keep.tile([P, J], F32, name=f"prod{t}_{c}", align_bytes=64)
-                if step < first_on_pe:
-                    nc.vector.tensor_copy(prod[:], planes[t][:].indirect(lists[c][:]))
-                    bare = psum.tile([G, POINTS, P], F32, name=f"bare{c}", tag=f"wide{c}")
-                    weighted = keep.tile([G, POINTS, P], F32, name=f"weighted{c}")
-                    for i in range(POINTS):
-                        nc.tensor.transpose(bare[:, i, :], prod[:, i::POINTS], ident[:])
-                    for i in range(POINTS):
-                        nc.scalar.activation(weighted[:, i, :], bare[:, i, :], COPY, scale=w_cols[c][:, i : i + 1])
-                        addends.append(weighted[:, i, :])
-                    continue
-                if last_plane and step == 0:
-                    nc.vector.memset(prod[:, CUT:], 0.0)
-                    gather(prod[:, :CUT], t, c, 0, CUT)
-                elif last_plane and step > last_on_pe:
-                    gather(prod, t, c, 0, J)
-                    gather(on_vector[:, J:], t, order[0], CUT, J)
-                else:
-                    gather(prod[:], t, c, 0, J)
-                if step <= last_on_pe:
-                    by_point = [prod[:, i::POINTS] for i in range(POINTS)]
-                    for i in range(POINTS):
-                        nc.tensor.matmul(
-                            acc[:],
-                            lhsT=by_point[i],
-                            rhs=ident[:],
-                            is_transpose=True,
-                            start=(step == first_on_pe and i == 0),
-                            stop=(step == last_on_pe and i == POINTS - 1),
-                        )
+                    gather_weighted(prod[:], t, c, 0, J)
+                for i in range(POINTS):
+                    nc.tensor.matmul(
+                        acc[:],
+                        lhsT=prod[:, i::POINTS],
+                        rhs=ident[:],
+                        is_transpose=True,
+                        start=(step == 0 and i == 0),
+                        stop=(step == len(order) - 1 and i == POINTS - 1),
+                    )
+                if t == 0 and step == 0:
+                    gather_pair(1)
+            if t + 2 < PACK:
+                gather_pair(t + 2)
+            if t == 1:
+                wo_bf = keep.tile([P, PACK, P, PACK], BF16, align_bytes=64, tag="prod0_0")
+                wo_dst = wo_bf[:].rearrange("p r m t -> p m t r")
+                wo_src = wo_raw[:].rearrange("p t (m r) -> p m t r", r=PACK)
+                for q in range(PACK):
+                    ms = slice(q * P // PACK, (q + 1) * P // PACK)
+                    nc.scalar.copy(wo_dst[:, ms], wo_src[:, ms])
+            if last_plane:
+                gather_weighted(on_vector[:, :J], t, 3, 0, J)
+                gather_weighted(on_vector[:, J:], t, 2, CUT, J)
             turned = keep.tile([G, P], F32, name=f"turned{t}", align_bytes=64)
             nc.scalar.copy(turned[:], acc[:])
-            addends.append(turned[:])
-            back = psum.tile([P, G], F32, name=f"back{t}", tag=f"back{turn % 2}")
-            for n, addend in enumerate(addends):
-                nc.tensor.matmul(
-                    back[:], lhsT=addend, rhs=ident[:], is_transpose=True, start=(n == 0), stop=(n == len(addends) - 1)
-                )
+            back = psum.tile([P, G], F32, name=f"back{t}", tag=f"back{t % 2}")
+            nc.tensor.transpose(back[:], turned[:], ident[:])
             if last_plane:
                 rest = keep.tile([P, G], F32, align_bytes=64)
                 one = on_vector[:, :CUT].rearrange("p (g i) -> p g i", i=POINTS)
@@ -161,23 +178,16 @@ def tile_attend_deformable_kernel(tc, vals, ca, cb, cc, cd, aw, wo, offs, offs2,
                 nc.vector.tensor_reduce(rest[:, CUT // POINTS :], two, mybir.AxisListType.XY, ADD)
                 for gs in (slice(0, CUT // POINTS), slice(CUT // POINTS, G)):
                     nc.vector.tensor_tensor(b_bf[:, gs, t], back[:, gs], rest[:, gs], ADD)
-                quantise_wo(f"turned{t}", blocks=2)
+                quantise_wo(f"turned{t}", 2)
             else:
                 nc.scalar.copy(b_bf[:, :, t], back[:])
-            if turn == 1:
-                wo_bf = keep.tile([P, PACK, P, PACK], BF16, tag=f"prod{t}_{spread_order[-1]}", align_bytes=64)
-                wo_dst = wo_bf[:].rearrange("p r m t -> p m t r")
-                wo_src = wo_raw[:].rearrange("p t (m r) -> p m t r", r=PACK)
-                for q in range(PACK):
-                    ms = slice(q * P // PACK, (q + 1) * P // PACK)
-                    nc.scalar.copy(wo_dst[:, ms], wo_src[:, ms])
 
         b_codes = keep.tile([P, G], U32, align_bytes=64)
         b_scales = keep.tile([P, G], U8, align_bytes=64)
         nc.vector.quantize_mx(
             out=b_codes[:].bitcast(FP8X4), scales=b_scales[:], in_=b_bf[:].rearrange("p g t -> p (g t)")
         )
-        quantise_wo("rest", blocks=2)
+        quantise_wo("rest", 2)
 
         out_rows = out.rearrange("(m r) g -> m r g", r=PACK)
         for r in range(PACK):

@@ -22,6 +22,7 @@ POINTS = J // G
 CORNERS = 4
 STRIPE = 16
 CUT = 384
+TAIL = 2 * J - CUT - J // 2
 
 
 def tile_attend_deformable_kernel(tc, vals, ca, cb, cc, cd, aw, wo, offs, offs2, offs3, offs4, out):
@@ -52,17 +53,17 @@ def tile_attend_deformable_kernel(tc, vals, ca, cb, cc, cd, aw, wo, offs, offs2,
         def load_plane(t):
             nc.sync.dma_start(planes[t][:], vals_planes[t])
 
-        nc.scalar.dma_start(planes[0][:], vals_planes[0])
         load_list(0)
-        load_list(1)
-        load_weights(att, aw)
-        load_corner(1)
-        load_corner(2)
+        nc.scalar.dma_start(planes[0][:], vals_planes[0])
         load_list(2)
+        load_weights(att, aw)
+        load_corner(2)
+        load_corner(0)
+        load_corner(1)
+        load_list(1)
         load_corner(3)
         load_plane(1)
         load_list(3)
-        load_corner(0)
         load_plane(2)
         load_plane(3)
         nc.sync.dma_start(wo_raw[:], wo.rearrange("(p t) f -> p t f", t=PACK))
@@ -72,7 +73,7 @@ def tile_attend_deformable_kernel(tc, vals, ca, cb, cc, cd, aw, wo, offs, offs2,
 
         w_banks = {}
         w_rows = {}
-        for c in (1, 2, 3, 0):
+        for c in (2, 0, 1, 3):
             w_col = keep.tile([P, POINTS], F32, name=f"w_col{c}")
             nc.gpsimd.tensor_tensor(w_col[:], corner[c][:], att[:], MULT)
             w_bank = psum.tile([P, POINTS, G], F32, name=f"w_bank{c}", tag=f"wide{c}")
@@ -86,32 +87,61 @@ def tile_attend_deformable_kernel(tc, vals, ca, cb, cc, cd, aw, wo, offs, offs2,
         def gather_weighted(dst, t, c, j0, j1):
             nc.vector.tensor_tensor(dst, planes[t][:].indirect(offsets(c, j0, j1)), w_rows[c][:, j0:j1], MULT)
 
+        slot = {}
+
+        def columns(name, after=None, width=J):
+            slot[name] = slot[after] if after else name
+            return keep.tile([P, width], F32, name=name, tag=slot[name], align_bytes=64)
+
         bare = {}
 
-        def gather_bare(dst, t, c):
+        def gather_bare(t, c, after=None):
+            if (t, c) == (PACK - 1, 1):
+                tail = columns("tail", after, TAIL + J)
+                bare["tail"] = tail
+                dst = tail[:, TAIL:]
+            else:
+                dst = columns(f"bare{t}_{c}", after)[:]
             bare[t, c] = dst
             window = planes[t][:].indirect(lists[c][:])
-            if (t, c) == (0, 1):
+            if c == 2:
                 nc.vector.tensor_copy(dst, window)
             else:
                 nc.scalar.activation(dst, window, COPY)
 
-        def gather_pair(t):
-            pair = keep.tile([P, 2, J], F32, name=f"pair{t}", tag=f"pair{t % 2}", align_bytes=64)
-            gather_bare(pair[:, 0, :], t, 0)
-            gather_bare(pair[:, 1, :], t, 1)
-
-        first_scalar = keep.tile([P, J], F32, align_bytes=64, tag="pair0")
-        first_vector = keep.tile([P, J], F32, align_bytes=64, tag="pair1")
-        gather_bare(first_scalar[:], 0, 0)
-        gather_bare(first_vector[:], 0, 1)
-        for c in (2, 3):
+        def copy_row(copy, c):
             w_row = keep.tile([P, G, POINTS], F32, name=f"w_row{c}", align_bytes=64)
-            nc.scalar.copy(w_row[:], w_banks[c])
+            copy(w_row[:], w_banks[c])
             w_rows[c] = w_row[:].rearrange("p g i -> p (g i)")
+
+        def weigh(prod, t, c, g0, g1):
+            nc.vector.tensor_tensor(
+                prod[:].rearrange("p (g i) -> p g i", i=POINTS)[:, g0:g1],
+                bare[t, c].rearrange("p (g i) -> p g i", i=POINTS)[:, g0:g1],
+                w_banks[c][:, g0:g1],
+                MULT,
+            )
+
+        short = columns("short")
+        zero = keep.tile([P, 1], F32)
+        nc.vector.memset(zero[:], 0.0)
+        nc.scalar.activation(short[:, CUT:], zero[:].to_broadcast([P, J - CUT]), COPY)
+        gather_bare(0, 0)
+        gather_bare(0, 2)
+        gather_bare(0, 1)
 
         wo_scales = keep.tile([P, F], U8, align_bytes=64)
         wo_codes = []
+
+        wo_bf = []
+
+        def round_wo(half, tag):
+            rounded = keep.tile([P, 2, P, PACK], BF16, align_bytes=64, name=f"wo_bf{half}", tag=tag)
+            src = wo_raw[:].rearrange("p t (m r) -> p m t r", r=PACK)[:, :, :, 2 * half : 2 * half + 2]
+            dst = rounded[:].rearrange("p r m t -> p m t r")
+            for ms in (slice(0, P // 2), slice(P // 2, P)):
+                nc.scalar.copy(dst[:, ms], src[:, ms])
+            wo_bf.append(rounded)
 
         def quantise_wo(tag, blocks):
             r = len(wo_codes)
@@ -119,27 +149,24 @@ def tile_attend_deformable_kernel(tc, vals, ca, cb, cc, cd, aw, wo, offs, offs2,
             nc.vector.quantize_mx(
                 out=codes[:].bitcast(FP8X4),
                 scales=wo_scales[:, r * P : (r + blocks) * P],
-                in_=wo_bf[:, r : r + blocks].rearrange("p r m t -> p (r m t)"),
+                in_=wo_bf[r // 2][:].rearrange("p r m t -> p (r m t)"),
             )
             wo_codes.extend(codes[:, n * P : (n + 1) * P] for n in range(blocks))
 
-        on_vector = keep.tile([P, 2 * J - CUT], F32, align_bytes=64)
         b_bf = keep.tile([P, G, PACK], BF16, align_bytes=64)
+        accs = []
         for t in range(PACK):
             last_plane = t == PACK - 1
-            acc = psum.tile([G, P], F32, name=f"acc{t}", tag=f"acc{t % 2}")
-            order = (1, 2, 3, 0) if t == 0 else (0, 1, 2) if last_plane else (2, 3, 0, 1)
+            acc = psum.tile([G, P], F32, name=f"acc{t}", tag=("acc0", "acc1", "wide3", "wide2")[t])
+            order = (2, 0, 1) if last_plane else (2, 0, 1, 3) if t == 0 else (2, 3, 0, 1)
             for step, c in enumerate(order):
-                prod = keep.tile([P, J], F32, name=f"prod{t}_{c}", align_bytes=64)
-                if (t, c) in bare:
-                    nc.vector.tensor_tensor(
-                        prod[:].rearrange("p (g i) -> p g i", i=POINTS),
-                        bare[t, c].rearrange("p (g i) -> p g i", i=POINTS),
-                        w_banks[c],
-                        MULT,
-                    )
+                prod = short if (t, c) == (PACK - 1, 2) else columns(f"prod{t}_{c}")
+                if (t, c) == (PACK - 1, 1):
+                    weigh(prod, t, c, 0, G // 2)
+                    weigh(prod, t, c, G // 2, G)
+                elif (t, c) in bare:
+                    weigh(prod, t, c, 0, G)
                 elif last_plane:
-                    nc.gpsimd.memset(prod[:, CUT:], 0.0)
                     gather_weighted(prod[:, :CUT], t, c, 0, CUT)
                 else:
                     gather_weighted(prod[:], t, c, 0, J)
@@ -152,35 +179,44 @@ def tile_attend_deformable_kernel(tc, vals, ca, cb, cc, cd, aw, wo, offs, offs2,
                         start=(step == 0 and i == 0),
                         stop=(step == len(order) - 1 and i == POINTS - 1),
                     )
-                if t == 0 and step == 0:
-                    gather_pair(1)
-            if t + 2 < PACK:
-                gather_pair(t + 2)
-            if t == 1:
-                wo_bf = keep.tile([P, PACK, P, PACK], BF16, align_bytes=64, tag="prod0_0")
-                wo_dst = wo_bf[:].rearrange("p r m t -> p m t r")
-                wo_src = wo_raw[:].rearrange("p t (m r) -> p m t r", r=PACK)
-                for q in range(PACK):
-                    ms = slice(q * P // PACK, (q + 1) * P // PACK)
-                    nc.scalar.copy(wo_dst[:, ms], wo_src[:, ms])
-            if last_plane:
-                gather_weighted(on_vector[:, :J], t, 3, 0, J)
-                gather_weighted(on_vector[:, J:], t, 2, CUT, J)
+                if (t, c) == (0, 2):
+                    copy_row(nc.scalar.copy, 2)
+                if (t, c) == (0, 1):
+                    copy_row(nc.scalar.copy, 3)
+                    gather_bare(1, 0, "bare0_2")
+                    gather_bare(1, 1, "prod0_2")
+                    gather_bare(2, 0, "bare0_0")
+                    gather_bare(2, 1, "bare0_1")
+                    gather_bare(3, 0, "prod0_0")
+                    gather_bare(3, 1, "prod0_1")
+            accs.append(acc)
+
+        on_vector = bare["tail"][:, : 2 * J - CUT]
+        gather_weighted(on_vector[:, :J], PACK - 1, 3, 0, J)
+        gather_weighted(on_vector[:, J:], PACK - 1, 2, CUT, J)
+
+        def turn_back(back, t):
             turned = keep.tile([G, P], F32, name=f"turned{t}", align_bytes=64)
-            nc.scalar.copy(turned[:], acc[:])
-            back = psum.tile([P, G], F32, name=f"back{t}", tag=f"back{t % 2}")
-            nc.tensor.transpose(back[:], turned[:], ident[:])
-            if last_plane:
-                rest = keep.tile([P, G], F32, align_bytes=64)
-                one = on_vector[:, :CUT].rearrange("p (g i) -> p g i", i=POINTS)
-                two = on_vector[:, CUT:].rearrange("p (c g i) -> p g c i", c=2, i=POINTS)
-                nc.vector.tensor_reduce(rest[:, : CUT // POINTS], one, mybir.AxisListType.X, ADD)
-                nc.vector.tensor_reduce(rest[:, CUT // POINTS :], two, mybir.AxisListType.XY, ADD)
-                for gs in (slice(0, CUT // POINTS), slice(CUT // POINTS, G)):
-                    nc.vector.tensor_tensor(b_bf[:, gs, t], back[:, gs], rest[:, gs], ADD)
-                quantise_wo(f"turned{t}", 2)
-            else:
-                nc.scalar.copy(b_bf[:, :, t], back[:])
+            nc.scalar.copy(turned[:], accs[t][:])
+            nc.tensor.transpose(back, turned[:], ident[:])
+
+        back = psum.tile([P, PACK, G], F32)
+        for t in range(PACK - 1):
+            turn_back(back[:, t, :], t)
+        nc.scalar.copy(b_bf[:, :, : PACK - 1], back[:, : PACK - 1, :].rearrange("p t g -> p g t"))
+        turn_back(back[:, PACK - 1, :], PACK - 1)
+        last_back = back[:, PACK - 1, :]
+        round_wo(0, slot["bare1_0"])
+        round_wo(1, slot["bare1_1"])
+
+        rest = keep.tile([P, G], F32, align_bytes=64)
+        one = on_vector[:, :CUT].rearrange("p (g i) -> p g i", i=POINTS)
+        two = on_vector[:, CUT:].rearrange("p (c g i) -> p g c i", c=2, i=POINTS)
+        nc.vector.tensor_reduce(rest[:, : CUT // POINTS], one, mybir.AxisListType.X, ADD)
+        nc.vector.tensor_reduce(rest[:, CUT // POINTS :], two, mybir.AxisListType.XY, ADD)
+        for gs in (slice(0, CUT // POINTS), slice(CUT // POINTS, G)):
+            nc.vector.tensor_tensor(b_bf[:, gs, PACK - 1], last_back[:, gs], rest[:, gs], ADD)
+        quantise_wo(f"turned{PACK - 1}", 2)
 
         b_codes = keep.tile([P, G], U32, align_bytes=64)
         b_scales = keep.tile([P, G], U8, align_bytes=64)
@@ -191,7 +227,7 @@ def tile_attend_deformable_kernel(tc, vals, ca, cb, cc, cd, aw, wo, offs, offs2,
 
         out_rows = out.rearrange("(m r) g -> m r g", r=PACK)
         for r in range(PACK):
-            y = psum.tile([P, G], F32, name=f"y{r}", tag=f"wide{r}")
+            y = psum.tile([P, G], F32, name=f"y{r}", tag=("wide0", "wide1", "acc0", "acc1")[r])
             nc.tensor.matmul_mx(
                 out=y[:],
                 lhsT=wo_codes[r].bitcast(FP8X4),

@@ -74,7 +74,7 @@ def tile_attend_deformable_kernel(tc, vals, ca, cb, cc, cd, aw, wo, offs, offs2,
         w_banks = {}
         w_rows = {}
         for c in (2, 0, 1, 3):
-            w_col = keep.tile([P, POINTS], F32, name=f"w_col{c}")
+            w_col = keep.tile([P, POINTS], F32, name=f"w_col{c}", align_bytes=64)
             nc.gpsimd.tensor_tensor(w_col[:], corner[c][:], att[:], MULT)
             w_bank = psum.tile([P, POINTS, G], F32, name=f"w_bank{c}", tag=f"wide{c}")
             for i in range(POINTS):
@@ -95,13 +95,7 @@ def tile_attend_deformable_kernel(tc, vals, ca, cb, cc, cd, aw, wo, offs, offs2,
 
         bare = {}
 
-        def gather_bare(t, c, after=None):
-            if (t, c) == (PACK - 1, 1):
-                tail = columns("tail", after, TAIL + J)
-                bare["tail"] = tail
-                dst = tail[:, TAIL:]
-            else:
-                dst = columns(f"bare{t}_{c}", after)[:]
+        def gather_bare(dst, t, c):
             bare[t, c] = dst
             window = planes[t][:].indirect(lists[c][:])
             if c == 2:
@@ -109,14 +103,14 @@ def tile_attend_deformable_kernel(tc, vals, ca, cb, cc, cd, aw, wo, offs, offs2,
             else:
                 nc.scalar.activation(dst, window, COPY)
 
-        def copy_row(copy, c):
+        def copy_row(c):
             w_row = keep.tile([P, G, POINTS], F32, name=f"w_row{c}", align_bytes=64)
-            copy(w_row[:], w_banks[c])
+            nc.scalar.copy(w_row[:], w_banks[c])
             w_rows[c] = w_row[:].rearrange("p g i -> p (g i)")
 
         def weigh(prod, t, c, g0, g1):
             nc.vector.tensor_tensor(
-                prod[:].rearrange("p (g i) -> p g i", i=POINTS)[:, g0:g1],
+                prod.rearrange("p (g i) -> p g i", i=POINTS)[:, g0:g1],
                 bare[t, c].rearrange("p (g i) -> p g i", i=POINTS)[:, g0:g1],
                 w_banks[c][:, g0:g1],
                 MULT,
@@ -126,21 +120,30 @@ def tile_attend_deformable_kernel(tc, vals, ca, cb, cc, cd, aw, wo, offs, offs2,
         zero = keep.tile([P, 1], F32)
         nc.vector.memset(zero[:], 0.0)
         nc.scalar.activation(short[:, CUT:], zero[:].to_broadcast([P, J - CUT]), COPY)
-        gather_bare(0, 0)
-        gather_bare(0, 2)
-        gather_bare(0, 1)
+        for c in (0, 2, 1):
+            gather_bare(columns(f"bare0_{c}")[:], 0, c)
 
         wo_scales = keep.tile([P, F], U8, align_bytes=64)
         wo_codes = []
 
         wo_bf = []
 
-        def round_wo(half, tag):
-            rounded = keep.tile([P, 2, P, PACK], BF16, align_bytes=64, name=f"wo_bf{half}", tag=tag)
-            src = wo_raw[:].rearrange("p t (m r) -> p m t r", r=PACK)[:, :, :, 2 * half : 2 * half + 2]
-            dst = rounded[:].rearrange("p r m t -> p m t r")
-            for ms in (slice(0, P // 2), slice(P // 2, P)):
-                nc.scalar.copy(dst[:, ms], src[:, ms])
+        def round_wo(half, rounded):
+            src = wo_raw[:].rearrange("p t (h n u s) -> p h n t u s", h=2, u=2, s=2)[:, half]
+            dst = rounded.rearrange("p (s n u t) -> p n t u s", s=2, u=2, t=PACK)
+            if half == 0:
+                for ns in (slice(0, P // 4), slice(P // 4, P // 2)):
+                    nc.scalar.copy(dst[:, ns], src[:, ns])
+            else:
+                for block in range(2):
+                    nc.gpsimd.tensor_scalar(
+                        rounded.rearrange("p (s m t) -> p s m t", s=2, t=PACK)[:, block],
+                        wo_raw[:].rearrange("p t (h m s) -> p h s m t", h=2, s=2)[:, half, block],
+                        1.0,
+                        0.0,
+                        MULT,
+                        ADD,
+                    )
             wo_bf.append(rounded)
 
         def quantise_wo(tag, blocks):
@@ -149,51 +152,54 @@ def tile_attend_deformable_kernel(tc, vals, ca, cb, cc, cd, aw, wo, offs, offs2,
             nc.vector.quantize_mx(
                 out=codes[:].bitcast(FP8X4),
                 scales=wo_scales[:, r * P : (r + blocks) * P],
-                in_=wo_bf[r // 2][:].rearrange("p r m t -> p (r m t)"),
+                in_=wo_bf[r // 2],
             )
             wo_codes.extend(codes[:, n * P : (n + 1) * P] for n in range(blocks))
 
         b_bf = keep.tile([P, G, PACK], BF16, align_bytes=64)
-        accs = []
-        for t in range(PACK):
-            last_plane = t == PACK - 1
-            acc = psum.tile([G, P], F32, name=f"acc{t}", tag=("acc0", "acc1", "wide3", "wide2")[t])
-            order = (2, 0, 1) if last_plane else (2, 0, 1, 3) if t == 0 else (2, 3, 0, 1)
-            for step, c in enumerate(order):
-                prod = short if (t, c) == (PACK - 1, 2) else columns(f"prod{t}_{c}")
-                if (t, c) == (PACK - 1, 1):
-                    weigh(prod, t, c, 0, G // 2)
-                    weigh(prod, t, c, G // 2, G)
-                elif (t, c) in bare:
-                    weigh(prod, t, c, 0, G)
-                elif last_plane:
-                    gather_weighted(prod[:, :CUT], t, c, 0, CUT)
-                else:
-                    gather_weighted(prod[:], t, c, 0, J)
-                for i in range(POINTS):
-                    nc.tensor.matmul(
-                        acc[:],
-                        lhsT=prod[:, i::POINTS],
-                        rhs=ident[:],
-                        is_transpose=True,
-                        start=(step == 0 and i == 0),
-                        stop=(step == len(order) - 1 and i == POINTS - 1),
-                    )
-                if (t, c) == (0, 2):
-                    copy_row(nc.scalar.copy, 2)
-                if (t, c) == (0, 1):
-                    copy_row(nc.scalar.copy, 3)
-                    gather_bare(1, 0, "bare0_2")
-                    gather_bare(1, 1, "prod0_2")
-                    gather_bare(2, 0, "bare0_0")
-                    gather_bare(2, 1, "bare0_1")
-                    gather_bare(3, 0, "prod0_0")
-                    gather_bare(3, 1, "prod0_1")
-            accs.append(acc)
+        last = PACK - 1
+        plain = [(t, c) for t in range(1, PACK) for c in range(2)]
+        fused = [(t, 2) for t in range(1, last)] + [(t, 3) for t in range(last)] + [(last, 2)]
+        steps = [(0, 2), (0, 0), (0, 1), fused[0]] + [step for pair in zip(fused[1:], plain) for step in pair] + plain[-1:]
+        banks = ("acc0", "acc1", "acc2", "wide2")
+        accs = [psum.tile([G, P], F32, name=f"acc{t}", tag=banks[t]) for t in range(PACK)]
+        for n, (t, c) in enumerate(steps):
+            if (t, c) == (last, 2):
+                prod = short[:]
+            elif (t, c) in fused[3:]:
+                prod = bare[steps[n - 3]]
+            else:
+                prod = columns(f"prod{t}_{c}")[:]
+            if (t, c) == (last, 1):
+                weigh(prod, t, c, 0, G // 2)
+                weigh(prod, t, c, G // 2, G)
+            elif (t, c) in bare:
+                weigh(prod, t, c, 0, G)
+            else:
+                width = CUT if t == last else J
+                gather_weighted(prod[:, :width], t, c, 0, width)
+            of_plane = [step for step in steps if step[0] == t]
+            for i in range(POINTS):
+                nc.tensor.matmul(
+                    accs[t][:],
+                    lhsT=prod[:, i::POINTS],
+                    rhs=ident[:],
+                    is_transpose=True,
+                    start=((t, c) == of_plane[0] and i == 0),
+                    stop=((t, c) == of_plane[-1] and i == POINTS - 1),
+                )
+            if (t, c) == (0, 2):
+                copy_row(2)
+            if (t, c) == (0, 1):
+                copy_row(3)
+                later = keep.tile([P, len(plain) * J + TAIL], F32, tag="w_col3", align_bytes=64)
+                for k, (plane, plain_corner) in enumerate(plain):
+                    j0 = k * J + (TAIL if k == len(plain) - 1 else 0)
+                    gather_bare(later[:, j0 : j0 + J], plane, plain_corner)
 
-        on_vector = bare["tail"][:, : 2 * J - CUT]
+        on_vector = later[:, (len(plain) - 1) * J :]
         gather_weighted(on_vector[:, :J], PACK - 1, 3, 0, J)
-        gather_weighted(on_vector[:, J:], PACK - 1, 2, CUT, J)
+        gather_weighted(on_vector[:, J : 2 * J - CUT], PACK - 1, 2, CUT, J)
 
         def turn_back(back, t):
             turned = keep.tile([G, P], F32, name=f"turned{t}", align_bytes=64)
@@ -206,12 +212,13 @@ def tile_attend_deformable_kernel(tc, vals, ca, cb, cc, cd, aw, wo, offs, offs2,
         nc.scalar.copy(b_bf[:, :, : PACK - 1], back[:, : PACK - 1, :].rearrange("p t g -> p g t"))
         turn_back(back[:, PACK - 1, :], PACK - 1)
         last_back = back[:, PACK - 1, :]
-        round_wo(0, slot["bare1_0"])
-        round_wo(1, slot["bare1_1"])
+        wo_first = keep.tile([P, 2 * F], BF16, align_bytes=64, tag=slot["prod1_1"])
+        round_wo(0, wo_first[:])
+        round_wo(1, bare[2, 0].bitcast(BF16))
 
         rest = keep.tile([P, G], F32, align_bytes=64)
         one = on_vector[:, :CUT].rearrange("p (g i) -> p g i", i=POINTS)
-        two = on_vector[:, CUT:].rearrange("p (c g i) -> p g c i", c=2, i=POINTS)
+        two = on_vector[:, CUT : 2 * J - CUT].rearrange("p (c g i) -> p g c i", c=2, i=POINTS)
         nc.vector.tensor_reduce(rest[:, : CUT // POINTS], one, mybir.AxisListType.X, ADD)
         nc.vector.tensor_reduce(rest[:, CUT // POINTS :], two, mybir.AxisListType.XY, ADD)
         for gs in (slice(0, CUT // POINTS), slice(CUT // POINTS, G)):
@@ -225,7 +232,7 @@ def tile_attend_deformable_kernel(tc, vals, ca, cb, cc, cd, aw, wo, offs, offs2,
         )
         quantise_wo("rest", 2)
 
-        out_rows = out.rearrange("(m r) g -> m r g", r=PACK)
+        out_rows = out.rearrange("(h m s) g -> h m s g", h=2, s=2)
         for r in range(PACK):
             y = psum.tile([P, G], F32, name=f"y{r}", tag=("wide0", "wide1", "acc0", "acc1")[r])
             nc.tensor.matmul_mx(
@@ -243,4 +250,4 @@ def tile_attend_deformable_kernel(tc, vals, ca, cb, cc, cd, aw, wo, offs, offs2,
             else:
                 nc.scalar.copy(y_sb[:, 1, :], y[:])
                 queue = nc.scalar if r == PACK - 1 else nc.sync
-                queue.dma_start(out_rows[:, r - 1 : r + 1, :], y_sb[:])
+                queue.dma_start(out_rows[r // 2], y_sb[:])

@@ -22,7 +22,6 @@ POINTS = J // G
 CORNERS = 4
 STRIPE = 16
 CUT = 384
-TAIL = 2 * J - CUT - J // 2
 
 
 def tile_attend_deformable_kernel(tc, vals, ca, cb, cc, cd, aw, wo, offs, offs2, offs3, offs4, out):
@@ -71,27 +70,22 @@ def tile_attend_deformable_kernel(tc, vals, ca, cb, cc, cd, aw, wo, offs, offs2,
         ident = keep.tile([P, P], F32)
         make_identity(nc, ident[:])
 
+        w_cols = {}
         w_banks = {}
         w_rows = {}
         for c in (2, 0, 1, 3):
-            w_col = keep.tile([P, POINTS], F32, name=f"w_col{c}", align_bytes=64)
-            nc.gpsimd.tensor_tensor(w_col[:], corner[c][:], att[:], MULT)
-            w_bank = psum.tile([P, POINTS, G], F32, name=f"w_bank{c}", tag=f"wide{c}")
+            w_cols[c] = keep.tile([P, POINTS], F32, name=f"w_col{c}", align_bytes=64)
+            nc.gpsimd.tensor_tensor(w_cols[c][:], corner[c][:], att[:], MULT)
+            w_bank = psum.tile([P, POINTS, G], F32, name=f"w_bank{c}", tag=f"bank{c}")
             for i in range(POINTS):
-                nc.tensor.transpose(w_bank[:, i, :], w_col[:, i : i + 1].to_broadcast([P, P]), ident[:])
+                nc.tensor.transpose(w_bank[:, i, :], w_cols[c][:, i : i + 1].to_broadcast([P, P]), ident[:])
             w_banks[c] = w_bank[:].rearrange("p i g -> p g i")
 
-        def offsets(c, j0, j1):
-            return lists[c][:, j0 // STRIPE : j1 // STRIPE]
+        def columns(name):
+            return keep.tile([P, J], F32, name=name, align_bytes=64)[:]
 
-        def gather_weighted(dst, t, c, j0, j1):
-            nc.vector.tensor_tensor(dst, planes[t][:].indirect(offsets(c, j0, j1)), w_rows[c][:, j0:j1], MULT)
-
-        slot = {}
-
-        def columns(name, after=None, width=J):
-            slot[name] = slot[after] if after else name
-            return keep.tile([P, width], F32, name=name, tag=slot[name], align_bytes=64)
+        def by_query(ap):
+            return ap.rearrange("p (g i) -> p g i", i=POINTS)
 
         bare = {}
 
@@ -103,138 +97,141 @@ def tile_attend_deformable_kernel(tc, vals, ca, cb, cc, cd, aw, wo, offs, offs2,
             else:
                 nc.scalar.activation(dst, window, COPY)
 
+        def gather_weighted(dst, t, c, j0, j1):
+            offsets = lists[c][:, j0 // STRIPE : j1 // STRIPE]
+            nc.vector.tensor_tensor(dst, planes[t][:].indirect(offsets), w_rows[c][:, j0:j1], MULT)
+
         def copy_row(c):
             w_row = keep.tile([P, G, POINTS], F32, name=f"w_row{c}", align_bytes=64)
             nc.scalar.copy(w_row[:], w_banks[c])
             w_rows[c] = w_row[:].rearrange("p g i -> p (g i)")
 
-        def weigh(prod, t, c, g0, g1):
-            nc.vector.tensor_tensor(
-                prod.rearrange("p (g i) -> p g i", i=POINTS)[:, g0:g1],
-                bare[t, c].rearrange("p (g i) -> p g i", i=POINTS)[:, g0:g1],
-                w_banks[c][:, g0:g1],
-                MULT,
-            )
-
+        last_turn = keep.tile([P, J + J // 2], F32, align_bytes=64)
         short = columns("short")
-        zero = keep.tile([P, 1], F32)
-        nc.vector.memset(zero[:], 0.0)
-        nc.scalar.activation(short[:, CUT:], zero[:].to_broadcast([P, J - CUT]), COPY)
+        rest = keep.tile([P, 2, G], F32, align_bytes=64)
+        nc.vector.memset(rest[:, 0, :], 0.0)
+        nc.scalar.activation(short[:, CUT:], rest[:, 0, : J - CUT], COPY)
         for c in (0, 2, 1):
-            gather_bare(columns(f"bare0_{c}")[:], 0, c)
+            gather_bare(columns(f"bare0_{c}"), 0, c)
 
-        wo_scales = keep.tile([P, F], U8, align_bytes=64)
-        wo_codes = []
-
-        wo_bf = []
-
-        def round_wo(half, rounded):
-            src = wo_raw[:].rearrange("p t (h n u s) -> p h n t u s", h=2, u=2, s=2)[:, half]
-            dst = rounded.rearrange("p (s n u t) -> p n t u s", s=2, u=2, t=PACK)
-            if half == 0:
-                for ns in (slice(0, P // 4), slice(P // 4, P // 2)):
-                    nc.scalar.copy(dst[:, ns], src[:, ns])
-            else:
-                for block in range(2):
-                    nc.gpsimd.tensor_scalar(
-                        rounded.rearrange("p (s m t) -> p s m t", s=2, t=PACK)[:, block],
-                        wo_raw[:].rearrange("p t (h m s) -> p h s m t", h=2, s=2)[:, half, block],
-                        1.0,
-                        0.0,
-                        MULT,
-                        ADD,
-                    )
-            wo_bf.append(rounded)
-
-        def quantise_wo(tag, blocks):
-            r = len(wo_codes)
-            codes = keep.tile([P, blocks * P], U32, align_bytes=64, name=f"wo_codes{r}", tag=tag)
-            nc.vector.quantize_mx(
-                out=codes[:].bitcast(FP8X4),
-                scales=wo_scales[:, r * P : (r + blocks) * P],
-                in_=wo_bf[r // 2],
-            )
-            wo_codes.extend(codes[:, n * P : (n + 1) * P] for n in range(blocks))
-
-        b_bf = keep.tile([P, G, PACK], BF16, align_bytes=64)
         last = PACK - 1
-        plain = [(t, c) for t in range(1, PACK) for c in range(2)]
-        fused = [(t, 2) for t in range(1, last)] + [(t, 3) for t in range(last)] + [(last, 2)]
-        steps = [(0, 2), (0, 0), (0, 1), fused[0]] + [step for pair in zip(fused[1:], plain) for step in pair] + plain[-1:]
-        banks = ("acc0", "acc1", "acc2", "wide2")
-        accs = [psum.tile([G, P], F32, name=f"acc{t}", tag=banks[t]) for t in range(PACK)]
-        for n, (t, c) in enumerate(steps):
+        steps = [(0, 2), (0, 0), (0, 1), (1, 2), (2, 2), (0, 3), (1, 3), (1, 0), (1, 1), (last, 2), (2, 3), (2, 0), (last, 0)]
+        accs = [psum.tile([G, 2, P], F32, name=f"acc{h}", tag=f"bank{4 + h}") for h in range(2)]
+        prods = {}
+        turned_bare = [psum.tile([G, 2, 2, P], F32, name=f"turned_bare{n}", tag=f"bank{3 - n}") for n in range(2)]
+        for t, c in steps:
             if (t, c) == (last, 2):
-                prod = short[:]
-            elif (t, c) in fused[3:]:
-                prod = bare[steps[n - 3]]
-            else:
-                prod = columns(f"prod{t}_{c}")[:]
-            if (t, c) == (last, 1):
-                weigh(prod, t, c, 0, G // 2)
-                weigh(prod, t, c, G // 2, G)
+                prod = short
+                gather_weighted(prod[:, :CUT], t, c, 0, CUT)
             elif (t, c) in bare:
-                weigh(prod, t, c, 0, G)
+                prod = last_turn[:, :J] if (t, c) == steps[-1] else columns(f"prod{t}_{c}")
+                nc.vector.tensor_tensor(by_query(prod), by_query(bare[t, c]), w_banks[c], MULT)
             else:
-                width = CUT if t == last else J
-                gather_weighted(prod[:, :width], t, c, 0, width)
-            of_plane = [step for step in steps if step[0] == t]
+                prod = bare[1, 1] if (t, c) == (2, 3) else columns(f"prod{t}_{c}")
+                gather_weighted(prod, t, c, 0, J)
+            prods[t, c] = prod
+            of_pair = [step for step in steps if step[0] // 2 == t // 2]
             for i in range(POINTS):
                 nc.tensor.matmul(
-                    accs[t][:],
+                    accs[t // 2][:, t % 2, :],
                     lhsT=prod[:, i::POINTS],
                     rhs=ident[:],
                     is_transpose=True,
-                    start=((t, c) == of_plane[0] and i == 0),
-                    stop=((t, c) == of_plane[-1] and i == POINTS - 1),
+                    start=((t, c) == of_pair[0] and i == 0),
+                    stop=((t, c) == of_pair[-1] and i == POINTS - 1),
                 )
             if (t, c) == (0, 2):
                 copy_row(2)
             if (t, c) == (0, 1):
                 copy_row(3)
-                later = keep.tile([P, len(plain) * J + TAIL], F32, tag="w_col3", align_bytes=64)
-                for k, (plane, plain_corner) in enumerate(plain):
-                    j0 = k * J + (TAIL if k == len(plain) - 1 else 0)
-                    gather_bare(later[:, j0 : j0 + J], plane, plain_corner)
+                later = keep.tile([P, 6 * J + J - CUT], F32, tag="w_col3", align_bytes=64)
+                for k, step in enumerate([(1, 0), (1, 1), (2, 1), (last, 1), (2, 0), (last, 0)]):
+                    gather_bare(later[:, k * J : (k + 1) * J], *step)
+            if c == 3 and t < 2:
+                for i in range(POINTS):
+                    nc.tensor.transpose(turned_bare[i // 2][:, i % 2, t, :], bare[2 + t, 1][:, i::POINTS], ident[:])
 
-        on_vector = later[:, (len(plain) - 1) * J :]
-        gather_weighted(on_vector[:, :J], PACK - 1, 3, 0, J)
-        gather_weighted(on_vector[:, J : 2 * J - CUT], PACK - 1, 2, CUT, J)
+        on_vector = later[:, 5 * J :]
+        gather_weighted(on_vector[:, :J], last, 3, 0, J)
+        gather_weighted(on_vector[:, J:], last, 2, CUT, J)
 
-        def turn_back(back, t):
-            turned = keep.tile([G, P], F32, name=f"turned{t}", align_bytes=64)
-            nc.scalar.copy(turned[:], accs[t][:])
-            nc.tensor.transpose(back, turned[:], ident[:])
+        weighted = keep.tile([G, POINTS, 2, P], F32)
+        for i in range(POINTS):
+            nc.scalar.activation(weighted[:, i], turned_bare[i // 2][:, i % 2], COPY, scale=w_cols[1][:, i : i + 1])
 
-        back = psum.tile([P, PACK, G], F32)
-        for t in range(PACK - 1):
-            turn_back(back[:, t, :], t)
-        nc.scalar.copy(b_bf[:, :, : PACK - 1], back[:, : PACK - 1, :].rearrange("p t g -> p g t"))
-        turn_back(back[:, PACK - 1, :], PACK - 1)
-        last_back = back[:, PACK - 1, :]
-        wo_first = keep.tile([P, 2 * F], BF16, align_bytes=64, tag=slot["prod1_1"])
-        round_wo(0, wo_first[:])
-        round_wo(1, bare[2, 0].bitcast(BF16))
+        turned = [keep.tile([G, 2, P], F32, name=f"turned{h}", align_bytes=64) for h in range(2)]
+        b_bf = last_turn[:, : J // 2].bitcast(BF16).rearrange("p (g t) -> p g t", t=PACK)
+        early_back = psum.tile([P, 2, G], F32, tag="bank7")
+        late_back = psum.tile([P, 2, G], F32, tag="bank6")
+        nc.scalar.copy(turned[0][:], accs[0][:])
+        for slot in range(2):
+            nc.tensor.transpose(early_back[:, slot, :], turned[0][:, slot, :], ident[:])
+        nc.scalar.copy(turned[1][:], accs[1][:])
+        sums = [(slot, weighted[:, i, slot, :]) for i in range(POINTS) for slot in range(2)]
+        sums = sums + [(slot, turned[1][:, slot, :]) for slot in range(2)]
+        for n, (slot, addend) in enumerate(sums):
+            nc.tensor.matmul(
+                late_back[:, slot, :],
+                lhsT=addend,
+                rhs=ident[:],
+                is_transpose=True,
+                start=(n == 0),
+                stop=(n == len(sums) - 1),
+            )
 
-        rest = keep.tile([P, G], F32, align_bytes=64)
-        one = on_vector[:, :CUT].rearrange("p (g i) -> p g i", i=POINTS)
-        two = on_vector[:, CUT : 2 * J - CUT].rearrange("p (c g i) -> p g c i", c=2, i=POINTS)
-        nc.vector.tensor_reduce(rest[:, : CUT // POINTS], one, mybir.AxisListType.X, ADD)
-        nc.vector.tensor_reduce(rest[:, CUT // POINTS :], two, mybir.AxisListType.XY, ADD)
+        nc.scalar.copy(b_bf[:, :, :2], early_back[:].rearrange("p t g -> p g t"))
+
+        wo_first = [prods[0, 3][:, : F // 2].bitcast(BF16), short[:, : F // 2].bitcast(BF16)]
+        for block in range(2):
+            nc.gpsimd.tensor_scalar(
+                wo_first[block].rearrange("p (m t) -> p m t", t=PACK),
+                wo_raw[:].rearrange("p t (h m s) -> p h s m t", h=2, s=2)[:, 0, block],
+                1.0,
+                0.0,
+                MULT,
+                ADD,
+            )
+        wo_second = last_turn[:, J // 2 :].bitcast(BF16)
+        src = wo_raw[:].rearrange("p t (h n u s) -> p h n t u s", h=2, u=2, s=2)[:, 1]
+        dst = wo_second.rearrange("p (s n u t) -> p n t u s", s=2, u=2, t=PACK)
+        for ns in (slice(0, P // 4), slice(P // 4, P // 2)):
+            nc.scalar.copy(dst[:, ns], src[:, ns])
+
+        wo_scales = keep.tile([P, F], U8, align_bytes=64)
+        wo_codes = []
+
+        def quantise_wo(rounded, tag, blocks):
+            r = len(wo_codes)
+            codes = keep.tile([P, blocks * P], U32, align_bytes=64, name=f"wo_codes{r}", tag=tag)
+            nc.vector.quantize_mx(
+                out=codes[:].bitcast(FP8X4), scales=wo_scales[:, r * P : (r + blocks) * P], in_=rounded
+            )
+            wo_codes.extend(codes[:, n * P : (n + 1) * P] for n in range(blocks))
+
+        one = by_query(on_vector[:, :CUT])
+        two = on_vector[:, CUT:].rearrange("p (c g i) -> p g c i", c=2, i=POINTS)
+        nc.vector.tensor_reduce(rest[:, 1, : CUT // POINTS], one, mybir.AxisListType.X, ADD)
+        nc.vector.tensor_reduce(rest[:, 1, CUT // POINTS :], two, mybir.AxisListType.XY, ADD)
         for gs in (slice(0, CUT // POINTS), slice(CUT // POINTS, G)):
-            nc.vector.tensor_tensor(b_bf[:, gs, PACK - 1], last_back[:, gs], rest[:, gs], ADD)
-        quantise_wo(f"turned{PACK - 1}", 2)
+            nc.vector.tensor_tensor(
+                b_bf[:, gs, 2:],
+                late_back[:].rearrange("p t g -> p g t")[:, gs],
+                rest[:].rearrange("p t g -> p g t")[:, gs],
+                ADD,
+            )
+        quantise_wo(wo_first[0], "turned0", 1)
+        quantise_wo(wo_first[1], "turned1", 1)
 
         b_codes = keep.tile([P, G], U32, align_bytes=64)
         b_scales = keep.tile([P, G], U8, align_bytes=64)
         nc.vector.quantize_mx(
-            out=b_codes[:].bitcast(FP8X4), scales=b_scales[:], in_=b_bf[:].rearrange("p g t -> p (g t)")
+            out=b_codes[:].bitcast(FP8X4), scales=b_scales[:], in_=b_bf.rearrange("p g t -> p (g t)")
         )
-        quantise_wo("rest", 2)
+        quantise_wo(wo_second, "rest", 2)
 
         out_rows = out.rearrange("(h m s) g -> h m s g", h=2, s=2)
         for r in range(PACK):
-            y = psum.tile([P, G], F32, name=f"y{r}", tag=("wide0", "wide1", "acc0", "acc1")[r])
+            y = psum.tile([P, G], F32, name=f"y{r}", tag=("bank1", "bank2", "bank3", "bank5")[r])
             nc.tensor.matmul_mx(
                 out=y[:],
                 lhsT=wo_codes[r].bitcast(FP8X4),

@@ -22,6 +22,7 @@ POINTS = J // G
 CORNERS = 4
 STRIPE = 16
 CUT = 384
+GAP = 2 * J - CUT - J // 2
 
 
 def tile_attend_deformable_kernel(tc, vals, ca, cb, cc, cd, aw, wo, offs, offs2, offs3, offs4, out):
@@ -115,7 +116,7 @@ def tile_attend_deformable_kernel(tc, vals, ca, cb, cc, cd, aw, wo, offs, offs2,
             gather_bare(columns(f"bare0_{c}"), 0, c)
 
         last = PACK - 1
-        steps = [(0, 2), (0, 0), (0, 1), (1, 2), (2, 2), (0, 3), (1, 3), (1, 0), (1, 1), (last, 2), (2, 3), (2, 0), (last, 0)]
+        steps = [(0, 2), (0, 0), (0, 1), (1, 2), (2, 2), (0, 3), (1, 3), (1, 0), (1, 1), (2, 0), (last, 2), (2, 3), (last, 0)]
         accs = [psum.tile([G, 2, P], F32, name=f"acc{h}", tag=f"bank{4 + h}") for h in range(2)]
         prods = {}
         turned_bare = [psum.tile([G, 2, 2, P], F32, name=f"turned_bare{n}", tag=f"bank{3 - n}") for n in range(2)]
@@ -125,9 +126,12 @@ def tile_attend_deformable_kernel(tc, vals, ca, cb, cc, cd, aw, wo, offs, offs2,
                 gather_weighted(prod[:, :CUT], t, c, 0, CUT)
             elif (t, c) in bare:
                 prod = last_turn[:, :J] if (t, c) == steps[-1] else columns(f"prod{t}_{c}")
-                nc.vector.tensor_tensor(by_query(prod), by_query(bare[t, c]), w_banks[c], MULT)
+                parts = 2 if (t, c) == steps[-1] else 1
+                for part in range(parts):
+                    gs = slice(part * G // parts, (part + 1) * G // parts)
+                    nc.vector.tensor_tensor(by_query(prod)[:, gs], by_query(bare[t, c])[:, gs], w_banks[c][:, gs], MULT)
             else:
-                prod = bare[1, 1] if (t, c) == (2, 3) else columns(f"prod{t}_{c}")
+                prod = columns(f"prod{t}_{c}")
                 gather_weighted(prod, t, c, 0, J)
             prods[t, c] = prod
             of_pair = [step for step in steps if step[0] // 2 == t // 2]
@@ -144,14 +148,18 @@ def tile_attend_deformable_kernel(tc, vals, ca, cb, cc, cd, aw, wo, offs, offs2,
                 copy_row(2)
             if (t, c) == (0, 1):
                 copy_row(3)
-                later = keep.tile([P, 6 * J + J - CUT], F32, tag="w_col3", align_bytes=64)
-                for k, step in enumerate([(1, 0), (1, 1), (2, 1), (last, 1), (2, 0), (last, 0)]):
-                    gather_bare(later[:, k * J : (k + 1) * J], *step)
-            if c == 3 and t < 2:
+                later = keep.tile([P, 6 * J + GAP], F32, tag="w_col3", align_bytes=64)
+                for k, step in enumerate([(1, 0), (1, 1), (2, 0), (2, 1), (last, 1), (last, 0)]):
+                    j0 = k * J + (GAP if step == steps[-1] else 0)
+                    gather_bare(later[:, j0 : j0 + J], *step)
+            if (t, c) in ((1, 1), (last, 2)):
+                slot = t // 2
                 for i in range(POINTS):
-                    nc.tensor.transpose(turned_bare[i // 2][:, i % 2, t, :], bare[2 + t, 1][:, i::POINTS], ident[:])
+                    nc.tensor.transpose(
+                        turned_bare[i // 2][:, i % 2, slot, :], bare[2 + slot, 1][:, i::POINTS], ident[:]
+                    )
 
-        on_vector = later[:, 5 * J :]
+        on_vector = later[:, 5 * J : 7 * J - CUT]
         gather_weighted(on_vector[:, :J], last, 3, 0, J)
         gather_weighted(on_vector[:, J:], last, 2, CUT, J)
 
@@ -181,16 +189,15 @@ def tile_attend_deformable_kernel(tc, vals, ca, cb, cc, cd, aw, wo, offs, offs2,
 
         nc.scalar.copy(b_bf[:, :, :2], early_back[:].rearrange("p t g -> p g t"))
 
-        wo_first = [prods[0, 3][:, : F // 2].bitcast(BF16), short[:, : F // 2].bitcast(BF16)]
-        for block in range(2):
-            nc.gpsimd.tensor_scalar(
-                wo_first[block].rearrange("p (m t) -> p m t", t=PACK),
-                wo_raw[:].rearrange("p t (h m s) -> p h s m t", h=2, s=2)[:, 0, block],
-                1.0,
-                0.0,
-                MULT,
-                ADD,
-            )
+        wo_first = prods[0, 3].bitcast(BF16)
+        nc.gpsimd.tensor_scalar(
+            wo_first.rearrange("p (s m t) -> p s m t", s=2, t=PACK),
+            wo_raw[:].rearrange("p t (h m s) -> p h s m t", h=2, s=2)[:, 0],
+            1.0,
+            0.0,
+            MULT,
+            ADD,
+        )
         wo_second = last_turn[:, J // 2 :].bitcast(BF16)
         src = wo_raw[:].rearrange("p t (h n u s) -> p h n t u s", h=2, u=2, s=2)[:, 1]
         dst = wo_second.rearrange("p (s n u t) -> p n t u s", s=2, u=2, t=PACK)
@@ -219,8 +226,7 @@ def tile_attend_deformable_kernel(tc, vals, ca, cb, cc, cd, aw, wo, offs, offs2,
                 rest[:].rearrange("p t g -> p g t")[:, gs],
                 ADD,
             )
-        quantise_wo(wo_first[0], "turned0", 1)
-        quantise_wo(wo_first[1], "turned1", 1)
+        quantise_wo(wo_first, "turned1", 2)
 
         b_codes = keep.tile([P, G], U32, align_bytes=64)
         b_scales = keep.tile([P, G], U8, align_bytes=64)

@@ -35,7 +35,7 @@ def tile_attend_deformable_kernel(tc, vals, ca, cb, cc, cd, aw, wo, offs, offs2,
         planes = [keep.tile([P, T], F32, name=f"plane{t}", align_bytes=64) for t in range(PACK)]
         corner = [keep.tile([P, POINTS], F32, name=f"corner{c}") for c in range(CORNERS)]
         att = keep.tile([P, POINTS], F32)
-        wo_raw = keep.tile([P, PACK, F], F32)
+        wo_raw = [keep.tile([P, PACK, F // 2], F32, name=f"wo_raw{h}") for h in range(2)]
 
         vals_planes = vals.rearrange("(p t) n -> t p n", t=PACK)
         list_src = (offs, offs2, offs3, offs4)
@@ -53,6 +53,9 @@ def tile_attend_deformable_kernel(tc, vals, ca, cb, cc, cd, aw, wo, offs, offs2,
         def load_plane(t):
             nc.sync.dma_start(planes[t][:], vals_planes[t])
 
+        def load_wo(h):
+            nc.sync.dma_start(wo_raw[h][:], wo.rearrange("(p t) (h f) -> h p t f", t=PACK, h=2)[h])
+
         load_list(0)
         nc.scalar.dma_start(planes[0][:], vals_planes[0])
         load_list(2)
@@ -65,8 +68,9 @@ def tile_attend_deformable_kernel(tc, vals, ca, cb, cc, cd, aw, wo, offs, offs2,
         load_plane(1)
         load_list(3)
         load_plane(2)
+        load_wo(0)
         load_plane(3)
-        nc.sync.dma_start(wo_raw[:], wo.rearrange("(p t) f -> p t f", t=PACK))
+        load_wo(1)
 
         ident = keep.tile([P, P], F32)
         make_identity(nc, ident[:])
@@ -103,9 +107,8 @@ def tile_attend_deformable_kernel(tc, vals, ca, cb, cc, cd, aw, wo, offs, offs2,
             nc.vector.tensor_tensor(dst, planes[t][:].indirect(offsets), w_rows[c][:, j0:j1], MULT)
 
         def copy_row(c):
-            w_row = keep.tile([P, G, POINTS], F32, name=f"w_row{c}", align_bytes=64)
-            nc.scalar.copy(w_row[:], w_banks[c])
-            w_rows[c] = w_row[:].rearrange("p g i -> p (g i)")
+            w_rows[c] = columns(f"w_row{c}")
+            nc.scalar.copy(by_query(w_rows[c]), w_banks[c])
 
         last_turn = keep.tile([P, J + J // 2], F32, align_bytes=64)
         short = columns("short")
@@ -116,7 +119,7 @@ def tile_attend_deformable_kernel(tc, vals, ca, cb, cc, cd, aw, wo, offs, offs2,
             gather_bare(columns(f"bare0_{c}"), 0, c)
 
         last = PACK - 1
-        steps = [(0, 2), (0, 0), (0, 1), (1, 2), (2, 2), (0, 3), (1, 3), (1, 0), (1, 1), (2, 0), (last, 2), (2, 3), (last, 0)]
+        steps = [(0, 2), (0, 0), (0, 1), (1, 2), (2, 2), (0, 3), (1, 0), (1, 1), (2, 0), (last, 2), (1, 3), (2, 3), (last, 0)]
         accs = [psum.tile([G, 2, P], F32, name=f"acc{h}", tag=f"bank{4 + h}") for h in range(2)]
         prods = {}
         turned_bare = [psum.tile([G, 2, 2, P], F32, name=f"turned_bare{n}", tag=f"bank{3 - n}") for n in range(2)]
@@ -152,8 +155,8 @@ def tile_attend_deformable_kernel(tc, vals, ca, cb, cc, cd, aw, wo, offs, offs2,
                 for k, step in enumerate([(1, 0), (1, 1), (2, 0), (2, 1), (last, 1), (last, 0)]):
                     j0 = k * J + (GAP if step == steps[-1] else 0)
                     gather_bare(later[:, j0 : j0 + J], *step)
-            if (t, c) in ((1, 1), (last, 2)):
-                slot = t // 2
+            if (t, c) in ((2, 0), (last, 2)):
+                slot = t - 2
                 for i in range(POINTS):
                     nc.tensor.transpose(
                         turned_bare[i // 2][:, i % 2, slot, :], bare[2 + slot, 1][:, i::POINTS], ident[:]
@@ -189,17 +192,17 @@ def tile_attend_deformable_kernel(tc, vals, ca, cb, cc, cd, aw, wo, offs, offs2,
 
         nc.scalar.copy(b_bf[:, :, :2], early_back[:].rearrange("p t g -> p g t"))
 
-        wo_first = prods[0, 3].bitcast(BF16)
+        wo_first = prods[1, 2].bitcast(BF16)
         nc.gpsimd.tensor_scalar(
             wo_first.rearrange("p (s m t) -> p s m t", s=2, t=PACK),
-            wo_raw[:].rearrange("p t (h m s) -> p h s m t", h=2, s=2)[:, 0],
+            wo_raw[0][:].rearrange("p t (m s) -> p s m t", s=2),
             1.0,
             0.0,
             MULT,
             ADD,
         )
         wo_second = last_turn[:, J // 2 :].bitcast(BF16)
-        src = wo_raw[:].rearrange("p t (h n u s) -> p h n t u s", h=2, u=2, s=2)[:, 1]
+        src = wo_raw[1][:].rearrange("p t (n u s) -> p n t u s", u=2, s=2)
         dst = wo_second.rearrange("p (s n u t) -> p n t u s", s=2, u=2, t=PACK)
         for ns in (slice(0, P // 4), slice(P // 4, P // 2)):
             nc.scalar.copy(dst[:, ns], src[:, ns])

@@ -35,7 +35,7 @@ def tile_attend_deformable_kernel(tc, vals, ca, cb, cc, cd, aw, wo, offs, offs2,
         planes = [keep.tile([P, T], F32, name=f"plane{t}", align_bytes=64) for t in range(PACK)]
         corner = [keep.tile([P, POINTS], F32, name=f"corner{c}") for c in range(CORNERS)]
         att = keep.tile([P, POINTS], F32)
-        wo_raw = [keep.tile([P, PACK, F // 2], F32, name=f"wo_raw{h}") for h in range(2)]
+        wo_raw = keep.tile([P, PACK, F], F32)
 
         vals_planes = vals.rearrange("(p t) n -> t p n", t=PACK)
         list_src = (offs, offs2, offs3, offs4)
@@ -53,9 +53,6 @@ def tile_attend_deformable_kernel(tc, vals, ca, cb, cc, cd, aw, wo, offs, offs2,
         def load_plane(t):
             nc.sync.dma_start(planes[t][:], vals_planes[t])
 
-        def load_wo(h):
-            nc.sync.dma_start(wo_raw[h][:], wo.rearrange("(p t) (h f) -> h p t f", t=PACK, h=2)[h])
-
         load_list(0)
         nc.scalar.dma_start(planes[0][:], vals_planes[0])
         load_list(2)
@@ -68,9 +65,8 @@ def tile_attend_deformable_kernel(tc, vals, ca, cb, cc, cd, aw, wo, offs, offs2,
         load_plane(1)
         load_list(3)
         load_plane(2)
-        load_wo(0)
+        nc.sync.dma_start(wo_raw[:], wo.rearrange("(p t) f -> p t f", t=PACK))
         load_plane(3)
-        load_wo(1)
 
         ident = keep.tile([P, P], F32)
         make_identity(nc, ident[:])
@@ -192,17 +188,17 @@ def tile_attend_deformable_kernel(tc, vals, ca, cb, cc, cd, aw, wo, offs, offs2,
 
         nc.scalar.copy(b_bf[:, :, :2], early_back[:].rearrange("p t g -> p g t"))
 
-        wo_first = prods[1, 2].bitcast(BF16)
+        wo_first = prods[2, 2].bitcast(BF16)
         nc.gpsimd.tensor_scalar(
             wo_first.rearrange("p (s m t) -> p s m t", s=2, t=PACK),
-            wo_raw[0][:].rearrange("p t (m s) -> p s m t", s=2),
+            wo_raw[:].rearrange("p t (h m s) -> p h s m t", h=2, s=2)[:, 0],
             1.0,
             0.0,
             MULT,
             ADD,
         )
         wo_second = last_turn[:, J // 2 :].bitcast(BF16)
-        src = wo_raw[1][:].rearrange("p t (n u s) -> p n t u s", u=2, s=2)
+        src = wo_raw[:].rearrange("p t (h n u s) -> p h n t u s", h=2, u=2, s=2)[:, 1]
         dst = wo_second.rearrange("p (s n u t) -> p n t u s", s=2, u=2, t=PACK)
         for ns in (slice(0, P // 4), slice(P // 4, P // 2)):
             nc.scalar.copy(dst[:, ns], src[:, ns])

@@ -107,6 +107,11 @@ def tile_attend_deformable_kernel(tc, vals, ca, cb, cc, cd, aw, wo, offs, offs2,
             nc.scalar.copy(by_query(w_rows[c]), w_banks[c])
 
         last_turn = keep.tile([P, J + J // 2], F32, align_bytes=64)
+        def round_wo(copy, rounded, half, ns):
+            src = wo_raw[:].rearrange("p t (h n u s) -> p h n t u s", h=2, u=2, s=2)[:, half]
+            dst = rounded.rearrange("p (s n u t) -> p n t u s", s=2, u=2, t=PACK)
+            copy(dst[:, ns], src[:, ns])
+
         short = columns("short")
         rest = keep.tile([P, 2, G], F32, align_bytes=64)
         nc.vector.memset(rest[:, 0, :], 0.0)
@@ -166,6 +171,10 @@ def tile_attend_deformable_kernel(tc, vals, ca, cb, cc, cd, aw, wo, offs, offs2,
         for i in range(POINTS):
             nc.scalar.activation(weighted[:, i], turned_bare[i // 2][:, i % 2], COPY, scale=w_cols[1][:, i : i + 1])
 
+        wo_first = bare[1, 0].bitcast(BF16)
+        for ns in (slice(0, P // 4), slice(P // 4, P // 2)):
+            round_wo(nc.scalar.copy, wo_first, 0, ns)
+
         turned = [keep.tile([G, 2, P], F32, name=f"turned{h}", align_bytes=64) for h in range(2)]
         b_bf = last_turn[:, : J // 2].bitcast(BF16).rearrange("p (g t) -> p g t", t=PACK)
         early_back = psum.tile([P, 2, G], F32, tag="bank7")
@@ -188,20 +197,8 @@ def tile_attend_deformable_kernel(tc, vals, ca, cb, cc, cd, aw, wo, offs, offs2,
 
         nc.scalar.copy(b_bf[:, :, :2], early_back[:].rearrange("p t g -> p g t"))
 
-        wo_first = prods[2, 2].bitcast(BF16)
-        nc.gpsimd.tensor_scalar(
-            wo_first.rearrange("p (s m t) -> p s m t", s=2, t=PACK),
-            wo_raw[:].rearrange("p t (h m s) -> p h s m t", h=2, s=2)[:, 0],
-            1.0,
-            0.0,
-            MULT,
-            ADD,
-        )
         wo_second = last_turn[:, J // 2 :].bitcast(BF16)
-        src = wo_raw[:].rearrange("p t (h n u s) -> p h n t u s", h=2, u=2, s=2)[:, 1]
-        dst = wo_second.rearrange("p (s n u t) -> p n t u s", s=2, u=2, t=PACK)
-        for ns in (slice(0, P // 4), slice(P // 4, P // 2)):
-            nc.scalar.copy(dst[:, ns], src[:, ns])
+        round_wo(nc.scalar.copy, wo_second, 1, slice(0, P // 2))
 
         wo_scales = keep.tile([P, F], U8, align_bytes=64)
         wo_codes = []

@@ -65,8 +65,8 @@ def tile_attend_deformable_kernel(tc, vals, ca, cb, cc, cd, aw, wo, offs, offs2,
         load_plane(1)
         load_list(3)
         load_plane(2)
-        nc.sync.dma_start(wo_raw[:], wo.rearrange("(p t) f -> p t f", t=PACK))
         load_plane(3)
+        nc.sync.dma_start(wo_raw[:], wo.rearrange("(p t) f -> p t f", t=PACK))
 
         ident = keep.tile([P, P], F32)
         make_identity(nc, ident[:])
@@ -120,7 +120,7 @@ def tile_attend_deformable_kernel(tc, vals, ca, cb, cc, cd, aw, wo, offs, offs2,
             gather_bare(columns(f"bare0_{c}"), 0, c)
 
         last = PACK - 1
-        steps = [(0, 2), (0, 0), (0, 1), (1, 2), (2, 2), (0, 3), (1, 0), (1, 1), (2, 0), (last, 2), (1, 3), (2, 3), (last, 0)]
+        steps = [(0, 2), (0, 0), (0, 1), (1, 2), (2, 2), (1, 0), (last, 2), (0, 3), (1, 1), (2, 0), (1, 3), (2, 3), (last, 0)]
         accs = [psum.tile([G, 2, P], F32, name=f"acc{h}", tag=f"bank{4 + h}") for h in range(2)]
         prods = {}
         turned_bare = [psum.tile([G, 2, 2, P], F32, name=f"turned_bare{n}", tag=f"bank{3 - n}") for n in range(2)]
@@ -151,19 +151,21 @@ def tile_attend_deformable_kernel(tc, vals, ca, cb, cc, cd, aw, wo, offs, offs2,
             if (t, c) == (0, 2):
                 copy_row(2)
             if (t, c) == (0, 1):
+                gather_bare(bare[0, 2], 1, 0)
+                gather_bare(bare[0, 0], 1, 1)
                 copy_row(3)
-                later = keep.tile([P, 6 * J + GAP], F32, tag="w_col3", align_bytes=64)
-                for k, step in enumerate([(1, 0), (1, 1), (2, 0), (2, 1), (last, 1), (last, 0)]):
+                later = keep.tile([P, 4 * J + GAP], F32, tag="w_col3", align_bytes=64)
+                for k, step in enumerate([(2, 0), (2, 1), (last, 1), (last, 0)]):
                     j0 = k * J + (GAP if step == steps[-1] else 0)
                     gather_bare(later[:, j0 : j0 + J], *step)
-            if (t, c) in ((2, 0), (last, 2)):
-                slot = t - 2
+            if (t, c) in ((2, 0), (1, 3)):
+                slot = 2 - t
                 for i in range(POINTS):
                     nc.tensor.transpose(
                         turned_bare[i // 2][:, i % 2, slot, :], bare[2 + slot, 1][:, i::POINTS], ident[:]
                     )
 
-        on_vector = later[:, 5 * J : 7 * J - CUT]
+        on_vector = later[:, 3 * J : 5 * J - CUT]
         gather_weighted(on_vector[:, :J], last, 3, 0, J)
         gather_weighted(on_vector[:, J:], last, 2, CUT, J)
 
@@ -171,7 +173,7 @@ def tile_attend_deformable_kernel(tc, vals, ca, cb, cc, cd, aw, wo, offs, offs2,
         for i in range(POINTS):
             nc.scalar.activation(weighted[:, i], turned_bare[i // 2][:, i % 2], COPY, scale=w_cols[1][:, i : i + 1])
 
-        wo_first = bare[1, 0].bitcast(BF16)
+        wo_first = bare[2, 0].bitcast(BF16)
         for ns in (slice(0, P // 4), slice(P // 4, P // 2)):
             round_wo(nc.scalar.copy, wo_first, 0, ns)
 

@@ -120,10 +120,17 @@ def tile_attend_deformable_kernel(tc, vals, ca, cb, cc, cd, aw, wo, offs, offs2,
             gather_bare(columns(f"bare0_{c}"), 0, c)
 
         last = PACK - 1
-        steps = [(0, 2), (0, 0), (0, 1), (1, 2), (2, 2), (1, 0), (last, 2), (0, 3), (1, 1), (2, 0), (1, 3), (2, 3), (last, 0)]
+        steps = [(0, 2), (0, 0), (0, 1), (1, 2), (2, 2), (1, 0), (last, 2), (0, 3), (1, 1), (1, 3), (2, 0), (2, 3), (last, 0)]
         accs = [psum.tile([G, 2, P], F32, name=f"acc{h}", tag=f"bank{4 + h}") for h in range(2)]
         prods = {}
         turned_bare = [psum.tile([G, 2, 2, P], F32, name=f"turned_bare{n}", tag=f"bank{3 - n}") for n in range(2)]
+        weighted = keep.tile([G, POINTS, 2, P], F32)
+        turned = [keep.tile([G, 2, P], F32, name=f"turned{h}", align_bytes=64) for h in range(2)]
+        late_back = psum.tile([P, 2, G], F32, tag="bank6")
+
+        def turn_back(slot, addend, start, stop):
+            nc.tensor.matmul(late_back[:, slot, :], lhsT=addend, rhs=ident[:], is_transpose=True, start=start, stop=stop)
+
         for t, c in steps:
             if (t, c) == (last, 2):
                 prod = short
@@ -155,50 +162,42 @@ def tile_attend_deformable_kernel(tc, vals, ca, cb, cc, cd, aw, wo, offs, offs2,
                 gather_bare(bare[0, 0], 1, 1)
                 copy_row(3)
                 later = keep.tile([P, 4 * J + GAP], F32, tag="w_col3", align_bytes=64)
-                for k, step in enumerate([(2, 0), (2, 1), (last, 1), (last, 0)]):
+                for k, step in enumerate([(2, 1), (last, 1), (2, 0), (last, 0)]):
                     j0 = k * J + (GAP if step == steps[-1] else 0)
                     gather_bare(later[:, j0 : j0 + J], *step)
-            if (t, c) in ((2, 0), (1, 3)):
-                slot = 2 - t
+            if (t, c) in ((last, 2), (0, 3)):
+                slot = c - 2
                 for i in range(POINTS):
                     nc.tensor.transpose(
                         turned_bare[i // 2][:, i % 2, slot, :], bare[2 + slot, 1][:, i::POINTS], ident[:]
                     )
+            if (t, c) == (2, 0):
+                for i in range(POINTS):
+                    nc.scalar.activation(
+                        weighted[:, i], turned_bare[i // 2][:, i % 2], COPY, scale=w_cols[1][:, i : i + 1]
+                    )
+                nc.scalar.copy(turned[0][:], accs[0][:])
+                wo_first = prods[1, 3].bitcast(BF16)
+                for ns in (slice(0, P // 4), slice(P // 4, P // 2)):
+                    round_wo(nc.scalar.copy, wo_first, 0, ns)
+                for slot in range(2):
+                    turn_back(slot, weighted[:, 0, slot, :], slot == 0, False)
 
         on_vector = later[:, 3 * J : 5 * J - CUT]
         gather_weighted(on_vector[:, :J], last, 3, 0, J)
         gather_weighted(on_vector[:, J:], last, 2, CUT, J)
 
-        weighted = keep.tile([G, POINTS, 2, P], F32)
-        for i in range(POINTS):
-            nc.scalar.activation(weighted[:, i], turned_bare[i // 2][:, i % 2], COPY, scale=w_cols[1][:, i : i + 1])
-
-        wo_first = bare[2, 0].bitcast(BF16)
-        for ns in (slice(0, P // 4), slice(P // 4, P // 2)):
-            round_wo(nc.scalar.copy, wo_first, 0, ns)
-
-        turned = [keep.tile([G, 2, P], F32, name=f"turned{h}", align_bytes=64) for h in range(2)]
-        b_bf = last_turn[:, : J // 2].bitcast(BF16).rearrange("p (g t) -> p g t", t=PACK)
         early_back = psum.tile([P, 2, G], F32, tag="bank7")
-        late_back = psum.tile([P, 2, G], F32, tag="bank6")
-        nc.scalar.copy(turned[0][:], accs[0][:])
         for slot in range(2):
             nc.tensor.transpose(early_back[:, slot, :], turned[0][:, slot, :], ident[:])
+        for i in range(1, POINTS):
+            for slot in range(2):
+                turn_back(slot, weighted[:, i, slot, :], False, False)
         nc.scalar.copy(turned[1][:], accs[1][:])
-        sums = [(slot, weighted[:, i, slot, :]) for i in range(POINTS) for slot in range(2)]
-        sums = sums + [(slot, turned[1][:, slot, :]) for slot in range(2)]
-        for n, (slot, addend) in enumerate(sums):
-            nc.tensor.matmul(
-                late_back[:, slot, :],
-                lhsT=addend,
-                rhs=ident[:],
-                is_transpose=True,
-                start=(n == 0),
-                stop=(n == len(sums) - 1),
-            )
-
+        for slot in range(2):
+            turn_back(slot, turned[1][:, slot, :], False, slot == 1)
+        b_bf = last_turn[:, : J // 2].bitcast(BF16).rearrange("p (g t) -> p g t", t=PACK)
         nc.scalar.copy(b_bf[:, :, :2], early_back[:].rearrange("p t g -> p g t"))
-
         wo_second = last_turn[:, J // 2 :].bitcast(BF16)
         round_wo(nc.scalar.copy, wo_second, 1, slice(0, P // 2))
 

@@ -21,8 +21,7 @@ PACK = 4
 POINTS = J // G
 CORNERS = 4
 STRIPE = 16
-CUT = 384
-GAP = 2 * J - CUT - J // 2
+TURNED_POINTS = 2
 
 
 def tile_attend_deformable_kernel(tc, vals, ca, cb, cc, cd, aw, wo, offs, offs2, offs3, offs4, out):
@@ -68,8 +67,11 @@ def tile_attend_deformable_kernel(tc, vals, ca, cb, cc, cd, aw, wo, offs, offs2,
         load_plane(3)
         nc.sync.dma_start(wo_raw[:], wo.rearrange("(p t) f -> p t f", t=PACK))
 
+        zero = keep.tile([P, 1], F32)
+        nc.vector.memset(zero[:], 0.0)
         ident = keep.tile([P, P], F32)
-        make_identity(nc, ident[:])
+        nc.scalar.activation(ident[:], zero[:].to_broadcast([P, P]), COPY)
+        make_identity(nc, ident[:], nomemset=True)
 
         w_cols = {}
         w_banks = {}
@@ -106,86 +108,82 @@ def tile_attend_deformable_kernel(tc, vals, ca, cb, cc, cd, aw, wo, offs, offs2,
             w_rows[c] = columns(f"w_row{c}")
             nc.scalar.copy(by_query(w_rows[c]), w_banks[c])
 
-        last_turn = keep.tile([P, J + J // 2], F32, align_bytes=64)
         def round_wo(copy, rounded, half, ns):
             src = wo_raw[:].rearrange("p t (h n u s) -> p h n t u s", h=2, u=2, s=2)[:, half]
             dst = rounded.rearrange("p (s n u t) -> p n t u s", s=2, u=2, t=PACK)
             copy(dst[:, ns], src[:, ns])
 
-        short = columns("short")
-        rest = keep.tile([P, 2, G], F32, align_bytes=64)
-        nc.vector.memset(rest[:, 0, :], 0.0)
-        nc.scalar.activation(short[:, CUT:], rest[:, 0, : J - CUT], COPY)
         for c in (0, 2, 1):
             gather_bare(columns(f"bare0_{c}"), 0, c)
 
         last = PACK - 1
-        steps = [(0, 2), (0, 0), (0, 1), (1, 2), (2, 2), (1, 0), (last, 2), (0, 3), (1, 1), (1, 3), (2, 0), (2, 3), (last, 0)]
+        steps = [(0, 2), (0, 0), (0, 1), (1, 2), (2, 2), (1, 0), (last, 2), (0, 3), (1, 3), (1, 1), (2, 0), (last, 0), (2, 3)]
         accs = [psum.tile([G, 2, P], F32, name=f"acc{h}", tag=f"bank{4 + h}") for h in range(2)]
         prods = {}
-        turned_bare = [psum.tile([G, 2, 2, P], F32, name=f"turned_bare{n}", tag=f"bank{3 - n}") for n in range(2)]
+        turned_bare = [psum.tile([G, 2, 2, P], F32, name=f"turned_bare{n}", tag=("bank2", "bank7")[n]) for n in range(2)]
         weighted = keep.tile([G, POINTS, 2, P], F32)
-        turned = [keep.tile([G, 2, P], F32, name=f"turned{h}", align_bytes=64) for h in range(2)]
+        turned_first = keep.tile([G, J], F32, align_bytes=64)
+        turned = [turned_first[:, : 2 * P].rearrange("g (t p) -> g t p", t=2), keep.tile([G, 2, P], F32, name="turned1", align_bytes=64)[:]]
         late_back = psum.tile([P, 2, G], F32, tag="bank6")
 
         def turn_back(slot, addend, start, stop):
             nc.tensor.matmul(late_back[:, slot, :], lhsT=addend, rhs=ident[:], is_transpose=True, start=start, stop=stop)
 
         for t, c in steps:
-            if (t, c) == (last, 2):
-                prod = short
-                gather_weighted(prod[:, :CUT], t, c, 0, CUT)
-            elif (t, c) in bare:
-                prod = last_turn[:, :J] if (t, c) == steps[-1] else columns(f"prod{t}_{c}")
-                parts = 2 if (t, c) == steps[-1] else 1
+            points = POINTS
+            if (t, c) in bare:
+                prod = columns(f"prod{t}_{c}")
+                parts = 2 if t == last else 1
                 for part in range(parts):
                     gs = slice(part * G // parts, (part + 1) * G // parts)
                     nc.vector.tensor_tensor(by_query(prod)[:, gs], by_query(bare[t, c])[:, gs], w_banks[c][:, gs], MULT)
+            elif (t, c) == steps[-1]:
+                prod = later[:, 3 * J : 4 * J]
+                gather_weighted(prod, t, c, 0, J)
+                points = TURNED_POINTS
             else:
                 prod = columns(f"prod{t}_{c}")
                 gather_weighted(prod, t, c, 0, J)
             prods[t, c] = prod
             of_pair = [step for step in steps if step[0] // 2 == t // 2]
-            for i in range(POINTS):
+            for i in range(points):
                 nc.tensor.matmul(
                     accs[t // 2][:, t % 2, :],
                     lhsT=prod[:, i::POINTS],
                     rhs=ident[:],
                     is_transpose=True,
                     start=((t, c) == of_pair[0] and i == 0),
-                    stop=((t, c) == of_pair[-1] and i == POINTS - 1),
+                    stop=((t, c) == of_pair[-1] and i == points - 1),
                 )
             if (t, c) == (0, 2):
                 copy_row(2)
             if (t, c) == (0, 1):
                 gather_bare(bare[0, 2], 1, 0)
-                gather_bare(bare[0, 0], 1, 1)
+                gather_bare(bare[0, 0], 2, 1)
                 copy_row(3)
-                later = keep.tile([P, 4 * J + GAP], F32, tag="w_col3", align_bytes=64)
-                for k, step in enumerate([(2, 1), (last, 1), (2, 0), (last, 0)]):
-                    j0 = k * J + (GAP if step == steps[-1] else 0)
+                later = keep.tile([P, 5 * J], F32, tag="w_col3", align_bytes=64)
+                for j0, step in zip((0, J, 2 * J, 3 * J + J // 2), [(last, 1), (1, 1), (2, 0), (last, 0)]):
                     gather_bare(later[:, j0 : j0 + J], *step)
-            if (t, c) in ((last, 2), (0, 3)):
-                slot = c - 2
+            if (t, c) in ((1, 2), (last, 2)):
+                slot = t // 2
                 for i in range(POINTS):
                     nc.tensor.transpose(
                         turned_bare[i // 2][:, i % 2, slot, :], bare[2 + slot, 1][:, i::POINTS], ident[:]
                     )
-            if (t, c) == (2, 0):
+            if (t, c) == (last, 0):
                 for i in range(POINTS):
                     nc.scalar.activation(
                         weighted[:, i], turned_bare[i // 2][:, i % 2], COPY, scale=w_cols[1][:, i : i + 1]
                     )
-                nc.scalar.copy(turned[0][:], accs[0][:])
-                wo_first = prods[1, 3].bitcast(BF16)
+                nc.scalar.copy(turned[0], accs[0][:])
+                wo_first = prods[1, 1].bitcast(BF16)
                 for ns in (slice(0, P // 4), slice(P // 4, P // 2)):
                     round_wo(nc.scalar.copy, wo_first, 0, ns)
                 for slot in range(2):
                     turn_back(slot, weighted[:, 0, slot, :], slot == 0, False)
 
-        on_vector = later[:, 3 * J : 5 * J - CUT]
-        gather_weighted(on_vector[:, :J], last, 3, 0, J)
-        gather_weighted(on_vector[:, J:], last, 2, CUT, J)
+        on_vector = later[:, 4 * J :]
+        gather_weighted(on_vector, last, 3, 0, J)
 
         early_back = psum.tile([P, 2, G], F32, tag="bank7")
         for slot in range(2):
@@ -193,12 +191,14 @@ def tile_attend_deformable_kernel(tc, vals, ca, cb, cc, cd, aw, wo, offs, offs2,
         for i in range(1, POINTS):
             for slot in range(2):
                 turn_back(slot, weighted[:, i, slot, :], False, False)
-        nc.scalar.copy(turned[1][:], accs[1][:])
+        nc.scalar.copy(turned[1], accs[1][:])
         for slot in range(2):
             turn_back(slot, turned[1][:, slot, :], False, slot == 1)
-        b_bf = last_turn[:, : J // 2].bitcast(BF16).rearrange("p (g t) -> p g t", t=PACK)
+
+        b_tile = keep.tile([P, G, PACK], BF16, align_bytes=64)
+        b_bf = b_tile[:]
         nc.scalar.copy(b_bf[:, :, :2], early_back[:].rearrange("p t g -> p g t"))
-        wo_second = last_turn[:, J // 2 :].bitcast(BF16)
+        wo_second = turned_first[:].bitcast(BF16)
         round_wo(nc.scalar.copy, wo_second, 1, slice(0, P // 2))
 
         wo_scales = keep.tile([P, F], U8, align_bytes=64)
@@ -212,11 +212,12 @@ def tile_attend_deformable_kernel(tc, vals, ca, cb, cc, cd, aw, wo, offs, offs2,
             )
             wo_codes.extend(codes[:, n * P : (n + 1) * P] for n in range(blocks))
 
-        one = by_query(on_vector[:, :CUT])
-        two = on_vector[:, CUT:].rearrange("p (c g i) -> p g c i", c=2, i=POINTS)
-        nc.vector.tensor_reduce(rest[:, 1, : CUT // POINTS], one, mybir.AxisListType.X, ADD)
-        nc.vector.tensor_reduce(rest[:, 1, CUT // POINTS :], two, mybir.AxisListType.XY, ADD)
-        for gs in (slice(0, CUT // POINTS), slice(CUT // POINTS, G)):
+        rest = keep.tile([P, 2, G], F32, align_bytes=64)
+        halves = (slice(0, G // 2), slice(G // 2, G))
+        nc.vector.tensor_reduce(rest[:, 0, :], by_query(prods[2, 3])[:, :, TURNED_POINTS:], mybir.AxisListType.X, ADD)
+        for gs in halves:
+            nc.vector.tensor_reduce(rest[:, 1, gs], by_query(on_vector)[:, gs], mybir.AxisListType.X, ADD)
+        for gs in halves:
             nc.vector.tensor_tensor(
                 b_bf[:, gs, 2:],
                 late_back[:].rearrange("p t g -> p g t")[:, gs],

@@ -22,6 +22,7 @@ POINTS = J // G
 CORNERS = 4
 STRIPE = 16
 TURNED_POINTS = 2
+EARLY_ADDENDS = 3
 
 
 def tile_attend_deformable_kernel(tc, vals, ca, cb, cc, cd, aw, wo, offs, offs2, offs3, offs4, out):
@@ -108,41 +109,42 @@ def tile_attend_deformable_kernel(tc, vals, ca, cb, cc, cd, aw, wo, offs, offs2,
             w_rows[c] = columns(f"w_row{c}")
             nc.scalar.copy(by_query(w_rows[c]), w_banks[c])
 
-        def round_wo(copy, rounded, half, ns):
-            src = wo_raw[:].rearrange("p t (h n u s) -> p h n t u s", h=2, u=2, s=2)[:, half]
-            dst = rounded.rearrange("p (s n u t) -> p n t u s", s=2, u=2, t=PACK)
-            copy(dst[:, ns], src[:, ns])
+        def round_wo(r, ns):
+            src = wo_raw[:].rearrange("p t (h n u s) -> p h s n t u", h=2, u=2, s=2)[:, r // 2, r % 2]
+            nc.scalar.copy(wo_bf[r].rearrange("p (n u t) -> p n t u", u=2, t=PACK)[:, ns], src[:, ns])
 
         for c in (0, 2, 1):
             gather_bare(columns(f"bare0_{c}"), 0, c)
 
         last = PACK - 1
-        steps = [(0, 2), (0, 0), (0, 1), (1, 2), (2, 2), (1, 0), (last, 2), (0, 3), (1, 3), (1, 1), (2, 0), (last, 0), (2, 3)]
+        steps = [(0, 2), (0, 0), (0, 1), (1, 2), (2, 2), (1, 0), (last, 2), (0, 3), (1, 3), (1, 1), (2, 0), (last, 3), (last, 0)]
         accs = [psum.tile([G, 2, P], F32, name=f"acc{h}", tag=f"bank{4 + h}") for h in range(2)]
         prods = {}
         turned_bare = [psum.tile([G, 2, 2, P], F32, name=f"turned_bare{n}", tag=("bank2", "bank7")[n]) for n in range(2)]
-        weighted = keep.tile([G, POINTS, 2, P], F32)
-        turned_first = keep.tile([G, J], F32, align_bytes=64)
-        turned = [turned_first[:, : 2 * P].rearrange("g (t p) -> g t p", t=2), keep.tile([G, 2, P], F32, name="turned1", align_bytes=64)[:]]
+        shared = keep.tile([G, 3 * J], F32, align_bytes=64)
+        weighted = shared[:, : 2 * J].rearrange("g (i s p) -> g i s p", i=POINTS, s=2)
+        turned = [keep.tile([G, 2, P], F32, name=f"turned{h}", align_bytes=64)[:] for h in range(2)]
+        addends = [(i, slot) for i in range(POINTS) for slot in range(2)]
+        block = J // 2
+        wo_bf = [shared[:, n * block : (n + 1) * block].bitcast(BF16) for n in (0, 1, 3, 4)]
         late_back = psum.tile([P, 2, G], F32, tag="bank6")
 
         def turn_back(slot, addend, start, stop):
             nc.tensor.matmul(late_back[:, slot, :], lhsT=addend, rhs=ident[:], is_transpose=True, start=start, stop=stop)
 
         for t, c in steps:
-            points = POINTS
+            points = TURNED_POINTS if (t, c) == steps[-1] else POINTS
             if (t, c) in bare:
                 prod = columns(f"prod{t}_{c}")
-                parts = 2 if t == last else 1
+                parts = 2 if t >= 2 else 1
                 for part in range(parts):
                     gs = slice(part * G // parts, (part + 1) * G // parts)
                     nc.vector.tensor_tensor(by_query(prod)[:, gs], by_query(bare[t, c])[:, gs], w_banks[c][:, gs], MULT)
-            elif (t, c) == steps[-1]:
-                prod = later[:, 3 * J : 4 * J]
+            elif (t, c) == (last, 3):
+                prod = later[:, 2 * J : 3 * J]
                 gather_weighted(prod, t, c, 0, J)
-                points = TURNED_POINTS
             else:
-                prod = columns(f"prod{t}_{c}")
+                prod = shared[:, 2 * J :] if (t, c) == (0, 3) else columns(f"prod{t}_{c}")
                 gather_weighted(prod, t, c, 0, J)
             prods[t, c] = prod
             of_pair = [step for step in steps if step[0] // 2 == t // 2]
@@ -162,7 +164,7 @@ def tile_attend_deformable_kernel(tc, vals, ca, cb, cc, cd, aw, wo, offs, offs2,
                 gather_bare(bare[0, 0], 2, 1)
                 copy_row(3)
                 later = keep.tile([P, 5 * J], F32, tag="w_col3", align_bytes=64)
-                for j0, step in zip((0, J, 2 * J, 3 * J + J // 2), [(last, 1), (1, 1), (2, 0), (last, 0)]):
+                for j0, step in zip((0, J, 2 * J + J // 2, 4 * J), [(last, 1), (1, 1), (2, 0), (last, 0)]):
                     gather_bare(later[:, j0 : j0 + J], *step)
             if (t, c) in ((1, 2), (last, 2)):
                 slot = t // 2
@@ -170,53 +172,52 @@ def tile_attend_deformable_kernel(tc, vals, ca, cb, cc, cd, aw, wo, offs, offs2,
                     nc.tensor.transpose(
                         turned_bare[i // 2][:, i % 2, slot, :], bare[2 + slot, 1][:, i::POINTS], ident[:]
                     )
-            if (t, c) == (last, 0):
+            if (t, c) == (0, 3):
+                nc.gpsimd.tensor_copy(
+                    wo_bf[3].rearrange("p (m t) -> p m t", t=PACK),
+                    wo_raw[:, :, F // 2 :].rearrange("p t (m s) -> p s m t", s=2)[:, 1],
+                )
+            if (t, c) == (2, 0):
                 for i in range(POINTS):
                     nc.scalar.activation(
                         weighted[:, i], turned_bare[i // 2][:, i % 2], COPY, scale=w_cols[1][:, i : i + 1]
                     )
                 nc.scalar.copy(turned[0], accs[0][:])
-                wo_first = prods[1, 1].bitcast(BF16)
-                for ns in (slice(0, P // 4), slice(P // 4, P // 2)):
-                    round_wo(nc.scalar.copy, wo_first, 0, ns)
-                for slot in range(2):
-                    turn_back(slot, weighted[:, 0, slot, :], slot == 0, False)
+                for i, slot in addends[:EARLY_ADDENDS]:
+                    turn_back(slot, weighted[:, i, slot, :], (i, slot) == addends[0], False)
+                round_wo(0, slice(0, P // 2))
+                round_wo(1, slice(0, P // 4))
 
-        on_vector = later[:, 4 * J :]
-        gather_weighted(on_vector, last, 3, 0, J)
+        on_vector = later[:, 3 * J + J // 2 : 4 * J + J // 2]
+        gather_weighted(on_vector, 2, 3, 0, J)
 
+        nc.scalar.copy(turned[1], accs[1][:])
+        for i, slot in addends[EARLY_ADDENDS:]:
+            turn_back(slot, weighted[:, i, slot, :], False, False)
+        for slot in range(2):
+            turn_back(slot, turned[1][:, slot, :], False, slot == 1)
         early_back = psum.tile([P, 2, G], F32, tag="bank7")
         for slot in range(2):
             nc.tensor.transpose(early_back[:, slot, :], turned[0][:, slot, :], ident[:])
-        for i in range(1, POINTS):
-            for slot in range(2):
-                turn_back(slot, weighted[:, i, slot, :], False, False)
-        nc.scalar.copy(turned[1], accs[1][:])
-        for slot in range(2):
-            turn_back(slot, turned[1][:, slot, :], False, slot == 1)
 
-        b_tile = keep.tile([P, G, PACK], BF16, align_bytes=64)
-        b_bf = b_tile[:]
+        round_wo(1, slice(P // 4, P // 2))
+        round_wo(2, slice(0, P // 2))
+        b_bf = keep.tile([P, G, PACK], BF16, align_bytes=64)
         nc.scalar.copy(b_bf[:, :, :2], early_back[:].rearrange("p t g -> p g t"))
-        wo_second = turned_first[:].bitcast(BF16)
-        round_wo(nc.scalar.copy, wo_second, 1, slice(0, P // 2))
 
         wo_scales = keep.tile([P, F], U8, align_bytes=64)
         wo_codes = []
 
-        def quantise_wo(rounded, tag, blocks):
+        def quantise_wo(codes, rounded, blocks):
             r = len(wo_codes)
-            codes = keep.tile([P, blocks * P], U32, align_bytes=64, name=f"wo_codes{r}", tag=tag)
-            nc.vector.quantize_mx(
-                out=codes[:].bitcast(FP8X4), scales=wo_scales[:, r * P : (r + blocks) * P], in_=rounded
-            )
+            nc.vector.quantize_mx(out=codes.bitcast(FP8X4), scales=wo_scales[:, r * P : (r + blocks) * P], in_=rounded)
             wo_codes.extend(codes[:, n * P : (n + 1) * P] for n in range(blocks))
 
         rest = keep.tile([P, 2, G], F32, align_bytes=64)
         halves = (slice(0, G // 2), slice(G // 2, G))
-        nc.vector.tensor_reduce(rest[:, 0, :], by_query(prods[2, 3])[:, :, TURNED_POINTS:], mybir.AxisListType.X, ADD)
+        nc.vector.tensor_reduce(rest[:, 1, :], by_query(prods[last, 0])[:, :, TURNED_POINTS:], mybir.AxisListType.X, ADD)
         for gs in halves:
-            nc.vector.tensor_reduce(rest[:, 1, gs], by_query(on_vector)[:, gs], mybir.AxisListType.X, ADD)
+            nc.vector.tensor_reduce(rest[:, 0, gs], by_query(on_vector)[:, gs], mybir.AxisListType.X, ADD)
         for gs in halves:
             nc.vector.tensor_tensor(
                 b_bf[:, gs, 2:],
@@ -224,14 +225,16 @@ def tile_attend_deformable_kernel(tc, vals, ca, cb, cc, cd, aw, wo, offs, offs2,
                 rest[:].rearrange("p t g -> p g t")[:, gs],
                 ADD,
             )
-        quantise_wo(wo_first, "turned1", 2)
+        first_codes = keep.tile([P, 2 * P], U32, align_bytes=64, tag="turned1")
+        quantise_wo(first_codes[:], shared[:, : 2 * block].bitcast(BF16), 2)
 
         b_codes = keep.tile([P, G], U32, align_bytes=64)
         b_scales = keep.tile([P, G], U8, align_bytes=64)
         nc.vector.quantize_mx(
-            out=b_codes[:].bitcast(FP8X4), scales=b_scales[:], in_=b_bf.rearrange("p g t -> p (g t)")
+            out=b_codes[:].bitcast(FP8X4), scales=b_scales[:], in_=b_bf[:].rearrange("p g t -> p (g t)")
         )
-        quantise_wo(wo_second, "rest", 2)
+        last_codes = keep.tile([P, 2 * P], U32, align_bytes=64, tag="b_bf")
+        quantise_wo(last_codes[:], shared[:, 3 * block : 5 * block].bitcast(BF16), 2)
 
         out_rows = out.rearrange("(h m s) g -> h m s g", h=2, s=2)
         for r in range(PACK):

@@ -22,7 +22,7 @@ POINTS = J // G
 CORNERS = 4
 STRIPE = 16
 TURNED_POINTS = 2
-EARLY_ADDENDS = 3
+EARLY_ADDENDS = 2
 
 
 def tile_attend_deformable_kernel(tc, vals, ca, cb, cc, cd, aw, wo, offs, offs2, offs3, offs4, out):
@@ -121,12 +121,17 @@ def tile_attend_deformable_kernel(tc, vals, ca, cb, cc, cd, aw, wo, offs, offs2,
         accs = [psum.tile([G, 2, P], F32, name=f"acc{h}", tag=f"bank{4 + h}") for h in range(2)]
         prods = {}
         turned_bare = [psum.tile([G, 2, 2, P], F32, name=f"turned_bare{n}", tag=("bank2", "bank7")[n]) for n in range(2)]
-        shared = keep.tile([G, 3 * J], F32, align_bytes=64)
-        weighted = shared[:, : 2 * J].rearrange("g (i s p) -> g i s p", i=POINTS, s=2)
-        turned = [keep.tile([G, 2, P], F32, name=f"turned{h}", align_bytes=64)[:] for h in range(2)]
+        block = 2 * P
+        shared = keep.tile([G, J + 5 * block], F32, align_bytes=64)
+
+        def pair_at(n):
+            return shared[:, J + n * block : J + (n + 1) * block].rearrange("g (s p) -> g s p", s=2)
+
+        weighted = [pair_at(n) for n in (4, 0, 1, 3)]
+        turned = [pair_at(2), keep.tile([G, 2, P], F32, name="turned1", align_bytes=64)[:]]
+        wo_all = shared[:, P : P + PACK * block].bitcast(BF16)
+        wo_bf = [wo_all[:, r * PACK * P : (r + 1) * PACK * P] for r in range(PACK)]
         addends = [(i, slot) for i in range(POINTS) for slot in range(2)]
-        block = J // 2
-        wo_bf = [shared[:, n * block : (n + 1) * block].bitcast(BF16) for n in (0, 1, 3, 4)]
         late_back = psum.tile([P, 2, G], F32, tag="bank6")
 
         def turn_back(slot, addend, start, stop):
@@ -135,7 +140,7 @@ def tile_attend_deformable_kernel(tc, vals, ca, cb, cc, cd, aw, wo, offs, offs2,
         for t, c in steps:
             points = TURNED_POINTS if (t, c) == steps[-1] else POINTS
             if (t, c) in bare:
-                prod = columns(f"prod{t}_{c}")
+                prod = shared[:, :J] if (t, c) == (1, 1) else columns(f"prod{t}_{c}")
                 parts = 2 if t >= 2 else 1
                 for part in range(parts):
                     gs = slice(part * G // parts, (part + 1) * G // parts)
@@ -144,7 +149,7 @@ def tile_attend_deformable_kernel(tc, vals, ca, cb, cc, cd, aw, wo, offs, offs2,
                 prod = later[:, 2 * J : 3 * J]
                 gather_weighted(prod, t, c, 0, J)
             else:
-                prod = shared[:, 2 * J :] if (t, c) == (0, 3) else columns(f"prod{t}_{c}")
+                prod = columns(f"prod{t}_{c}")
                 gather_weighted(prod, t, c, 0, J)
             prods[t, c] = prod
             of_pair = [step for step in steps if step[0] // 2 == t // 2]
@@ -172,19 +177,14 @@ def tile_attend_deformable_kernel(tc, vals, ca, cb, cc, cd, aw, wo, offs, offs2,
                     nc.tensor.transpose(
                         turned_bare[i // 2][:, i % 2, slot, :], bare[2 + slot, 1][:, i::POINTS], ident[:]
                     )
-            if (t, c) == (0, 3):
-                nc.gpsimd.tensor_copy(
-                    wo_bf[3].rearrange("p (m t) -> p m t", t=PACK),
-                    wo_raw[:, :, F // 2 :].rearrange("p t (m s) -> p s m t", s=2)[:, 1],
-                )
             if (t, c) == (2, 0):
                 for i in range(POINTS):
                     nc.scalar.activation(
-                        weighted[:, i], turned_bare[i // 2][:, i % 2], COPY, scale=w_cols[1][:, i : i + 1]
+                        weighted[i], turned_bare[i // 2][:, i % 2], COPY, scale=w_cols[1][:, i : i + 1]
                     )
                 nc.scalar.copy(turned[0], accs[0][:])
                 for i, slot in addends[:EARLY_ADDENDS]:
-                    turn_back(slot, weighted[:, i, slot, :], (i, slot) == addends[0], False)
+                    turn_back(slot, weighted[i][:, slot, :], (i, slot) == addends[0], False)
                 round_wo(0, slice(0, P // 2))
                 round_wo(1, slice(0, P // 4))
 
@@ -193,17 +193,19 @@ def tile_attend_deformable_kernel(tc, vals, ca, cb, cc, cd, aw, wo, offs, offs2,
 
         nc.scalar.copy(turned[1], accs[1][:])
         for i, slot in addends[EARLY_ADDENDS:]:
-            turn_back(slot, weighted[:, i, slot, :], False, False)
+            turn_back(slot, weighted[i][:, slot, :], False, False)
         for slot in range(2):
             turn_back(slot, turned[1][:, slot, :], False, slot == 1)
         early_back = psum.tile([P, 2, G], F32, tag="bank7")
-        for slot in range(2):
+        for slot in (1, 0):
             nc.tensor.transpose(early_back[:, slot, :], turned[0][:, slot, :], ident[:])
 
         round_wo(1, slice(P // 4, P // 2))
         round_wo(2, slice(0, P // 2))
+        round_wo(3, slice(0, P // 4))
         b_bf = keep.tile([P, G, PACK], BF16, align_bytes=64)
         nc.scalar.copy(b_bf[:, :, :2], early_back[:].rearrange("p t g -> p g t"))
+        round_wo(3, slice(P // 4, P // 2))
 
         wo_scales = keep.tile([P, F], U8, align_bytes=64)
         wo_codes = []
@@ -226,15 +228,15 @@ def tile_attend_deformable_kernel(tc, vals, ca, cb, cc, cd, aw, wo, offs, offs2,
                 ADD,
             )
         first_codes = keep.tile([P, 2 * P], U32, align_bytes=64, tag="turned1")
-        quantise_wo(first_codes[:], shared[:, : 2 * block].bitcast(BF16), 2)
+        quantise_wo(first_codes[:], wo_all[:, : 2 * PACK * P], 2)
 
         b_codes = keep.tile([P, G], U32, align_bytes=64)
         b_scales = keep.tile([P, G], U8, align_bytes=64)
         nc.vector.quantize_mx(
             out=b_codes[:].bitcast(FP8X4), scales=b_scales[:], in_=b_bf[:].rearrange("p g t -> p (g t)")
         )
-        last_codes = keep.tile([P, 2 * P], U32, align_bytes=64, tag="b_bf")
-        quantise_wo(last_codes[:], shared[:, 3 * block : 5 * block].bitcast(BF16), 2)
+        last_codes = keep.tile([P, 2 * P], U32, align_bytes=64)
+        quantise_wo(last_codes[:], wo_all[:, 2 * PACK * P :], 2)
 
         out_rows = out.rearrange("(h m s) g -> h m s g", h=2, s=2)
         for r in range(PACK):

@@ -109,28 +109,28 @@ def tile_attend_deformable_kernel(tc, vals, ca, cb, cc, cd, aw, wo, offs, offs2,
             w_rows[c] = columns(f"w_row{c}")
             nc.scalar.copy(by_query(w_rows[c]), w_banks[c])
 
-        def round_wo(r, ns):
-            src = wo_raw[:].rearrange("p t (h n u s) -> p h s n t u", h=2, u=2, s=2)[:, r // 2, r % 2]
-            nc.scalar.copy(wo_bf[r].rearrange("p (n u t) -> p n t u", u=2, t=PACK)[:, ns], src[:, ns])
+        def round_wo(copy, half, ns):
+            src = wo_raw[:].rearrange("p t (h n u s) -> p h n t u s", h=2, u=2, s=2)[:, half]
+            dst = wo_bf[half].rearrange("p (s n u t) -> p n t u s", s=2, u=2, t=PACK)
+            copy(dst[:, ns], src[:, ns])
 
         for c in (0, 2, 1):
             gather_bare(columns(f"bare0_{c}"), 0, c)
 
         last = PACK - 1
-        steps = [(0, 2), (0, 0), (0, 1), (1, 2), (2, 2), (1, 0), (last, 2), (0, 3), (1, 3), (1, 1), (2, 0), (last, 3), (last, 0)]
+        steps = [(0, 2), (0, 0), (0, 1), (1, 2), (1, 0), (2, 2), (last, 2), (0, 3), (1, 3), (1, 1), (2, 0), (last, 3), (last, 0)]
         accs = [psum.tile([G, 2, P], F32, name=f"acc{h}", tag=f"bank{4 + h}") for h in range(2)]
         prods = {}
         turned_bare = [psum.tile([G, 2, 2, P], F32, name=f"turned_bare{n}", tag=("bank2", "bank7")[n]) for n in range(2)]
         block = 2 * P
-        shared = keep.tile([G, J + 5 * block], F32, align_bytes=64)
+        shared = keep.tile([G, 5 * block], F32, align_bytes=64)
 
         def pair_at(n):
-            return shared[:, J + n * block : J + (n + 1) * block].rearrange("g (s p) -> g s p", s=2)
+            return shared[:, n * block : (n + 1) * block].rearrange("g (s p) -> g s p", s=2)
 
         weighted = [pair_at(n) for n in (4, 0, 1, 3)]
-        turned = [pair_at(2), keep.tile([G, 2, P], F32, name="turned1", align_bytes=64)[:]]
-        wo_all = shared[:, P : P + PACK * block].bitcast(BF16)
-        wo_bf = [wo_all[:, r * PACK * P : (r + 1) * PACK * P] for r in range(PACK)]
+        first_words = pair_at(2)[:, 0, :]
+        turned = keep.tile([G, 2, P], F32, name="turned1", align_bytes=64)
         addends = [(i, slot) for i in range(POINTS) for slot in range(2)]
         late_back = psum.tile([P, 2, G], F32, tag="bank6")
 
@@ -140,7 +140,7 @@ def tile_attend_deformable_kernel(tc, vals, ca, cb, cc, cd, aw, wo, offs, offs2,
         for t, c in steps:
             points = TURNED_POINTS if (t, c) == steps[-1] else POINTS
             if (t, c) in bare:
-                prod = shared[:, :J] if (t, c) == (1, 1) else columns(f"prod{t}_{c}")
+                prod = later[:, 5 * J :] if (t, c) == (1, 1) else columns(f"prod{t}_{c}")
                 parts = 2 if t >= 2 else 1
                 for part in range(parts):
                     gs = slice(part * G // parts, (part + 1) * G // parts)
@@ -168,10 +168,11 @@ def tile_attend_deformable_kernel(tc, vals, ca, cb, cc, cd, aw, wo, offs, offs2,
                 gather_bare(bare[0, 2], 1, 0)
                 gather_bare(bare[0, 0], 2, 1)
                 copy_row(3)
-                later = keep.tile([P, 5 * J], F32, tag="w_col3", align_bytes=64)
+                later = keep.tile([P, 6 * J], F32, tag="w_col3", align_bytes=64)
+                wo_bf = [later[:, 5 * J - P : 6 * J - P].bitcast(BF16), shared[:, P // 2 : P // 2 + J].bitcast(BF16)]
                 for j0, step in zip((0, J, 2 * J + J // 2, 4 * J), [(last, 1), (1, 1), (2, 0), (last, 0)]):
                     gather_bare(later[:, j0 : j0 + J], *step)
-            if (t, c) in ((1, 2), (last, 2)):
+            if (t, c) in ((1, 0), (last, 2)):
                 slot = t // 2
                 for i in range(POINTS):
                     nc.tensor.transpose(
@@ -182,30 +183,30 @@ def tile_attend_deformable_kernel(tc, vals, ca, cb, cc, cd, aw, wo, offs, offs2,
                     nc.scalar.activation(
                         weighted[i], turned_bare[i // 2][:, i % 2], COPY, scale=w_cols[1][:, i : i + 1]
                     )
-                nc.scalar.copy(turned[0], accs[0][:])
+                nc.scalar.copy(
+                    first_words.bitcast(BF16).rearrange("g (p t) -> g p t", t=2), accs[0][:].rearrange("g t p -> g p t")
+                )
                 for i, slot in addends[:EARLY_ADDENDS]:
                     turn_back(slot, weighted[i][:, slot, :], (i, slot) == addends[0], False)
-                round_wo(0, slice(0, P // 2))
-                round_wo(1, slice(0, P // 4))
+                round_wo(nc.scalar.copy, 0, slice(P // 4, P // 2))
 
         on_vector = later[:, 3 * J + J // 2 : 4 * J + J // 2]
         gather_weighted(on_vector, 2, 3, 0, J)
+        round_wo(nc.vector.tensor_copy, 0, slice(0, P // 4))
 
-        nc.scalar.copy(turned[1], accs[1][:])
+        nc.scalar.copy(turned[:], accs[1][:])
         for i, slot in addends[EARLY_ADDENDS:]:
             turn_back(slot, weighted[i][:, slot, :], False, False)
         for slot in range(2):
-            turn_back(slot, turned[1][:, slot, :], False, slot == 1)
-        early_back = psum.tile([P, 2, G], F32, tag="bank7")
-        for slot in (1, 0):
-            nc.tensor.transpose(early_back[:, slot, :], turned[0][:, slot, :], ident[:])
+            turn_back(slot, turned[:, slot, :], False, slot == 1)
+        early_back = psum.tile([P, G], F32, tag="bank7")
+        nc.tensor.transpose(early_back[:], first_words, ident[:])
 
-        round_wo(1, slice(P // 4, P // 2))
-        round_wo(2, slice(0, P // 2))
-        round_wo(3, slice(0, P // 4))
+        round_wo(nc.scalar.copy, 1, slice(0, 3 * P // 8))
         b_bf = keep.tile([P, G, PACK], BF16, align_bytes=64)
-        nc.scalar.copy(b_bf[:, :, :2], early_back[:].rearrange("p t g -> p g t"))
-        round_wo(3, slice(P // 4, P // 2))
+        b_words = b_bf[:].rearrange("p g t -> p (g t)").bitcast(F32).rearrange("p (g w) -> p g w", w=2)
+        nc.scalar.copy(b_words[:, :, 0], early_back[:])
+        round_wo(nc.scalar.copy, 1, slice(3 * P // 8, P // 2))
 
         wo_scales = keep.tile([P, F], U8, align_bytes=64)
         wo_codes = []
@@ -228,7 +229,7 @@ def tile_attend_deformable_kernel(tc, vals, ca, cb, cc, cd, aw, wo, offs, offs2,
                 ADD,
             )
         first_codes = keep.tile([P, 2 * P], U32, align_bytes=64, tag="turned1")
-        quantise_wo(first_codes[:], wo_all[:, : 2 * PACK * P], 2)
+        quantise_wo(first_codes[:], wo_bf[0], 2)
 
         b_codes = keep.tile([P, G], U32, align_bytes=64)
         b_scales = keep.tile([P, G], U8, align_bytes=64)
@@ -236,7 +237,7 @@ def tile_attend_deformable_kernel(tc, vals, ca, cb, cc, cd, aw, wo, offs, offs2,
             out=b_codes[:].bitcast(FP8X4), scales=b_scales[:], in_=b_bf[:].rearrange("p g t -> p (g t)")
         )
         last_codes = keep.tile([P, 2 * P], U32, align_bytes=64)
-        quantise_wo(last_codes[:], wo_all[:, 2 * PACK * P :], 2)
+        quantise_wo(last_codes[:], wo_bf[1], 2)
 
         out_rows = out.rearrange("(h m s) g -> h m s g", h=2, s=2)
         for r in range(PACK):

@@ -21,8 +21,7 @@ PACK = 4
 POINTS = J // G
 CORNERS = 4
 STRIPE = 16
-TURNED_POINTS = 2
-EARLY_ADDENDS = 2
+TURNED_POINTS = 3
 
 
 def tile_attend_deformable_kernel(tc, vals, ca, cb, cc, cd, aw, wo, offs, offs2, offs3, offs4, out):
@@ -93,120 +92,149 @@ def tile_attend_deformable_kernel(tc, vals, ca, cb, cc, cd, aw, wo, offs, offs2,
 
         bare = {}
 
-        def gather_bare(dst, t, c):
+        def gather_on_scalar(dst, t, c):
             bare[t, c] = dst
-            window = planes[t][:].indirect(lists[c][:])
-            if c == 2:
-                nc.vector.tensor_copy(dst, window)
-            else:
-                nc.scalar.activation(dst, window, COPY)
+            nc.scalar.activation(dst, planes[t][:].indirect(lists[c][:]), COPY)
 
-        def gather_weighted(dst, t, c, j0, j1):
-            offsets = lists[c][:, j0 // STRIPE : j1 // STRIPE]
-            nc.vector.tensor_tensor(dst, planes[t][:].indirect(offsets), w_rows[c][:, j0:j1], MULT)
+        def gather_weighted(dst, t, c, parts=1):
+            for part in range(parts):
+                j0, j1 = part * J // parts, (part + 1) * J // parts
+                offsets = lists[c][:, j0 // STRIPE : j1 // STRIPE]
+                nc.vector.tensor_tensor(dst[:, j0:j1], planes[t][:].indirect(offsets), w_rows[c][:, j0:j1], MULT)
 
         def copy_row(c):
             w_rows[c] = columns(f"w_row{c}")
             nc.scalar.copy(by_query(w_rows[c]), w_banks[c])
+
+        first_sums = psum.tile([G, 2, P], F32, tag="bank4")
+        third_sums = psum.tile([G, P], F32, tag="bank5")
+        last_sums = psum.tile([G, P], F32, tag="bank3")
+        sums = [first_sums[:, 0, :], first_sums[:, 1, :], third_sums[:], last_sums[:]]
+        opens = [(0, 2), (2, 2), (3, 2)]
+        closes = [(1, 1), (2, 0), (3, 0)]
+
+        def add_up(prod, t, c, points=POINTS):
+            for i in range(points):
+                nc.tensor.matmul(
+                    sums[t],
+                    lhsT=prod[:, i::points],
+                    rhs=ident[:],
+                    is_transpose=True,
+                    start=((t, c) in opens and i == 0),
+                    stop=((t, c) in closes and i == points - 1),
+                )
+
+        def fused(dst, t, c):
+            gather_weighted(dst, t, c)
+            add_up(dst, t, c)
+
+        def weigh(dst, t, c, parts=1):
+            for part in range(parts):
+                gs = slice(part * G // parts, (part + 1) * G // parts)
+                nc.vector.tensor_tensor(by_query(dst)[:, gs], by_query(bare[t, c])[:, gs], w_banks[c][:, gs], MULT)
+            add_up(dst, t, c)
+
+        turned_bare = [psum.tile([G, 2, 2, P], F32, name=f"turned_bare{n}", tag=("bank2", "bank7")[n]) for n in range(2)]
+
+        def turn_bare(t):
+            for i in range(POINTS):
+                nc.tensor.transpose(turned_bare[i // 2][:, i % 2, t - 2, :], bare[t, 1][:, i::POINTS], ident[:])
+
+        block = 2 * P
+        shared = keep.tile([G, 6 * block], F32, align_bytes=64)
+        weighted = [shared[:, n * block : (n + 1) * block].rearrange("g (s p) -> g s p", s=2) for n in (3, 4, 0, 5)]
+        first_words = shared[:, 2 * block : 2 * block + P]
+        late_back = psum.tile([P, 2, G], F32, tag="bank6")
+
+        def weigh_turned(i):
+            nc.scalar.activation(weighted[i], turned_bare[i // 2][:, i % 2], COPY, scale=w_cols[1][:, i : i + 1])
+
+        def turn_back(slot, addend, start=False, stop=False):
+            nc.tensor.matmul(late_back[:, slot, :], lhsT=addend, rhs=ident[:], is_transpose=True, start=start, stop=stop)
+
+        def turn_back_weighted(i):
+            for slot in range(2):
+                turn_back(slot, weighted[i][:, slot, :], start=(i == 0 and slot == 0))
+
+        later = keep.tile([P, 4 * J], F32, tag="w_col3", align_bytes=64)
+        pair = keep.tile([P, 2 * J], F32, align_bytes=64)
+        wo_bf = [pair[:, J - P // 2 : 2 * J - P // 2].bitcast(BF16), shared[:, P // 2 : P // 2 + J].bitcast(BF16)]
 
         def round_wo(copy, half, ns):
             src = wo_raw[:].rearrange("p t (h n u s) -> p h n t u s", h=2, u=2, s=2)[:, half]
             dst = wo_bf[half].rearrange("p (s n u t) -> p n t u s", s=2, u=2, t=PACK)
             copy(dst[:, ns], src[:, ns])
 
-        for c in (0, 2, 1):
-            gather_bare(columns(f"bare0_{c}"), 0, c)
+        quarters = [slice(q * P // 8, (q + 1) * P // 8) for q in range(4)]
 
-        last = PACK - 1
-        steps = [(0, 2), (0, 0), (0, 1), (1, 2), (1, 0), (2, 2), (last, 2), (0, 3), (1, 3), (1, 1), (2, 0), (last, 3), (last, 0)]
-        accs = [psum.tile([G, 2, P], F32, name=f"acc{h}", tag=f"bank{4 + h}") for h in range(2)]
-        prods = {}
-        turned_bare = [psum.tile([G, 2, 2, P], F32, name=f"turned_bare{n}", tag=("bank2", "bank7")[n]) for n in range(2)]
-        block = 2 * P
-        shared = keep.tile([G, 5 * block], F32, align_bytes=64)
+        gather_on_scalar(columns("bare00"), 0, 0)
+        bare[0, 2] = columns("bare02")
+        nc.vector.tensor_copy(bare[0, 2], planes[0][:].indirect(lists[2][:]))
+        gather_on_scalar(columns("bare01"), 0, 1)
+        weigh(columns("prod02"), 0, 2)
+        copy_row(2)
+        weigh(columns("prod00"), 0, 0)
+        weigh(columns("prod01"), 0, 1)
+        gather_on_scalar(bare[0, 2], 1, 0)
+        gather_on_scalar(bare[0, 0], 2, 1)
+        copy_row(3)
+        gather_on_scalar(later[:, J + J // 2 : 2 * J + J // 2], 3, 1)
+        gather_on_scalar(later[:, 3 * J :], 1, 1)
 
-        def pair_at(n):
-            return shared[:, n * block : (n + 1) * block].rearrange("g (s p) -> g s p", s=2)
+        fused(columns("prod12"), 1, 2)
+        weigh(columns("prod10"), 1, 0)
+        turn_bare(2)
+        fused(columns("prod22"), 2, 2)
+        turn_bare(3)
+        fused(pair[:, :J], 3, 2)
+        weigh_turned(0)
+        gather_on_scalar(bare[3, 1], 2, 0)
+        weigh_turned(1)
+        gather_on_scalar(pair[:, :J], 3, 0)
+        weigh_turned(2)
+        weigh_turned(3)
+        fused(columns("prod03"), 0, 3)
+        turn_back_weighted(0)
+        fused(columns("prod13"), 1, 3)
+        weigh(pair[:, J:], 1, 1)
+        weigh(columns("prod20"), 2, 0, parts=2)
+        turn_back_weighted(1)
 
-        weighted = [pair_at(n) for n in (4, 0, 1, 3)]
-        first_words = pair_at(2)[:, 0, :]
+        nc.scalar.copy(
+            first_words.bitcast(BF16).rearrange("g (p t) -> g p t", t=2), first_sums[:].rearrange("g t p -> g p t")
+        )
         turned = keep.tile([G, 2, P], F32, name="turned1", align_bytes=64)
-        addends = [(i, slot) for i in range(POINTS) for slot in range(2)]
-        late_back = psum.tile([P, 2, G], F32, tag="bank6")
+        nc.scalar.copy(turned[:, 0, :], third_sums[:])
+        round_wo(nc.scalar.copy, 0, slice(quarters[1].start, quarters[3].stop))
 
-        def turn_back(slot, addend, start, stop):
-            nc.tensor.matmul(late_back[:, slot, :], lhsT=addend, rhs=ident[:], is_transpose=True, start=start, stop=stop)
+        fused(later[:, J // 2 + P : J + J // 2 + P], 3, 3)
+        rest = keep.tile([P, 2, G], F32, align_bytes=64)
+        prod_last = keep.tile([P, G * TURNED_POINTS], F32, align_bytes=64)
+        nc.vector.tensor_tensor(
+            prod_last[:].rearrange("p (g i) -> p g i", i=TURNED_POINTS),
+            by_query(bare[3, 0])[:, :, :TURNED_POINTS],
+            w_banks[0][:, :, :TURNED_POINTS],
+            MULT,
+        )
+        add_up(prod_last[:], 3, 0, TURNED_POINTS)
+        nc.vector.tensor_tensor(
+            rest[:, 1, :], by_query(bare[3, 0])[:, :, TURNED_POINTS], w_banks[0][:, :, TURNED_POINTS], MULT
+        )
+        on_vector = later[:, J + J // 2 + P : 2 * J + J // 2 + P]
+        gather_weighted(on_vector, 2, 3, parts=2)
 
-        for t, c in steps:
-            points = TURNED_POINTS if (t, c) == steps[-1] else POINTS
-            if (t, c) in bare:
-                prod = later[:, 5 * J :] if (t, c) == (1, 1) else columns(f"prod{t}_{c}")
-                parts = 2 if t >= 2 else 1
-                for part in range(parts):
-                    gs = slice(part * G // parts, (part + 1) * G // parts)
-                    nc.vector.tensor_tensor(by_query(prod)[:, gs], by_query(bare[t, c])[:, gs], w_banks[c][:, gs], MULT)
-            elif (t, c) == (last, 3):
-                prod = later[:, 2 * J : 3 * J]
-                gather_weighted(prod, t, c, 0, J)
-            else:
-                prod = columns(f"prod{t}_{c}")
-                gather_weighted(prod, t, c, 0, J)
-            prods[t, c] = prod
-            of_pair = [step for step in steps if step[0] // 2 == t // 2]
-            for i in range(points):
-                nc.tensor.matmul(
-                    accs[t // 2][:, t % 2, :],
-                    lhsT=prod[:, i::POINTS],
-                    rhs=ident[:],
-                    is_transpose=True,
-                    start=((t, c) == of_pair[0] and i == 0),
-                    stop=((t, c) == of_pair[-1] and i == points - 1),
-                )
-            if (t, c) == (0, 2):
-                copy_row(2)
-            if (t, c) == (0, 1):
-                gather_bare(bare[0, 2], 1, 0)
-                gather_bare(bare[0, 0], 2, 1)
-                copy_row(3)
-                later = keep.tile([P, 6 * J], F32, tag="w_col3", align_bytes=64)
-                wo_bf = [later[:, 5 * J - P : 6 * J - P].bitcast(BF16), shared[:, P // 2 : P // 2 + J].bitcast(BF16)]
-                for j0, step in zip((0, J, 2 * J + J // 2, 4 * J), [(last, 1), (1, 1), (2, 0), (last, 0)]):
-                    gather_bare(later[:, j0 : j0 + J], *step)
-            if (t, c) in ((1, 0), (last, 2)):
-                slot = t // 2
-                for i in range(POINTS):
-                    nc.tensor.transpose(
-                        turned_bare[i // 2][:, i % 2, slot, :], bare[2 + slot, 1][:, i::POINTS], ident[:]
-                    )
-            if (t, c) == (2, 0):
-                for i in range(POINTS):
-                    nc.scalar.activation(
-                        weighted[i], turned_bare[i // 2][:, i % 2], COPY, scale=w_cols[1][:, i : i + 1]
-                    )
-                nc.scalar.copy(
-                    first_words.bitcast(BF16).rearrange("g (p t) -> g p t", t=2), accs[0][:].rearrange("g t p -> g p t")
-                )
-                for i, slot in addends[:EARLY_ADDENDS]:
-                    turn_back(slot, weighted[i][:, slot, :], (i, slot) == addends[0], False)
-                round_wo(nc.scalar.copy, 0, slice(P // 4, P // 2))
-
-        on_vector = later[:, 3 * J + J // 2 : 4 * J + J // 2]
-        gather_weighted(on_vector, 2, 3, 0, J)
-        round_wo(nc.vector.tensor_copy, 0, slice(0, P // 4))
-
-        nc.scalar.copy(turned[:], accs[1][:])
-        for i, slot in addends[EARLY_ADDENDS:]:
-            turn_back(slot, weighted[i][:, slot, :], False, False)
-        for slot in range(2):
-            turn_back(slot, turned[:, slot, :], False, slot == 1)
+        nc.scalar.copy(turned[:, 1, :], last_sums[:])
+        turn_back_weighted(2)
+        turn_back_weighted(3)
+        turn_back(0, turned[:, 0, :])
+        turn_back(1, turned[:, 1, :], stop=True)
         early_back = psum.tile([P, G], F32, tag="bank7")
         nc.tensor.transpose(early_back[:], first_words, ident[:])
 
-        round_wo(nc.scalar.copy, 1, slice(0, 3 * P // 8))
+        round_wo(nc.scalar.copy, 1, slice(quarters[0].start, quarters[2].stop))
         b_bf = keep.tile([P, G, PACK], BF16, align_bytes=64)
-        b_words = b_bf[:].rearrange("p g t -> p (g t)").bitcast(F32).rearrange("p (g w) -> p g w", w=2)
-        nc.scalar.copy(b_words[:, :, 0], early_back[:])
-        round_wo(nc.scalar.copy, 1, slice(3 * P // 8, P // 2))
+        nc.scalar.copy(b_bf[:, :, :2], early_back[:].bitcast(BF16).rearrange("p (g t) -> p g t", t=2))
+        round_wo(nc.scalar.copy, 1, quarters[3])
 
         wo_scales = keep.tile([P, F], U8, align_bytes=64)
         wo_codes = []
@@ -216,11 +244,10 @@ def tile_attend_deformable_kernel(tc, vals, ca, cb, cc, cd, aw, wo, offs, offs2,
             nc.vector.quantize_mx(out=codes.bitcast(FP8X4), scales=wo_scales[:, r * P : (r + blocks) * P], in_=rounded)
             wo_codes.extend(codes[:, n * P : (n + 1) * P] for n in range(blocks))
 
-        rest = keep.tile([P, 2, G], F32, align_bytes=64)
         halves = (slice(0, G // 2), slice(G // 2, G))
-        nc.vector.tensor_reduce(rest[:, 1, :], by_query(prods[last, 0])[:, :, TURNED_POINTS:], mybir.AxisListType.X, ADD)
         for gs in halves:
             nc.vector.tensor_reduce(rest[:, 0, gs], by_query(on_vector)[:, gs], mybir.AxisListType.X, ADD)
+        round_wo(nc.vector.tensor_copy, 0, quarters[0])
         for gs in halves:
             nc.vector.tensor_tensor(
                 b_bf[:, gs, 2:],

@@ -128,10 +128,8 @@ def tile_attend_deformable_kernel(tc, vals, ca, cb, cc, cd, aw, wo, offs, offs2,
             gather_weighted(dst, t, c)
             add_up(dst, t, c)
 
-        def weigh(dst, t, c, parts=1):
-            for part in range(parts):
-                gs = slice(part * G // parts, (part + 1) * G // parts)
-                nc.vector.tensor_tensor(by_query(dst)[:, gs], by_query(bare[t, c])[:, gs], w_banks[c][:, gs], MULT)
+        def weigh(dst, t, c):
+            nc.vector.tensor_tensor(by_query(dst), by_query(bare[t, c]), w_banks[c], MULT)
             add_up(dst, t, c)
 
         turned_bare = [psum.tile([G, 2, 2, P], F32, name=f"turned_bare{n}", tag=("bank2", "bank7")[n]) for n in range(2)]
@@ -156,7 +154,7 @@ def tile_attend_deformable_kernel(tc, vals, ca, cb, cc, cd, aw, wo, offs, offs2,
             for slot in range(2):
                 turn_back(slot, weighted[i][:, slot, :], start=(i == 0 and slot == 0))
 
-        later = keep.tile([P, 4 * J], F32, tag="w_col3", align_bytes=64)
+        later = keep.tile([P, 2 * J], F32, tag="w_col3", align_bytes=64)
         pair = keep.tile([P, 2 * J], F32, align_bytes=64)
         wo_bf = [pair[:, J - P // 2 : 2 * J - P // 2].bitcast(BF16), shared[:, P // 2 : P // 2 + J].bitcast(BF16)]
 
@@ -178,8 +176,8 @@ def tile_attend_deformable_kernel(tc, vals, ca, cb, cc, cd, aw, wo, offs, offs2,
         gather_on_scalar(bare[0, 2], 1, 0)
         gather_on_scalar(bare[0, 0], 2, 1)
         copy_row(3)
-        gather_on_scalar(later[:, J + J // 2 : 2 * J + J // 2], 3, 1)
-        gather_on_scalar(later[:, 3 * J :], 1, 1)
+        gather_on_scalar(later[:, :J], 3, 1)
+        gather_on_scalar(later[:, J:], 1, 1)
 
         fused(columns("prod12"), 1, 2)
         weigh(columns("prod10"), 1, 0)
@@ -193,11 +191,12 @@ def tile_attend_deformable_kernel(tc, vals, ca, cb, cc, cd, aw, wo, offs, offs2,
         gather_on_scalar(pair[:, :J], 3, 0)
         weigh_turned(2)
         weigh_turned(3)
-        fused(columns("prod03"), 0, 3)
+        prod03 = columns("prod03")
+        fused(prod03, 0, 3)
         turn_back_weighted(0)
         fused(columns("prod13"), 1, 3)
         weigh(pair[:, J:], 1, 1)
-        weigh(columns("prod20"), 2, 0, parts=2)
+        weigh(columns("prod20"), 2, 0)
         turn_back_weighted(1)
 
         nc.scalar.copy(
@@ -207,7 +206,7 @@ def tile_attend_deformable_kernel(tc, vals, ca, cb, cc, cd, aw, wo, offs, offs2,
         nc.scalar.copy(turned[:, 0, :], third_sums[:])
         round_wo(nc.scalar.copy, 0, slice(quarters[1].start, quarters[3].stop))
 
-        fused(later[:, J // 2 + P : J + J // 2 + P], 3, 3)
+        fused(prod03, 3, 3)
         rest = keep.tile([P, 2, G], F32, align_bytes=64)
         prod_last = keep.tile([P, G * TURNED_POINTS], F32, align_bytes=64)
         nc.vector.tensor_tensor(
@@ -220,7 +219,7 @@ def tile_attend_deformable_kernel(tc, vals, ca, cb, cc, cd, aw, wo, offs, offs2,
         nc.vector.tensor_tensor(
             rest[:, 1, :], by_query(bare[3, 0])[:, :, TURNED_POINTS], w_banks[0][:, :, TURNED_POINTS], MULT
         )
-        on_vector = later[:, J + J // 2 + P : 2 * J + J // 2 + P]
+        on_vector = bare[2, 0]
         gather_weighted(on_vector, 2, 3, parts=2)
 
         nc.scalar.copy(turned[:, 1, :], last_sums[:])

from contextlib import ExitStack

import concourse.mybir as mybir
from concourse.masks import make_identity

E, T, J, G, F = 512, 1024, 512, 128, 512
FLOPS = 2 * E * F * G

F32 = mybir.dt.float32
BF16 = mybir.dt.bfloat16
U32 = mybir.dt.uint32
U16 = mybir.dt.uint16
U8 = mybir.dt.uint8
FP8X4 = mybir.dt.float8_e4m3fn_x4
MULT = mybir.AluOpType.mult
ADD = mybir.AluOpType.add
COPY = mybir.ActivationFunctionType.Copy

P = 128
PACK = 4
POINTS = J // G
CORNERS = 4
STRIPE = 16
TURNED_POINTS = 3


def tile_attend_deformable_kernel(tc, vals, ca, cb, cc, cd, aw, wo, offs, offs2, offs3, offs4, out):
    nc = tc.nc
    with ExitStack() as ctx:
        keep = ctx.enter_context(tc.tile_pool(name="keep", bufs=1))
        psum = ctx.enter_context(tc.psum_pool(name="psum", bufs=1))

        lists = [keep.tile([P, J // STRIPE], U16, name=f"list{c}") for c in range(CORNERS)]
        planes = [keep.tile([P, T], F32, name=f"plane{t}", align_bytes=64) for t in range(PACK)]
        corner = [keep.tile([P, POINTS], F32, name=f"corner{c}") for c in range(CORNERS)]
        att = keep.tile([P, POINTS], F32)
        wo_raw = keep.tile([P, PACK, F], F32)

        vals_planes = vals.rearrange("(p t) n -> t p n", t=PACK)
        list_src = (offs, offs2, offs3, offs4)
        corner_src = (ca, cb, cc, cd)

        def load_weights(tile, src):
            nc.sync.dma_start(tile[:], src.rearrange("o (g i) -> (o g) i", i=POINTS))

        def load_corner(c):
            load_weights(corner[c], corner_src[c])

        def load_list(c):
            nc.sync.dma_start(lists[c][:], list_src[c])

        def load_plane(t):
            nc.sync.dma_start(planes[t][:], vals_planes[t])

        load_list(0)
        nc.scalar.dma_start(planes[0][:], vals_planes[0])
        load_list(2)
        load_weights(att, aw)
        load_corner(2)
        load_corner(0)
        load_corner(1)
        load_list(1)
        load_corner(3)
        load_plane(1)
        load_list(3)
        load_plane(2)
        load_plane(3)
        nc.sync.dma_start(wo_raw[:], wo.rearrange("(p t) f -> p t f", t=PACK))

        zero = keep.tile([P, 1], F32)
        nc.vector.memset(zero[:], 0.0)
        ident = keep.tile([P, P], F32)
        nc.scalar.activation(ident[:], zero[:].to_broadcast([P, P]), COPY)
        make_identity(nc, ident[:], nomemset=True)

        w_cols = {}
        w_banks = {}
        w_rows = {}
        for c in (2, 0, 1, 3):
            w_cols[c] = keep.tile([P, POINTS], F32, name=f"w_col{c}", align_bytes=64)
            nc.gpsimd.tensor_tensor(w_cols[c][:], corner[c][:], att[:], MULT)
            w_bank = psum.tile([P, POINTS, G], F32, name=f"w_bank{c}", tag=f"bank{c}")
            for i in range(POINTS):
                nc.tensor.transpose(w_bank[:, i, :], w_cols[c][:, i : i + 1].to_broadcast([P, P]), ident[:])
            w_banks[c] = w_bank[:].rearrange("p i g -> p g i")

        def columns(name):
            return keep.tile([P, J], F32, name=name, align_bytes=64)[:]

        def by_query(ap):
            return ap.rearrange("p (g i) -> p g i", i=POINTS)

        bare = {}

        def gather_on_scalar(dst, t, c):
            bare[t, c] = dst
            nc.scalar.activation(dst, planes[t][:].indirect(lists[c][:]), COPY)

        def gather_weighted(dst, t, c, parts=1):
            for part in range(parts):
                j0, j1 = part * J // parts, (part + 1) * J // parts
                offsets = lists[c][:, j0 // STRIPE : j1 // STRIPE]
                nc.vector.tensor_tensor(dst[:, j0:j1], planes[t][:].indirect(offsets), w_rows[c][:, j0:j1], MULT)

        def copy_row(c):
            w_rows[c] = columns(f"w_row{c}")
            nc.scalar.copy(by_query(w_rows[c]), w_banks[c])

        first_sums = psum.tile([G, 2, P], F32, tag="bank4")
        third_sums = psum.tile([G, P], F32, tag="bank5")
        last_sums = psum.tile([G, P], F32, tag="bank3")
        sums = [first_sums[:, 0, :], first_sums[:, 1, :], third_sums[:], last_sums[:]]
        opens = [(0, 2), (2, 2), (3, 2)]
        closes = [(1, 1), (2, 0), (3, 0)]

        def add_up(prod, t, c, points=POINTS):
            for i in range(points):
                nc.tensor.matmul(
                    sums[t],
                    lhsT=prod[:, i::points],
                    rhs=ident[:],
                    is_transpose=True,
                    start=((t, c) in opens and i == 0),
                    stop=((t, c) in closes and i == points - 1),
                )

        def fused(dst, t, c):
            gather_weighted(dst, t, c)
            add_up(dst, t, c)

        def weigh(dst, t, c):
            nc.vector.tensor_tensor(by_query(dst), by_query(bare[t, c]), w_banks[c], MULT)
            add_up(dst, t, c)

        turned_bare = [psum.tile([G, 2, 2, P], F32, name=f"turned_bare{n}", tag=("bank2", "bank7")[n]) for n in range(2)]

        def turn_bare(t):
            for i in range(POINTS):
                nc.tensor.transpose(turned_bare[i // 2][:, i % 2, t - 2, :], bare[t, 1][:, i::POINTS], ident[:])

        block = 2 * P
        shared = keep.tile([G, 6 * block], F32, align_bytes=64)
        weighted = [shared[:, n * block : (n + 1) * block].rearrange("g (s p) -> g s p", s=2) for n in (3, 4, 0, 5)]
        first_words = shared[:, 2 * block : 2 * block + P]
        late_back = psum.tile([P, 2, G], F32, tag="bank6")

        def weigh_turned(i):
            nc.scalar.activation(weighted[i], turned_bare[i // 2][:, i % 2], COPY, scale=w_cols[1][:, i : i + 1])

        def turn_back(slot, addend, start=False, stop=False):
            nc.tensor.matmul(late_back[:, slot, :], lhsT=addend, rhs=ident[:], is_transpose=True, start=start, stop=stop)

        def turn_back_weighted(i):
            for slot in range(2):
                turn_back(slot, weighted[i][:, slot, :], start=(i == 0 and slot == 0))

        later = keep.tile([P, 2 * J], F32, tag="w_col3", align_bytes=64)
        pair = keep.tile([P, 2 * J], F32, align_bytes=64)
        wo_bf = [pair[:, J - P // 2 : 2 * J - P // 2].bitcast(BF16), shared[:, P // 2 : P // 2 + J].bitcast(BF16)]

        def round_wo(copy, half, ns):
            src = wo_raw[:].rearrange("p t (h n u s) -> p h n t u s", h=2, u=2, s=2)[:, half]
            dst = wo_bf[half].rearrange("p (s n u t) -> p n t u s", s=2, u=2, t=PACK)
            copy(dst[:, ns], src[:, ns])

        quarters = [slice(q * P // 8, (q + 1) * P // 8) for q in range(4)]

        gather_on_scalar(columns("bare00"), 0, 0)
        bare[0, 2] = columns("bare02")
        nc.vector.tensor_copy(bare[0, 2], planes[0][:].indirect(lists[2][:]))
        gather_on_scalar(columns("bare01"), 0, 1)
        weigh(columns("prod02"), 0, 2)
        copy_row(2)
        weigh(columns("prod00"), 0, 0)
        weigh(columns("prod01"), 0, 1)
        gather_on_scalar(bare[0, 2], 1, 0)
        gather_on_scalar(bare[0, 0], 2, 1)
        copy_row(3)
        gather_on_scalar(later[:, :J], 3, 1)
        gather_on_scalar(later[:, J:], 1, 1)

        fused(columns("prod12"), 1, 2)
        weigh(columns("prod10"), 1, 0)
        turn_bare(2)
        fused(columns("prod22"), 2, 2)
        turn_bare(3)
        fused(pair[:, :J], 3, 2)
        weigh_turned(0)
        gather_on_scalar(bare[3, 1], 2, 0)
        weigh_turned(1)
        gather_on_scalar(pair[:, :J], 3, 0)
        weigh_turned(2)
        weigh_turned(3)
        prod03 = columns("prod03")
        fused(prod03, 0, 3)
        turn_back_weighted(0)
        fused(columns("prod13"), 1, 3)
        weigh(pair[:, J:], 1, 1)
        weigh(columns("prod20"), 2, 0)
        turn_back_weighted(1)

        nc.scalar.copy(
            first_words.bitcast(BF16).rearrange("g (p t) -> g p t", t=2), first_sums[:].rearrange("g t p -> g p t")
        )
        turned = keep.tile([G, 2, P], F32, name="turned1", align_bytes=64)
        nc.scalar.copy(turned[:, 0, :], third_sums[:])
        round_wo(nc.scalar.copy, 0, slice(quarters[1].start, quarters[3].stop))

        fused(prod03, 3, 3)
        rest = keep.tile([P, 2, G], F32, align_bytes=64)
        prod_last = keep.tile([P, G * TURNED_POINTS], F32, align_bytes=64)
        nc.vector.tensor_tensor(
            prod_last[:].rearrange("p (g i) -> p g i", i=TURNED_POINTS),
            by_query(bare[3, 0])[:, :, :TURNED_POINTS],
            w_banks[0][:, :, :TURNED_POINTS],
            MULT,
        )
        add_up(prod_last[:], 3, 0, TURNED_POINTS)
        nc.vector.tensor_tensor(
            rest[:, 1, :], by_query(bare[3, 0])[:, :, TURNED_POINTS], w_banks[0][:, :, TURNED_POINTS], MULT
        )
        on_vector = bare[2, 0]
        gather_weighted(on_vector, 2, 3, parts=2)

        nc.scalar.copy(turned[:, 1, :], last_sums[:])
        turn_back_weighted(2)
        turn_back_weighted(3)
        turn_back(0, turned[:, 0, :])
        turn_back(1, turned[:, 1, :], stop=True)
        early_back = psum.tile([P, G], F32, tag="bank7")
        nc.tensor.transpose(early_back[:], first_words, ident[:])

        round_wo(nc.scalar.copy, 1, slice(quarters[0].start, quarters[2].stop))
        b_bf = keep.tile([P, G, PACK], BF16, align_bytes=64)
        nc.scalar.copy(b_bf[:, :, :2], early_back[:].bitcast(BF16).rearrange("p (g t) -> p g t", t=2))
        round_wo(nc.scalar.copy, 1, quarters[3])

        wo_scales = keep.tile([P, F], U8, align_bytes=64)
        wo_codes = []

        def quantise_wo(codes, rounded, blocks):
            r = len(wo_codes)
            nc.vector.quantize_mx(out=codes.bitcast(FP8X4), scales=wo_scales[:, r * P : (r + blocks) * P], in_=rounded)
            wo_codes.extend(codes[:, n * P : (n + 1) * P] for n in range(blocks))

        halves = (slice(0, G // 2), slice(G // 2, G))
        for gs in halves:
            nc.vector.tensor_reduce(rest[:, 0, gs], by_query(on_vector)[:, gs], mybir.AxisListType.X, ADD)
        round_wo(nc.vector.tensor_copy, 0, quarters[0])
        for gs in halves:
            nc.vector.tensor_tensor(
                b_bf[:, gs, 2:],
                late_back[:].rearrange("p t g -> p g t")[:, gs],
                rest[:].rearrange("p t g -> p g t")[:, gs],
                ADD,
            )
        first_codes = keep.tile([P, 2 * P], U32, align_bytes=64, tag="turned1")
        quantise_wo(first_codes[:], wo_bf[0], 2)

        b_codes = keep.tile([P, G], U32, align_bytes=64)
        b_scales = keep.tile([P, G], U8, align_bytes=64)
        nc.vector.quantize_mx(
            out=b_codes[:].bitcast(FP8X4), scales=b_scales[:], in_=b_bf[:].rearrange("p g t -> p (g t)")
        )
        last_codes = keep.tile([P, 2 * P], U32, align_bytes=64)
        quantise_wo(last_codes[:], wo_bf[1], 2)

        out_rows = out.rearrange("(h m s) g -> h m s g", h=2, s=2)
        for r in range(PACK):
            y = psum.tile([P, G], F32, name=f"y{r}", tag=("bank1", "bank2", "bank3", "bank5")[r])
            nc.tensor.matmul_mx(
                out=y[:],
                lhsT=wo_codes[r].bitcast(FP8X4),
                lhsT_scale=wo_scales[:, r * P : (r + 1) * P],
                rhs=b_codes[:].bitcast(FP8X4),
                rhs_scale=b_scales[:],
                start=True,
                stop=True,
            )
            if r % 2 == 0:
                y_sb = keep.tile([P, 2, G], F32, name=f"y_sb{r}")
                nc.vector.tensor_copy(y_sb[:, 0, :], y[:])
            else:
                nc.scalar.copy(y_sb[:, 1, :], y[:])
                queue = nc.scalar if r == PACK - 1 else nc.sync
                queue.dma_start(out_rows[r // 2], y_sb[:])
